import numpy as np
import ml_dtypes


def mxq(x, axis, fmt="e4m3"):
    dtype, down = {"e4m3": (ml_dtypes.float8_e4m3fn, 7), "e5m2": (ml_dtypes.float8_e5m2, 14)}[fmt]
    v = np.moveaxis(np.asarray(x, np.float32).astype(ml_dtypes.bfloat16).astype(np.float64), axis, -1)
    blocks = v.reshape(v.shape[:-1] + (-1, 32))
    amax = np.abs(blocks).max(-1, keepdims=True)
    byte = np.maximum(np.where(amax > 0, np.frexp(amax)[1] - 1 + 127, 0) - down, 1)
    scale = np.exp2(byte - 127.0)
    codes = (blocks / scale).astype(np.float32).astype(dtype).astype(np.float64)
    return np.moveaxis((codes * scale).reshape(v.shape), -1, axis)


WIDE = False


def mx_kscale(k):
    if not WIDE:
        return np.ones(k)
    levels = np.array([30, -30])
    if k % 512:
        return np.exp2(np.random.permutation(np.resize(levels, k // 32))).repeat(32)
    a = np.empty((k // 512, 16))
    for p in range(k // 512):
        a[p, :8] = np.random.permutation(np.resize(levels, 8))
        for g in range(8):
            far = levels[np.abs(levels - a[p, g]) >= 10]
            a[p, g + 8] = far[np.random.randint(len(far))]
    return np.exp2(a.ravel()).repeat(32)


def f64(x):
    return np.asarray(x).astype(np.float64)


def striped(idx):
    return np.tile(idx.reshape(-1, 16).T, (8, 1)).astype(np.uint16)


def unstriped(offs):
    return offs[:16].T.reshape(-1).astype(np.int64)


def bf(x):
    return np.asarray(x, np.float32).astype(ml_dtypes.bfloat16)


E2M1 = np.array([0.0, 0.5, 1.0, 1.5, 2.0, 3.0, 4.0, 6.0, -0.0, -0.5, -1.0, -1.5, -2.0, -3.0, -4.0, -6.0])


def pack_weight(w, fmt):
    k, n = w.shape
    w = f64(bf(w)).reshape(k // 32, 32, n)
    amax = np.abs(w).max(1)
    if fmt in ("e4m3", "e5m2"):
        byte = np.frexp(amax)[1] - 1 + 127 - (7 if fmt == "e4m3" else 14)
    else:
        mant, ex = np.frexp(amax / 6.0)
        byte = np.where(mant > 0.5, ex, ex - 1) + 127
    byte = np.clip(np.where(amax > 0, byte, 1), 1, 254)
    scaled = (w * np.exp2(127.0 - byte)[:, None, :]).reshape(k, n).astype(np.float32)
    by_word = np.ascontiguousarray(scaled.reshape(k // 512, 128, 4, n).transpose(0, 1, 3, 2))
    if fmt in ("e4m3", "e5m2"):
        words = by_word.astype(ml_dtypes.float8_e4m3fn if fmt == "e4m3" else ml_dtypes.float8_e5m2).view(np.uint8)
    else:
        c = by_word.astype(ml_dtypes.float4_e2m1fn).view(np.uint8) & 0xF
        words = c[..., 0::2] | (c[..., 1::2] << 4)
    return np.ascontiguousarray(words), np.ascontiguousarray(byte.astype(np.uint8).reshape(k // 512, 16, n))


def unpack_weight(words, scales, fmt):
    g, p, n, _ = words.shape
    if fmt in ("e4m3", "e5m2"):
        vals = np.ascontiguousarray(words).view(ml_dtypes.float8_e4m3fn if fmt == "e4m3" else ml_dtypes.float8_e5m2).astype(np.float64)
    else:
        nib = np.empty((g, p, n, 4), np.uint8)
        nib[..., 0::2] = words & 0xF
        nib[..., 1::2] = words >> 4
        vals = E2M1[nib]
    vals = vals * np.repeat(np.exp2(scales.astype(np.float64) - 127.0), 8, axis=1)[..., None]
    return vals.transpose(0, 1, 3, 2).reshape(g * 512, n)


T, S, K, H, N, T2 = 2048, 1024, 512, 1024, 512, 2048

def setup_inputs():
    n = np.random.standard_normal
    s = mx_kscale(K)[:, None]
    u = mx_kscale(H)[:, None]
    tab_words, tab_scales = pack_weight(n((K, T)) * np.exp(1.0 * n((1, T))) * s, "e5m2")
    wf_words, wf_scales = pack_weight(2.0 * n((H, H)) / np.sqrt(H) / u * u.T, "e4m3")
    return {
        "tab_words": tab_words, "tab_scales": tab_scales,
        "offs": striped(np.random.permutation(T)[:S]),
        "sT": (1.0 / (1.0 + np.exp(-n((H, T))))).astype(np.float32),
        "w1": (n((K, H)) / np.sqrt(K) / s * u.T).astype(np.float32),
        "price": (np.exp(0.3 * n(H)) * u[:, 0]).astype(np.float32),
        "wf_words": wf_words, "wf_scales": wf_scales,
        "w2": (2.0 * n((H, N)) / np.sqrt(H) / u).astype(np.float32),
        "offs2": striped(np.random.permutation(T2)[:S]),
        "wgo": np.exp(0.3 * n((128, S))).astype(np.float32),
    }

def reference(tab_words, tab_scales, offs, sT, w1, price, wf_words, wf_scales, w2, offs2, wgo):
    v = unpack_weight(tab_words, tab_scales, "e5m2")[:, unstriped(offs)]
    x = f64(sT)[:, unstriped(offs)]
    c = mxq(x * f64(price)[:, None], 0, "e4m3")
    wf = unpack_weight(wf_words, wf_scales, "e4m3")
    d = mxq(f64(w1), 0, "e4m3").T @ v + wf.T @ c
    h = d * (x * (1.0 - x))
    y = mxq(f64(w2), 0, "e4m3").T @ mxq(h, 0, "e4m3")
    out = np.zeros((N, T2))
    out[:, unstriped(offs2)] = np.tile(f64(wgo), (N // 128, 1)) * y
    return out

@@ -1,0 +1,259 @@
+from contextlib import ExitStack
+
+import concourse.mybir as mybir
+
+T, S, K, H, N, T2 = 2048, 1024, 512, 1024, 512, 2048
+FLOPS = 2 * S * (K * H + H * H + H * N)
+
+F32 = mybir.dt.float32
+BF16 = mybir.dt.bfloat16
+I32 = mybir.dt.int32
+U32 = mybir.dt.uint32
+U16 = mybir.dt.uint16
+U8 = mybir.dt.uint8
+E4 = mybir.dt.float8_e4m3fn_x4
+E5 = mybir.dt.float8_e5m2_x4
+MULT = mybir.AluOpType.mult
+SUB = mybir.AluOpType.subtract
+ADD = mybir.AluOpType.add
+COPY = mybir.ActivationFunctionType.Copy
+
+P = 128
+PACK = 4
+PASS = P * PACK
+HALF = 512
+BLOCKS = H // PASS
+HALVES = S // HALF
+PLANES = BLOCKS * PACK
+NT = N // P
+PAGES = NT - 1
+
+KIB = 1024
+PLANE_SLOTS = 5
+SLOT = 8 * KIB
+TAB_AT = PLANE_SLOTS * SLOT
+ROWS_AT = [TAB_AT + SLOT, TAB_AT + 2 * SLOT]
+CODES = 4 * HALF
+MX_BYTES = CODES + HALF
+
+
+def tile_list_handover_gradient_kernel(
+    tc, tab_words, tab_scales, offs, sT, w1, price, wf_words, wf_scales, w2, offs2, wgo, out
+):
+    nc = tc.nc
+    with ExitStack() as ctx:
+        keep = ctx.enter_context(tc.tile_pool(name="keep", bufs=1))
+        ring = ctx.enter_context(tc.tile_pool(name="ring", bufs=3))
+        arena = ctx.enter_context(tc.tile_pool(name="arena", bufs=1))
+        psum = ctx.enter_context(tc.psum_pool(name="psum", bufs=1))
+
+        def placed(shape, dtype, name, at):
+            return arena.tile(shape, dtype, name=name, align_bytes=64, offset=at)
+
+        idx = keep.tile([P, S // 16], U16, name="idx")
+        idx2 = keep.tile([P, S // 16], U16, name="idx2")
+        price_sb = keep.tile([P, BLOCKS, PACK], F32, name="price_sb")
+        tab_s = keep.tile([P, T], U8, name="tab_s", align_bytes=64)
+        v_w = [keep.tile([P, HALF], U32, name="v_w%d" % h, align_bytes=64) for h in range(HALVES)]
+        v_s = [keep.tile([P, HALF], U8, name="v_s%d" % h, align_bytes=64) for h in range(HALVES)]
+        wf_s_raw = keep.tile([P, H], U8, name="wf_s_raw", align_bytes=64)
+        wf_s = keep.tile([P, H], U8, name="wf_s", align_bytes=64)
+        wf_w = keep.tile([P, BLOCKS * H], I32, name="wf_w", align_bytes=64)
+        wgo_sb = keep.tile([P, S], F32, name="wgo_sb")
+        pages = [keep.tile([P, T2], F32, name="page%d" % u) for u in range(PAGES)]
+
+        def quantize(name, grouped, at=None):
+            if at is None:
+                codes = keep.tile([P, HALF], U32, name=name + "_w", align_bytes=64)
+                scales = keep.tile([P, HALF], U8, name=name + "_s", align_bytes=64)
+            else:
+                codes = placed([P, HALF], U32, name + "_w", at)
+                scales = placed([P, HALF], U8, name + "_s", at + CODES)
+            nc.vector.quantize_mx(out=codes[:].bitcast(E4), scales=scales[:], in_=grouped[:])
+            return codes, scales
+
+        def interleave(rows):
+            grouped = ring.tile([P, HALF * PACK], BF16, name="grouped", align_bytes=64)
+            nc.scalar.copy(
+                out=grouped[:].rearrange("p (c i t) -> p c t i", i=4, t=PACK),
+                in_=rows.rearrange("p t (c i) -> p c t i", i=4),
+            )
+            return grouped
+
+        def interleave_w1(raw):
+            grouped = ring.tile([P, HALF * PACK], BF16, name="grouped", align_bytes=64)
+            nc.scalar.copy(
+                out=grouped[:].rearrange("p (t m j) -> p m t j", t=PACK, j=PACK),
+                in_=raw[:].rearrange("p j (m t) -> p m t j", t=PACK),
+            )
+            return grouped
+
+        nc.vector.memset(tab_s[:].bitcast(I32), 0)
+        nc.vector.memset(wf_s_raw[:].bitcast(I32), 0)
+        for page in pages:
+            nc.vector.memset(page[:], 0.0)
+
+        s_rows = sT.rearrange("(b p t) n -> b t p n", p=P, t=PACK)
+        tab_s_rows = tab_scales[0].bitcast(I32).rearrange("(q r) n -> r q n", r=4)
+        wf_s_rows = wf_scales.bitcast(I32)
+
+        def slot_of(k):
+            return (k % PLANE_SLOTS) * SLOT
+
+        def load_wf_scales(q):
+            nc.sync.dma_start(
+                out=wf_s_raw[32 * q : 32 * q + 4 * BLOCKS, :].bitcast(I32),
+                in_=wf_s_rows[:, 4 * q : 4 * q + 4, :],
+            )
+
+        def load_raw(rows):
+            raw = ring.tile([P, PACK, HALF], F32, name="raw")
+            nc.sync.dma_start(out=raw[:], in_=rows.rearrange("(p j) c -> p j c", j=PACK))
+            return raw
+
+        slope = {}
+        c_rows = {}
+        c_grouped = {}
+
+        def pick_plane(k):
+            b, t = divmod(k, PACK)
+            plane = placed([P, T], F32, "plane%d" % k, slot_of(k))
+            nc.sync.dma_start(out=plane[:], in_=s_rows[b, t])
+            if k == 0:
+                nc.sync.dma_start(out=price_sb[:], in_=price.rearrange("(b p t) -> p b t", p=P, t=PACK))
+            x = ring.tile([P, S], F32, name="x")
+            nc.vector.tensor_copy(x[:], plane[:].indirect(idx[:]))
+            if t == 0:
+                c_rows[b] = placed([P, HALVES, PACK, HALF], BF16, "c_rows%d" % b, ROWS_AT[b])
+            for half in range(HALVES):
+                nc.scalar.activation(
+                    out=c_rows[b][:, half, t, :],
+                    in_=x[:, half * HALF : (half + 1) * HALF],
+                    func=COPY,
+                    scale=price_sb[:, b, t : t + 1],
+                )
+                if t == PACK - 1:
+                    c_grouped[b, half] = interleave(c_rows[b][:, half, :, :])
+            return x
+
+        def make_slope(k, x, at=None):
+            if at is None:
+                slope[k] = keep.tile([P, S], F32, name="slope%d" % k)
+            else:
+                slope[k] = placed([P, S], F32, "slope%d" % k, at)
+            nc.vector.scalar_tensor_tensor(out=slope[k][:], in0=x[:], scalar=1.0, in1=x[:], op0=SUB, op1=MULT)
+
+        c_mx = {}
+        nc.sync.dma_start(idx[:], offs)
+        make_slope(0, pick_plane(0))
+        make_slope(1, pick_plane(1))
+        grouped = interleave_w1(load_raw(w1[:, 0:PASS]))
+        load_wf_scales(0)
+        make_slope(2, pick_plane(2))
+        load_wf_scales(1)
+        make_slope(3, pick_plane(3))
+        w1_mx = [quantize("w1a", grouped, slot_of(3))]
+        load_wf_scales(2)
+        make_slope(4, pick_plane(4))
+        c_mx[0, 0] = quantize("c00", c_grouped[0, 0], slot_of(4))
+        grouped = interleave_w1(load_raw(w1[:, PASS:H]))
+        load_wf_scales(3)
+        make_slope(5, pick_plane(5))
+        c_mx[0, 1] = quantize("c01", c_grouped[0, 1], slot_of(5))
+        wf_raw = ring.tile([P, BLOCKS, H], I32, name="raw")
+        nc.sync.dma_start(out=wf_raw[:], in_=wf_words.rearrange("a p n t -> p a (n t)").bitcast(I32))
+        nc.vector.tensor_copy(
+            out=wf_w[:].rearrange("p (g t c i) -> p g c t i", t=PACK, c=32, i=4),
+            in_=wf_raw[:].rearrange("p a (b c i t) -> p (a b) c t i", t=PACK, c=32, i=4),
+        )
+        nc.vector.tensor_copy(
+            out=wf_s[:].rearrange("p (b t m) -> p b t m", t=PACK, m=P),
+            in_=wf_s_raw[:].rearrange("p (b m t) -> p b t m", t=PACK, m=P),
+        )
+        w2_grouped = interleave(load_raw(w2[0:PASS, :])[:])
+        make_slope(6, pick_plane(6))
+        w1_mx.append(quantize("w1b", grouped, slot_of(6)))
+        x_last = pick_plane(7)
+        w2_mx = [quantize("w2a", w2_grouped, slot_of(7))]
+        for r in range(4):
+            nc.sync.dma_start(out=tab_s[r:P:32, :].bitcast(I32), in_=tab_s_rows[r])
+        tab_w = placed([P, T], I32, "tab_w", TAB_AT)
+        nc.sync.dma_start(out=tab_w[:], in_=tab_words[0].rearrange("p n t -> p (n t)").bitcast(I32))
+        w2_raw = load_raw(w2[PASS:H, :])
+        nc.sync.dma_start(idx2[:], offs2)
+        nc.sync.dma_start(out=wgo_sb[:], in_=wgo)
+        for half in range(HALVES):
+            picks = idx[:, half * HALF // 16 : (half + 1) * HALF // 16]
+            nc.vector.tensor_copy(v_w[half][:], tab_w[:].bitcast(U32).indirect(picks))
+            nc.vector.tensor_copy(v_s[half][:], tab_s[:].indirect(picks))
+        c_mx[1, 0] = quantize("c10", c_grouped[1, 0], TAB_AT)
+        make_slope(7, x_last, TAB_AT + SLOT // 2)
+        c_mx[1, 1] = quantize("c11", c_grouped[1, 1])
+        w2_mx.append(quantize("w2b", interleave(w2_raw[:])))
+
+        h_mx = {}
+        h_rows = {}
+
+        def feedback_pass(d, a, k, half):
+            nc.tensor.matmul_mx(
+                out=d[:],
+                lhsT=wf_w[:, a * H + k * P : a * H + (k + 1) * P].bitcast(E4),
+                lhsT_scale=wf_s[4 * a : P, k * P : (k + 1) * P],
+                rhs=c_mx[a, half][0][:].bitcast(E4),
+                rhs_scale=c_mx[a, half][1][:],
+                start=(a == 0),
+                stop=(a == BLOCKS - 1),
+            )
+
+        def first_stage(half, b):
+            users = slice(half * HALF, (half + 1) * HALF)
+            if b == 0:
+                h_rows[half] = placed([P, BLOCKS, PACK, HALF], BF16, "h_rows%d" % half, ROWS_AT[half])
+            for t in range(PACK):
+                k = b * PACK + t
+                d = psum.tile([P, HALF], F32, name="d", bufs=6)
+                feedback_pass(d, 0, k, half)
+                nc.tensor.matmul_mx(
+                    out=d[:],
+                    lhsT=w1_mx[b][0][:, t * P : (t + 1) * P].bitcast(E4),
+                    lhsT_scale=w1_mx[b][1][:, t * P : (t + 1) * P],
+                    rhs=v_w[half][:].bitcast(E5),
+                    rhs_scale=v_s[half][:],
+                    start=False,
+                    stop=False,
+                )
+                feedback_pass(d, 1, k, half)
+                nc.vector.scalar_tensor_tensor(
+                    out=h_rows[half][:, b, t, :], in0=d[:], scalar=-1.0, in1=slope[k][:, users], op0=MULT, op1=MULT
+                )
+            h_mx[b, half] = quantize("h%d%d" % (b, half), interleave(h_rows[half][:, b, :, :]))
+
+        def second_stage(half, u, at):
+            users = slice(half * HALF, (half + 1) * HALF)
+            slots = idx2[:, half * HALF // 16 : (half + 1) * HALF // 16]
+            y = psum.tile([P, HALF], F32, name="y", bufs=2)
+            for b in range(BLOCKS):
+                nc.tensor.matmul_mx(
+                    out=y[:],
+                    lhsT=w2_mx[b][0][:, u * P : (u + 1) * P].bitcast(E4),
+                    lhsT_scale=w2_mx[b][1][:, u * P : (u + 1) * P],
+                    rhs=h_mx[b, half][0][:].bitcast(E4),
+                    rhs_scale=h_mx[b, half][1][:],
+                    start=(b == 0),
+                    stop=(b == BLOCKS - 1),
+                )
+            y_sb = placed([P, HALF], F32, "y%d%d" % (half, u), at)
+            nc.scalar.copy(out=y_sb[:], in_=y[:])
+            nc.vector.tensor_tensor(pages[u % PAGES][:].indirect(slots), y_sb[:], wgo_sb[:, users], MULT)
+            if half == HALVES - 1:
+                nc.sync.dma_start(out=out[u * P : (u + 1) * P, :], in_=pages[u % PAGES][:])
+
+        first_stage(0, 0)
+        first_stage(0, 1)
+        first_stage(1, 0)
+        second_stage(0, 0, ROWS_AT[0])
+        first_stage(1, 1)
+        order = [(0, 1), (0, 2), (1, 0), (1, 1), (1, 2), (0, 3), (1, 3)]
+        for n, (half, u) in enumerate(order):
+            at = ROWS_AT[1] + n * 4 * HALF if n < 4 else ROWS_AT[0] + (n - 3) * 4 * HALF
+            second_stage(half, u, at)

@@ -31,10 +31,8 @@ PAGES = NT - 1
 KIB = 1024
 PLANE_SLOTS = 5
 SLOT = 8 * KIB
-TAB_AT = PLANE_SLOTS * SLOT
-ROWS_AT = [TAB_AT + SLOT, TAB_AT + 2 * SLOT]
-CODES = 4 * HALF
-MX_BYTES = CODES + HALF
+ROWS_AT = [PLANE_SLOTS * SLOT, (PLANE_SLOTS + 1) * SLOT]
+POOL_PLANES = (0, 1, 2, 4, 5)
 
 
 def tile_list_handover_gradient_kernel(
@@ -54,26 +52,25 @@ def tile_list_handover_gradient_kernel(
         idx2 = keep.tile([P, S // 16], U16, name="idx2")
         price_sb = keep.tile([P, BLOCKS, PACK], F32, name="price_sb")
         tab_s = keep.tile([P, T], U8, name="tab_s", align_bytes=64)
-        v_w = [keep.tile([P, HALF], U32, name="v_w%d" % h, align_bytes=64) for h in range(HALVES)]
-        v_s = [keep.tile([P, HALF], U8, name="v_s%d" % h, align_bytes=64) for h in range(HALVES)]
+        v_w = keep.tile([P, S], U32, name="v_w", align_bytes=64)
+        v_s = keep.tile([P, S], U8, name="v_s", align_bytes=64)
         wf_s_raw = keep.tile([P, H], U8, name="wf_s_raw", align_bytes=64)
-        wf_s = keep.tile([P, H], U8, name="wf_s", align_bytes=64)
+        tab_w = keep.tile([P, T], I32, name="tab_w", align_bytes=64)
         wf_w = keep.tile([P, BLOCKS * H], I32, name="wf_w", align_bytes=64)
         wgo_sb = keep.tile([P, S], F32, name="wgo_sb")
         pages = [keep.tile([P, T2], F32, name="page%d" % u) for u in range(PAGES)]
 
         def quantize(name, grouped, at=None):
+            codes = keep.tile([P, HALF], U32, name=name + "_w", align_bytes=64)
             if at is None:
-                codes = keep.tile([P, HALF], U32, name=name + "_w", align_bytes=64)
                 scales = keep.tile([P, HALF], U8, name=name + "_s", align_bytes=64)
             else:
-                codes = placed([P, HALF], U32, name + "_w", at)
-                scales = placed([P, HALF], U8, name + "_s", at + CODES)
+                scales = placed([P, HALF], U8, name + "_s", at)
             nc.vector.quantize_mx(out=codes[:].bitcast(E4), scales=scales[:], in_=grouped[:])
             return codes, scales
 
         def interleave(rows):
-            grouped = ring.tile([P, HALF * PACK], BF16, name="grouped", align_bytes=64)
+            grouped = ring.tile([P, HALF * PACK], BF16, name="grouped", align_bytes=64, bufs=5)
             nc.scalar.copy(
                 out=grouped[:].rearrange("p (c i t) -> p c t i", i=4, t=PACK),
                 in_=rows.rearrange("p t (c i) -> p c t i", i=4),
@@ -81,17 +78,17 @@ def tile_list_handover_gradient_kernel(
             return grouped
 
         def interleave_w1(raw):
-            grouped = ring.tile([P, HALF * PACK], BF16, name="grouped", align_bytes=64)
+            grouped = ring.tile([P, HALF * PACK], BF16, name="grouped", align_bytes=64, bufs=5)
             nc.scalar.copy(
                 out=grouped[:].rearrange("p (t m j) -> p m t j", t=PACK, j=PACK),
                 in_=raw[:].rearrange("p j (m t) -> p m t j", t=PACK),
             )
             return grouped
 
-        nc.vector.memset(tab_s[:].bitcast(I32), 0)
-        nc.vector.memset(wf_s_raw[:].bitcast(I32), 0)
+        nc.gpsimd.memset(tab_s[:].bitcast(I32), 0)
+        nc.gpsimd.memset(wf_s_raw[:].bitcast(I32), 0)
         for page in pages:
-            nc.vector.memset(page[:], 0.0)
+            nc.gpsimd.memset(page[:], 0.0)
 
         s_rows = sT.rearrange("(b p t) n -> b t p n", p=P, t=PACK)
         tab_s_rows = tab_scales[0].bitcast(I32).rearrange("(q r) n -> r q n", r=4)
@@ -115,16 +112,26 @@ def tile_list_handover_gradient_kernel(
         c_rows = {}
         c_grouped = {}
 
-        def pick_plane(k):
+        def pick_plane(k, behind_load=None):
             b, t = divmod(k, PACK)
             plane = placed([P, T], F32, "plane%d" % k, slot_of(k))
             nc.sync.dma_start(out=plane[:], in_=s_rows[b, t])
             if k == 0:
                 nc.sync.dma_start(out=price_sb[:], in_=price.rearrange("(b p t) -> p b t", p=P, t=PACK))
-            x = ring.tile([P, S], F32, name="x")
+            if behind_load is not None:
+                behind_load()
+            x = ring.tile([P, S], F32, name="x", bufs=5)
             nc.vector.tensor_copy(x[:], plane[:].indirect(idx[:]))
             if t == 0:
                 c_rows[b] = placed([P, HALVES, PACK, HALF], BF16, "c_rows%d" % b, ROWS_AT[b])
+            if t < PACK - 1:
+                nc.scalar.activation(
+                    out=c_rows[b][:, :, t, :],
+                    in_=x[:].rearrange("p (h j) -> p h j", h=HALVES),
+                    func=COPY,
+                    scale=price_sb[:, b, t : t + 1],
+                )
+                return x
             for half in range(HALVES):
                 nc.scalar.activation(
                     out=c_rows[b][:, half, t, :],
@@ -132,8 +139,7 @@ def tile_list_handover_gradient_kernel(
                     func=COPY,
                     scale=price_sb[:, b, t : t + 1],
                 )
-                if t == PACK - 1:
-                    c_grouped[b, half] = interleave(c_rows[b][:, half, :, :])
+                c_grouped[b, half] = interleave(c_rows[b][:, half, :, :])
             return x
 
         def make_slope(k, x, at=None):
@@ -141,55 +147,55 @@ def tile_list_handover_gradient_kernel(
                 slope[k] = keep.tile([P, S], F32, name="slope%d" % k)
             else:
                 slope[k] = placed([P, S], F32, "slope%d" % k, at)
-            nc.vector.scalar_tensor_tensor(out=slope[k][:], in0=x[:], scalar=1.0, in1=x[:], op0=SUB, op1=MULT)
+            if k in POOL_PLANES:
+                nc.gpsimd.tensor_scalar(slope[k][:], x[:], 1.0, -1.0, MULT, ADD)
+                nc.gpsimd.tensor_tensor(slope[k][:], slope[k][:], x[:], MULT)
+            else:
+                nc.vector.scalar_tensor_tensor(out=slope[k][:], in0=x[:], scalar=1.0, in1=x[:], op0=SUB, op1=MULT)
 
         c_mx = {}
         nc.sync.dma_start(idx[:], offs)
-        make_slope(0, pick_plane(0))
-        make_slope(1, pick_plane(1))
-        grouped = interleave_w1(load_raw(w1[:, 0:PASS]))
-        load_wf_scales(0)
-        make_slope(2, pick_plane(2))
-        load_wf_scales(1)
-        make_slope(3, pick_plane(3))
-        w1_mx = [quantize("w1a", grouped, slot_of(3))]
-        load_wf_scales(2)
-        make_slope(4, pick_plane(4))
-        c_mx[0, 0] = quantize("c00", c_grouped[0, 0], slot_of(4))
-        grouped = interleave_w1(load_raw(w1[:, PASS:H]))
-        load_wf_scales(3)
-        make_slope(5, pick_plane(5))
-        c_mx[0, 1] = quantize("c01", c_grouped[0, 1], slot_of(5))
-        wf_raw = ring.tile([P, BLOCKS, H], I32, name="raw")
-        nc.sync.dma_start(out=wf_raw[:], in_=wf_words.rearrange("a p n t -> p a (n t)").bitcast(I32))
-        nc.vector.tensor_copy(
-            out=wf_w[:].rearrange("p (g t c i) -> p g c t i", t=PACK, c=32, i=4),
-            in_=wf_raw[:].rearrange("p a (b c i t) -> p (a b) c t i", t=PACK, c=32, i=4),
-        )
+        for k in range(3):
+            make_slope(k, pick_plane(k))
+        for r in range(4):
+            nc.sync.dma_start(out=tab_s[r:P:32, :].bitcast(I32), in_=tab_s_rows[r])
+        nc.sync.dma_start(out=tab_w[:], in_=tab_words[0].rearrange("p n t -> p (n t)").bitcast(I32))
+        nc.vector.tensor_copy(v_w[:], tab_w[:].bitcast(U32).indirect(idx[:]))
+        nc.vector.tensor_copy(v_s[:], tab_s[:].indirect(idx[:]))
+        w1_grouped = [interleave_w1(load_raw(w1[:, 0:PASS]))]
+        for q in range(4):
+            load_wf_scales(q)
+        x = pick_plane(3, lambda: w1_grouped.append(interleave_w1(load_raw(w1[:, PASS:H]))))
+        make_slope(3, x)
+        w1_mx = [quantize("w1a", w1_grouped[0], slot_of(3))]
+        wf_s = placed([P, H], U8, "wf_s", slot_of(3) + HALF)
         nc.vector.tensor_copy(
             out=wf_s[:].rearrange("p (b t m) -> p b t m", t=PACK, m=P),
             in_=wf_s_raw[:].rearrange("p (b m t) -> p b t m", t=PACK, m=P),
         )
-        w2_grouped = interleave(load_raw(w2[0:PASS, :])[:])
-        make_slope(6, pick_plane(6))
-        w1_mx.append(quantize("w1b", grouped, slot_of(6)))
-        x_last = pick_plane(7)
-        w2_mx = [quantize("w2a", w2_grouped, slot_of(7))]
-        for r in range(4):
-            nc.sync.dma_start(out=tab_s[r:P:32, :].bitcast(I32), in_=tab_s_rows[r])
-        tab_w = placed([P, T], I32, "tab_w", TAB_AT)
-        nc.sync.dma_start(out=tab_w[:], in_=tab_words[0].rearrange("p n t -> p (n t)").bitcast(I32))
-        w2_raw = load_raw(w2[PASS:H, :])
+        make_slope(4, pick_plane(4))
+        make_slope(5, pick_plane(5))
+        x6 = pick_plane(6)
+        x7 = pick_plane(7)
+        wf_raw = ring.tile([P, BLOCKS, H], I32, name="raw")
+        nc.sync.dma_start(out=wf_raw[:], in_=wf_words.rearrange("a p n t -> p a (n t)").bitcast(I32))
+        w2_raw = [load_raw(w2[b * PASS : (b + 1) * PASS, :]) for b in range(BLOCKS)]
         nc.sync.dma_start(idx2[:], offs2)
         nc.sync.dma_start(out=wgo_sb[:], in_=wgo)
-        for half in range(HALVES):
-            picks = idx[:, half * HALF // 16 : (half + 1) * HALF // 16]
-            nc.vector.tensor_copy(v_w[half][:], tab_w[:].bitcast(U32).indirect(picks))
-            nc.vector.tensor_copy(v_s[half][:], tab_s[:].indirect(picks))
-        c_mx[1, 0] = quantize("c10", c_grouped[1, 0], TAB_AT)
-        make_slope(7, x_last, TAB_AT + SLOT // 2)
+
+        late = slot_of(7)
+        c_mx[0, 0] = quantize("c00", c_grouped[0, 0], late)
+        nc.vector.tensor_copy(
+            out=wf_w[:].rearrange("p (g t c i) -> p g c t i", t=PACK, c=32, i=4),
+            in_=wf_raw[:].rearrange("p a (b c i t) -> p (a b) c t i", t=PACK, c=32, i=4),
+        )
+        w1_mx.append(quantize("w1b", w1_grouped[1], late + HALF))
+        c_mx[0, 1] = quantize("c01", c_grouped[0, 1], late + 2 * HALF)
+        make_slope(6, x6, late + SLOT // 2)
+        make_slope(7, x7)
+        c_mx[1, 0] = quantize("c10", c_grouped[1, 0])
         c_mx[1, 1] = quantize("c11", c_grouped[1, 1])
-        w2_mx.append(quantize("w2b", interleave(w2_raw[:])))
+        w2_mx = [quantize("w2%d" % b, interleave(w2_raw[b][:])) for b in range(BLOCKS)]
 
         h_mx = {}
         h_rows = {}
@@ -201,7 +207,7 @@ def tile_list_handover_gradient_kernel(
                 lhsT_scale=wf_s[4 * a : P, k * P : (k + 1) * P],
                 rhs=c_mx[a, half][0][:].bitcast(E4),
                 rhs_scale=c_mx[a, half][1][:],
-                start=(a == 0),
+                start=False,
                 stop=(a == BLOCKS - 1),
             )
 
@@ -212,16 +218,16 @@ def tile_list_handover_gradient_kernel(
             for t in range(PACK):
                 k = b * PACK + t
                 d = psum.tile([P, HALF], F32, name="d", bufs=6)
-                feedback_pass(d, 0, k, half)
                 nc.tensor.matmul_mx(
                     out=d[:],
                     lhsT=w1_mx[b][0][:, t * P : (t + 1) * P].bitcast(E4),
                     lhsT_scale=w1_mx[b][1][:, t * P : (t + 1) * P],
-                    rhs=v_w[half][:].bitcast(E5),
-                    rhs_scale=v_s[half][:],
-                    start=False,
+                    rhs=v_w[:, users].bitcast(E5),
+                    rhs_scale=v_s[:, users],
+                    start=True,
                     stop=False,
                 )
+                feedback_pass(d, 0, k, half)
                 feedback_pass(d, 1, k, half)
                 nc.vector.scalar_tensor_tensor(
                     out=h_rows[half][:, b, t, :], in0=d[:], scalar=-1.0, in1=slope[k][:, users], op0=MULT, op1=MULT

@@ -32,7 +32,8 @@ KIB = 1024
 PLANE_SLOTS = 5
 SLOT = 8 * KIB
 ROWS_AT = [PLANE_SLOTS * SLOT, (PLANE_SLOTS + 1) * SLOT]
-POOL_PLANES = (0, 1, 2, 4, 5)
+POOL_PLANES = 6
+SCALAR_PLANES = 2
 
 
 def tile_list_handover_gradient_kernel(
@@ -69,8 +70,11 @@ def tile_list_handover_gradient_kernel(
             nc.vector.quantize_mx(out=codes[:].bitcast(E4), scales=scales[:], in_=grouped[:])
             return codes, scales
 
-        def interleave(rows):
-            grouped = ring.tile([P, HALF * PACK], BF16, name="grouped", align_bytes=64, bufs=5)
+        def interleave(rows, name=None, at=None):
+            if at is None:
+                grouped = ring.tile([P, HALF * PACK], BF16, name="grouped", align_bytes=64, bufs=5)
+            else:
+                grouped = placed([P, HALF * PACK], BF16, name, at)
             nc.scalar.copy(
                 out=grouped[:].rearrange("p (c i t) -> p c t i", i=4, t=PACK),
                 in_=rows.rearrange("p t (c i) -> p c t i", i=4),
@@ -112,16 +116,17 @@ def tile_list_handover_gradient_kernel(
         c_rows = {}
         c_grouped = {}
 
-        def pick_plane(k, behind_load=None):
+        def pick_plane(k):
             b, t = divmod(k, PACK)
             plane = placed([P, T], F32, "plane%d" % k, slot_of(k))
             nc.sync.dma_start(out=plane[:], in_=s_rows[b, t])
             if k == 0:
                 nc.sync.dma_start(out=price_sb[:], in_=price.rearrange("(b p t) -> p b t", p=P, t=PACK))
-            if behind_load is not None:
-                behind_load()
             x = ring.tile([P, S], F32, name="x", bufs=5)
             nc.vector.tensor_copy(x[:], plane[:].indirect(idx[:]))
+            if k < SCALAR_PLANES:
+                slope[k] = keep.tile([P, S], F32, name="slope%d" % k)
+                nc.scalar.activation(out=slope[k][:], in_=x[:], func=COPY, bias=-1.0)
             if t == 0:
                 c_rows[b] = placed([P, HALVES, PACK, HALF], BF16, "c_rows%d" % b, ROWS_AT[b])
             if t < PACK - 1:
@@ -139,23 +144,25 @@ def tile_list_handover_gradient_kernel(
                     func=COPY,
                     scale=price_sb[:, b, t : t + 1],
                 )
-                c_grouped[b, half] = interleave(c_rows[b][:, half, :, :])
+                at = slot_of(k) if (b, half) == (0, 1) else None
+                c_grouped[b, half] = interleave(c_rows[b][:, half, :, :], "c01_grouped", at)
             return x
 
         def make_slope(k, x, at=None):
-            if at is None:
-                slope[k] = keep.tile([P, S], F32, name="slope%d" % k)
-            else:
+            if at is not None:
                 slope[k] = placed([P, S], F32, "slope%d" % k, at)
-            if k in POOL_PLANES:
-                nc.gpsimd.tensor_scalar(slope[k][:], x[:], 1.0, -1.0, MULT, ADD)
+            elif k >= SCALAR_PLANES:
+                slope[k] = keep.tile([P, S], F32, name="slope%d" % k)
+            if k < POOL_PLANES:
+                if k >= SCALAR_PLANES:
+                    nc.gpsimd.tensor_scalar(slope[k][:], x[:], 1.0, -1.0, MULT, ADD)
                 nc.gpsimd.tensor_tensor(slope[k][:], slope[k][:], x[:], MULT)
             else:
                 nc.vector.scalar_tensor_tensor(out=slope[k][:], in0=x[:], scalar=1.0, in1=x[:], op0=SUB, op1=MULT)
 
         c_mx = {}
         nc.sync.dma_start(idx[:], offs)
-        for k in range(3):
+        for k in range(PACK):
             make_slope(k, pick_plane(k))
         for r in range(4):
             nc.sync.dma_start(out=tab_s[r:P:32, :].bitcast(I32), in_=tab_s_rows[r])
@@ -165,15 +172,17 @@ def tile_list_handover_gradient_kernel(
         w1_grouped = [interleave_w1(load_raw(w1[:, 0:PASS]))]
         for q in range(4):
             load_wf_scales(q)
-        x = pick_plane(3, lambda: w1_grouped.append(interleave_w1(load_raw(w1[:, PASS:H]))))
-        make_slope(3, x)
-        w1_mx = [quantize("w1a", w1_grouped[0], slot_of(3))]
-        wf_s = placed([P, H], U8, "wf_s", slot_of(3) + HALF)
+        x4 = pick_plane(4)
+        w1_grouped.append(interleave_w1(load_raw(w1[:, PASS:H])))
+        middle = slot_of(4)
+        c_mx[0, 0] = quantize("c00", c_grouped[0, 0], middle)
+        wf_s = placed([P, H], U8, "wf_s", middle + 2 * HALF)
         nc.vector.tensor_copy(
             out=wf_s[:].rearrange("p (b t m) -> p b t m", t=PACK, m=P),
             in_=wf_s_raw[:].rearrange("p (b m t) -> p b t m", t=PACK, m=P),
         )
-        make_slope(4, pick_plane(4))
+        c_mx[0, 1] = quantize("c01", c_grouped[0, 1], middle + HALF)
+        make_slope(4, x4, slot_of(3))
         make_slope(5, pick_plane(5))
         x6 = pick_plane(6)
         x7 = pick_plane(7)
@@ -184,13 +193,12 @@ def tile_list_handover_gradient_kernel(
         nc.sync.dma_start(out=wgo_sb[:], in_=wgo)
 
         late = slot_of(7)
-        c_mx[0, 0] = quantize("c00", c_grouped[0, 0], late)
+        w1_mx = [quantize("w1a", w1_grouped[0], late)]
         nc.vector.tensor_copy(
             out=wf_w[:].rearrange("p (g t c i) -> p g c t i", t=PACK, c=32, i=4),
             in_=wf_raw[:].rearrange("p a (b c i t) -> p (a b) c t i", t=PACK, c=32, i=4),
         )
         w1_mx.append(quantize("w1b", w1_grouped[1], late + HALF))
-        c_mx[0, 1] = quantize("c01", c_grouped[0, 1], late + 2 * HALF)
         make_slope(6, x6, late + SLOT // 2)
         make_slope(7, x7)
         c_mx[1, 0] = quantize("c10", c_grouped[1, 0])

@@ -26,14 +26,19 @@ BLOCKS = H // PASS
 HALVES = S // HALF
 PLANES = BLOCKS * PACK
 NT = N // P
-PAGES = NT - 1
+COLS = N // 2
 
 KIB = 1024
-PLANE_SLOTS = 5
-SLOT = 8 * KIB
-ROWS_AT = [PLANE_SLOTS * SLOT, (PLANE_SLOTS + 1) * SLOT]
-POOL_PLANES = 6
-SCALAR_PLANES = 2
+PRICE_AT = 0
+BASE = KIB
+SLOT = [BASE + 8 * KIB, BASE + 16 * KIB, 64, BASE + 24 * KIB, BASE + 32 * KIB]
+ROWS = [BASE + 40 * KIB, BASE + 48 * KIB]
+GROUPED = [BASE + (56 + 4 * g) * KIB for g in range(3)]
+XS = [BASE + (68 + 4 * g) * KIB for g in range(6)]
+PAGE1 = BASE + 92 * KIB
+PAGE2 = BASE + 100 * KIB
+PAGE3 = BASE + 108 * KIB
+SCALAR_PLANES = 4
 
 
 def tile_list_handover_gradient_kernel(
@@ -42,215 +47,241 @@ def tile_list_handover_gradient_kernel(
     nc = tc.nc
     with ExitStack() as ctx:
         keep = ctx.enter_context(tc.tile_pool(name="keep", bufs=1))
-        ring = ctx.enter_context(tc.tile_pool(name="ring", bufs=3))
         arena = ctx.enter_context(tc.tile_pool(name="arena", bufs=1))
         psum = ctx.enter_context(tc.psum_pool(name="psum", bufs=1))
 
-        def placed(shape, dtype, name, at):
+        def placed(shape, dtype, name, at=None):
+            if at is None:
+                return keep.tile(shape, dtype, name=name, align_bytes=64)
             return arena.tile(shape, dtype, name=name, align_bytes=64, offset=at)
 
         idx = keep.tile([P, S // 16], U16, name="idx")
         idx2 = keep.tile([P, S // 16], U16, name="idx2")
-        price_sb = keep.tile([P, BLOCKS, PACK], F32, name="price_sb")
-        tab_s = keep.tile([P, T], U8, name="tab_s", align_bytes=64)
-        v_w = keep.tile([P, S], U32, name="v_w", align_bytes=64)
-        v_s = keep.tile([P, S], U8, name="v_s", align_bytes=64)
-        wf_s_raw = keep.tile([P, H], U8, name="wf_s_raw", align_bytes=64)
-        tab_w = keep.tile([P, T], I32, name="tab_w", align_bytes=64)
-        wf_w = keep.tile([P, BLOCKS * H], I32, name="wf_w", align_bytes=64)
-        wgo_sb = keep.tile([P, S], F32, name="wgo_sb")
-        pages = [keep.tile([P, T2], F32, name="page%d" % u) for u in range(PAGES)]
 
-        def quantize(name, grouped, at=None):
-            codes = keep.tile([P, HALF], U32, name=name + "_w", align_bytes=64)
-            if at is None:
-                scales = keep.tile([P, HALF], U8, name=name + "_s", align_bytes=64)
-            else:
-                scales = placed([P, HALF], U8, name + "_s", at)
+        def quantize(name, grouped, width=HALF, at=None):
+            codes = placed([P, width], U32, name + "_w")
+            scales = placed([P, width], U8, name + "_s", at)
             nc.vector.quantize_mx(out=codes[:].bitcast(E4), scales=scales[:], in_=grouped[:])
             return codes, scales
 
-        def interleave(rows, name=None, at=None):
-            if at is None:
-                grouped = ring.tile([P, HALF * PACK], BF16, name="grouped", align_bytes=64, bufs=5)
-            else:
-                grouped = placed([P, HALF * PACK], BF16, name, at)
+        def interleave(name, rows, at=None, width=HALF):
+            grouped = placed([P, width * PACK], BF16, name + "_g", at)
             nc.scalar.copy(
                 out=grouped[:].rearrange("p (c i t) -> p c t i", i=4, t=PACK),
                 in_=rows.rearrange("p t (c i) -> p c t i", i=4),
             )
             return grouped
 
-        def interleave_w1(raw):
-            grouped = ring.tile([P, HALF * PACK], BF16, name="grouped", align_bytes=64, bufs=5)
+        def interleave_w1(name, raw, at=None):
+            grouped = placed([P, HALF * PACK], BF16, name + "_g", at)
             nc.scalar.copy(
                 out=grouped[:].rearrange("p (t m j) -> p m t j", t=PACK, j=PACK),
                 in_=raw[:].rearrange("p j (m t) -> p m t j", t=PACK),
             )
             return grouped
 
-        nc.gpsimd.memset(tab_s[:].bitcast(I32), 0)
-        nc.gpsimd.memset(wf_s_raw[:].bitcast(I32), 0)
-        for page in pages:
-            nc.gpsimd.memset(page[:], 0.0)
-
-        s_rows = sT.rearrange("(b p t) n -> b t p n", p=P, t=PACK)
-        tab_s_rows = tab_scales[0].bitcast(I32).rearrange("(q r) n -> r q n", r=4)
-        wf_s_rows = wf_scales.bitcast(I32)
-
-        def slot_of(k):
-            return (k % PLANE_SLOTS) * SLOT
-
-        def load_wf_scales(q):
-            nc.sync.dma_start(
-                out=wf_s_raw[32 * q : 32 * q + 4 * BLOCKS, :].bitcast(I32),
-                in_=wf_s_rows[:, 4 * q : 4 * q + 4, :],
-            )
-
-        def load_raw(rows):
-            raw = ring.tile([P, PACK, HALF], F32, name="raw")
+        def load_raw(name, rows, at):
+            raw = placed([P, PACK, HALF], F32, name, at)
             nc.sync.dma_start(out=raw[:], in_=rows.rearrange("(p j) c -> p j c", j=PACK))
             return raw
 
-        slope = {}
-        c_rows = {}
-        c_grouped = {}
+        def load_wf(a, at):
+            raw = placed([P, H], I32, "wf_raw%d" % a, at)
+            nc.sync.dma_start(out=raw[:], in_=wf_words[a].rearrange("p n t -> p (n t)").bitcast(I32))
+            return raw
 
-        def pick_plane(k):
-            b, t = divmod(k, PACK)
-            plane = placed([P, T], F32, "plane%d" % k, slot_of(k))
-            nc.sync.dma_start(out=plane[:], in_=s_rows[b, t])
-            if k == 0:
-                nc.sync.dma_start(out=price_sb[:], in_=price.rearrange("(b p t) -> p b t", p=P, t=PACK))
-            x = ring.tile([P, S], F32, name="x", bufs=5)
-            nc.vector.tensor_copy(x[:], plane[:].indirect(idx[:]))
-            if k < SCALAR_PLANES:
-                slope[k] = keep.tile([P, S], F32, name="slope%d" % k)
-                nc.scalar.activation(out=slope[k][:], in_=x[:], func=COPY, bias=-1.0)
-            if t == 0:
-                c_rows[b] = placed([P, HALVES, PACK, HALF], BF16, "c_rows%d" % b, ROWS_AT[b])
-            if t < PACK - 1:
-                nc.scalar.activation(
-                    out=c_rows[b][:, :, t, :],
-                    in_=x[:].rearrange("p (h j) -> p h j", h=HALVES),
-                    func=COPY,
-                    scale=price_sb[:, b, t : t + 1],
-                )
-                return x
-            for half in range(HALVES):
-                nc.scalar.activation(
-                    out=c_rows[b][:, half, t, :],
-                    in_=x[:, half * HALF : (half + 1) * HALF],
-                    func=COPY,
-                    scale=price_sb[:, b, t : t + 1],
-                )
-                at = slot_of(k) if (b, half) == (0, 1) else None
-                c_grouped[b, half] = interleave(c_rows[b][:, half, :, :], "c01_grouped", at)
-            return x
+        def deal_wf(a, raw, at=None):
+            words = placed([P, H], I32, "wf_w%d" % a, at)
+            nc.vector.tensor_copy(
+                out=words[:].rearrange("p (b t c i) -> p b c t i", t=PACK, c=32, i=4),
+                in_=raw[:].rearrange("p (b c i t) -> p b c t i", t=PACK, c=32, i=4),
+            )
+            return words
 
-        def make_slope(k, x, at=None):
-            if at is not None:
-                slope[k] = placed([P, S], F32, "slope%d" % k, at)
-            elif k >= SCALAR_PLANES:
-                slope[k] = keep.tile([P, S], F32, name="slope%d" % k)
-            if k < POOL_PLANES:
-                if k >= SCALAR_PLANES:
-                    nc.gpsimd.tensor_scalar(slope[k][:], x[:], 1.0, -1.0, MULT, ADD)
-                nc.gpsimd.tensor_tensor(slope[k][:], slope[k][:], x[:], MULT)
-            else:
-                nc.vector.scalar_tensor_tensor(out=slope[k][:], in0=x[:], scalar=1.0, in1=x[:], op0=SUB, op1=MULT)
+        s_rows = sT.rearrange("(b p t) n -> b t p n", p=P, t=PACK)
 
-        c_mx = {}
+        def load_plane(k):
+            plane = placed([P, T], F32, "plane%d" % k, SLOT[k % 5])
+            nc.sync.dma_start(out=plane[:], in_=s_rows[k // PACK, k % PACK])
+            return plane
+
+        wf_s_raw = placed([P, H], U8, "wf_s_raw", PAGE1)
+        tab_s = placed([P, T], U8, "tab_s", PRICE_AT)
+        pages = [placed([P, T2], F32, "page0")]
+        nc.gpsimd.memset(wf_s_raw[:].bitcast(I32), 0)
+        nc.gpsimd.memset(tab_s[32:64, :].bitcast(I32), 0)
+        nc.gpsimd.memset(tab_s[64:P, :].bitcast(I32), 0)
+        nc.gpsimd.memset(pages[0][:], 0.0)
+
         nc.sync.dma_start(idx[:], offs)
-        for k in range(PACK):
-            make_slope(k, pick_plane(k))
-        for r in range(4):
-            nc.sync.dma_start(out=tab_s[r:P:32, :].bitcast(I32), in_=tab_s_rows[r])
-        nc.sync.dma_start(out=tab_w[:], in_=tab_words[0].rearrange("p n t -> p (n t)").bitcast(I32))
-        nc.vector.tensor_copy(v_w[:], tab_w[:].bitcast(U32).indirect(idx[:]))
-        nc.vector.tensor_copy(v_s[:], tab_s[:].indirect(idx[:]))
-        w1_grouped = [interleave_w1(load_raw(w1[:, 0:PASS]))]
+        nc.sync.dma_start(
+            out=tab_s[0:32, :].bitcast(I32),
+            in_=tab_scales[0].bitcast(I32).unsqueeze(1).to_broadcast([16, 2, T // 4]),
+        )
+        wf_raw0 = load_wf(0, SLOT[4] - 2 * KIB)
+        planes = [load_plane(0), load_plane(1)]
         for q in range(4):
-            load_wf_scales(q)
-        x4 = pick_plane(4)
-        w1_grouped.append(interleave_w1(load_raw(w1[:, PASS:H])))
-        middle = slot_of(4)
-        c_mx[0, 0] = quantize("c00", c_grouped[0, 0], middle)
-        wf_s = placed([P, H], U8, "wf_s", middle + 2 * HALF)
+            nc.scalar.dma_start(
+                out=wf_s_raw[32 * q : 32 * q + 4 * BLOCKS, :].bitcast(I32),
+                in_=wf_scales.bitcast(I32)[:, 4 * q : 4 * q + 4, :],
+            )
+
+        v_s_raw = placed([P, S], U8, "v_s_raw")
+        nc.vector.tensor_copy(v_s_raw[:], tab_s[:].indirect(idx[:]))
+        wf_w = [deal_wf(0, wf_raw0)]
+        wf_s = placed([P, H], U8, "wf_s")
         nc.vector.tensor_copy(
             out=wf_s[:].rearrange("p (b t m) -> p b t m", t=PACK, m=P),
             in_=wf_s_raw[:].rearrange("p (b m t) -> p b t m", t=PACK, m=P),
         )
-        c_mx[0, 1] = quantize("c01", c_grouped[0, 1], middle + HALF)
-        make_slope(4, x4, slot_of(3))
-        make_slope(5, pick_plane(5))
-        x6 = pick_plane(6)
-        x7 = pick_plane(7)
-        wf_raw = ring.tile([P, BLOCKS, H], I32, name="raw")
-        nc.sync.dma_start(out=wf_raw[:], in_=wf_words.rearrange("a p n t -> p a (n t)").bitcast(I32))
-        w2_raw = [load_raw(w2[b * PASS : (b + 1) * PASS, :]) for b in range(BLOCKS)]
-        nc.sync.dma_start(idx2[:], offs2)
+        price_sb = placed([P, BLOCKS, PACK], F32, "price_sb", PRICE_AT)
+        nc.sync.dma_start(out=price_sb[:], in_=price.rearrange("(b p t) -> p b t", p=P, t=PACK))
+        v_s = placed([P, S], U8, "v_s")
+        for r in range(4):
+            nc.sync.dma_start(out=v_s[r:P:32, :].bitcast(I32), in_=v_s_raw[2 * r : 32 : 8, :].bitcast(I32))
+        pages.append(placed([P, T2], F32, "page1", PAGE1))
+        nc.gpsimd.memset(pages[1][:], 0.0)
+
+        x_at = [XS[0], XS[1], XS[2], XS[3], XS[4], XS[5], XS[0], XS[2]]
+        xs = {}
+        slope = {}
+        c_rows = {}
+        c_grouped = {}
+
+        def price_rows(k, halves):
+            b, t = divmod(k, PACK)
+            lo, hi = halves[0], halves[-1] + 1
+            nc.scalar.activation(
+                out=c_rows[b][:, lo:hi, t, :],
+                in_=xs[k][:, lo * HALF : hi * HALF].rearrange("p (h j) -> p h j", j=HALF),
+                func=COPY,
+                scale=price_sb[:, b, t : t + 1],
+            )
+
+        def pool_slope(k, first, width, at=None):
+            x = xs[k][:, first * HALF : first * HALF + width]
+            tile = placed([P, width], F32, "slope%d_%d" % (k, first), at)
+            if k < SCALAR_PLANES:
+                nc.scalar.activation(out=tile[:], in_=x, func=COPY, bias=-1.0)
+            else:
+                nc.gpsimd.tensor_scalar(tile[:], x, 1.0, -1.0, MULT, ADD)
+            nc.gpsimd.tensor_tensor(tile[:], tile[:], x, MULT)
+            for half in range(width // HALF):
+                slope[k, first + half] = tile[:, half * HALF : (half + 1) * HALF]
+
+        def vector_slope(k, at):
+            tile = placed([P, S], F32, "slope%d" % k, at)
+            nc.vector.scalar_tensor_tensor(out=tile[:], in0=xs[k][:], scalar=1.0, in1=xs[k][:], op0=SUB, op1=MULT)
+            for half in range(HALVES):
+                slope[k, half] = tile[:, half * HALF : (half + 1) * HALF]
+
+        for k in range(PLANES):
+            b, t = divmod(k, PACK)
+            if k >= 2:
+                planes.append(load_plane(k))
+            xs[k] = placed([P, S], F32, "x%d" % k, x_at[k])
+            nc.vector.tensor_copy(xs[k][:], planes[k][:].indirect(idx[:]))
+            if t == 0:
+                c_rows[b] = placed([P, HALVES, PACK, HALF], BF16, "c_rows%d" % b, ROWS[b])
+            if k < PLANES - 2:
+                pool_slope(k, 0, S if k < PLANES - 3 else HALF)
+            if k < PLANES - 1:
+                price_rows(k, [0, 1])
+            if k == PACK - 1:
+                for half in range(HALVES):
+                    c_grouped[0, half] = interleave("c0%d" % half, c_rows[0][:, half, :, :], GROUPED[half])
+
+        c_mx = {}
+        c_mx[0, 0] = quantize("c00", c_grouped[0, 0], at=SLOT[2])
+        pool_slope(PLANES - 3, 1, HALF, GROUPED[0])
+
+        wf_raw1 = load_wf(1, XS[1])
+        tab_w = placed([P, T], I32, "tab_w", SLOT[3])
+        nc.sync.dma_start(out=tab_w[:], in_=tab_words[0].rearrange("p n t -> p (n t)").bitcast(I32))
+        w1_raw = [load_raw("w1_raw0", w1[:, 0:PASS], SLOT[4]), load_raw("w1_raw1", w1[:, PASS:H], SLOT[0])]
+        w2_raw = [load_raw("w2_raw0", w2[0:PASS, :], SLOT[1]), load_raw("w2_raw1", w2[PASS:H, :], BASE)]
+        wgo_sb = placed([P, S], F32, "wgo_sb", XS[4])
         nc.sync.dma_start(out=wgo_sb[:], in_=wgo)
+        nc.sync.dma_start(idx2[:], offs2)
 
-        late = slot_of(7)
-        w1_mx = [quantize("w1a", w1_grouped[0], late)]
-        nc.vector.tensor_copy(
-            out=wf_w[:].rearrange("p (g t c i) -> p g c t i", t=PACK, c=32, i=4),
-            in_=wf_raw[:].rearrange("p a (b c i t) -> p (a b) c t i", t=PACK, c=32, i=4),
-        )
-        w1_mx.append(quantize("w1b", w1_grouped[1], late + HALF))
-        make_slope(6, x6, late + SLOT // 2)
-        make_slope(7, x7)
-        c_mx[1, 0] = quantize("c10", c_grouped[1, 0])
-        c_mx[1, 1] = quantize("c11", c_grouped[1, 1])
-        w2_mx = [quantize("w2%d" % b, interleave(w2_raw[b][:])) for b in range(BLOCKS)]
+        v_w = placed([P, S], U32, "v_w")
+        nc.vector.tensor_copy(v_w[:], tab_w[:].bitcast(U32).indirect(idx[:]))
 
-        h_mx = {}
+        price_rows(PLANES - 1, [0])
+        c_grouped[1, 0] = interleave("c10", c_rows[1][:, 0, :, :], GROUPED[2])
+        w1_grouped = [interleave_w1("w1a", w1_raw[0], PAGE2)]
+        w1_grouped.append(interleave_w1("w1b", w1_raw[1], PAGE3 + 4 * KIB))
+        price_rows(PLANES - 1, [1])
+        c_grouped[1, 1] = interleave("c11", c_rows[1][:, 1, :, :], SLOT[0])
+
+        after = SLOT[3]
+        wf_w.append(deal_wf(1, wf_raw1, after + 4 * KIB))
+        c_mx[1, 0] = quantize("c10", c_grouped[1, 0], at=after)
+        c_mx[0, 1] = quantize("c01", c_grouped[0, 1], at=after + HALF)
+        vector_slope(PLANES - 2, GROUPED[2])
+        w1_mx = [quantize("w1a", w1_grouped[0])]
+        vector_slope(PLANES - 1, SLOT[4] + 4 * KIB)
+
         h_rows = {}
+        h_mx = {}
+        w2_mx = {}
+        rows_at = {(0, 0): ROWS[0], (1, 0): ROWS[0] + 4 * KIB, (0, 1): ROWS[1], (1, 1): ROWS[1] + 4 * KIB}
 
         def feedback_pass(d, a, k, half):
             nc.tensor.matmul_mx(
                 out=d[:],
-                lhsT=wf_w[:, a * H + k * P : a * H + (k + 1) * P].bitcast(E4),
+                lhsT=wf_w[a][:, k * P : (k + 1) * P].bitcast(E4),
                 lhsT_scale=wf_s[4 * a : P, k * P : (k + 1) * P],
                 rhs=c_mx[a, half][0][:].bitcast(E4),
                 rhs_scale=c_mx[a, half][1][:],
-                start=False,
-                stop=(a == BLOCKS - 1),
+                start=(a == 0),
+                stop=False,
             )
 
-        def first_stage(half, b):
+        def table_pass(d, k, half):
+            b, t = divmod(k, PACK)
             users = slice(half * HALF, (half + 1) * HALF)
-            if b == 0:
-                h_rows[half] = placed([P, BLOCKS, PACK, HALF], BF16, "h_rows%d" % half, ROWS_AT[half])
+            nc.tensor.matmul_mx(
+                out=d[:],
+                lhsT=w1_mx[b][0][:, t * P : (t + 1) * P].bitcast(E4),
+                lhsT_scale=w1_mx[b][1][:, t * P : (t + 1) * P],
+                rhs=v_w[:, users].bitcast(E5),
+                rhs_scale=v_s[:, users],
+                start=False,
+                stop=True,
+            )
+
+        banks = {}
+
+        def feedback(a, b, half):
+            if a == 0:
+                h_rows[b, half] = placed([P, PACK, HALF], BF16, "h_rows%d%d" % (b, half), rows_at[b, half])
+                banks[b, half] = [psum.tile([P, HALF], F32, name="acc", bufs=8) for t in range(PACK)]
             for t in range(PACK):
+                feedback_pass(banks[b, half][t], a, b * PACK + t, half)
+
+        def close_tiles(b, half, tiles):
+            for t in tiles:
                 k = b * PACK + t
-                d = psum.tile([P, HALF], F32, name="d", bufs=6)
-                nc.tensor.matmul_mx(
-                    out=d[:],
-                    lhsT=w1_mx[b][0][:, t * P : (t + 1) * P].bitcast(E4),
-                    lhsT_scale=w1_mx[b][1][:, t * P : (t + 1) * P],
-                    rhs=v_w[:, users].bitcast(E5),
-                    rhs_scale=v_s[:, users],
-                    start=True,
-                    stop=False,
-                )
-                feedback_pass(d, 0, k, half)
-                feedback_pass(d, 1, k, half)
+                d = banks[b, half][t]
+                table_pass(d, k, half)
                 nc.vector.scalar_tensor_tensor(
-                    out=h_rows[half][:, b, t, :], in0=d[:], scalar=-1.0, in1=slope[k][:, users], op0=MULT, op1=MULT
+                    out=h_rows[b, half][:, t, :], in0=slope[k, half], scalar=-1.0, in1=d[:], op0=MULT, op1=MULT
                 )
-            h_mx[b, half] = quantize("h%d%d" % (b, half), interleave(h_rows[half][:, b, :, :]))
+
+        def cast_w2(b, part, at):
+            return interleave("w2_%d%d" % (b, part), w2_raw[b][:, :, part * COLS : (part + 1) * COLS], at, COLS)
 
         def second_stage(half, u, at):
             users = slice(half * HALF, (half + 1) * HALF)
             slots = idx2[:, half * HALF // 16 : (half + 1) * HALF // 16]
-            y = psum.tile([P, HALF], F32, name="y", bufs=2)
+            part, col = divmod(u * P, COLS)
+            y = psum.tile([P, HALF], F32, name="acc", bufs=8)
             for b in range(BLOCKS):
                 nc.tensor.matmul_mx(
                     out=y[:],
-                    lhsT=w2_mx[b][0][:, u * P : (u + 1) * P].bitcast(E4),
-                    lhsT_scale=w2_mx[b][1][:, u * P : (u + 1) * P],
+                    lhsT=w2_mx[b, part][0][:, col : col + P].bitcast(E4),
+                    lhsT_scale=w2_mx[b, part][1][:, col : col + P],
                     rhs=h_mx[b, half][0][:].bitcast(E4),
                     rhs_scale=h_mx[b, half][1][:],
                     start=(b == 0),
@@ -258,16 +289,41 @@ def tile_list_handover_gradient_kernel(
                 )
             y_sb = placed([P, HALF], F32, "y%d%d" % (half, u), at)
             nc.scalar.copy(out=y_sb[:], in_=y[:])
-            nc.vector.tensor_tensor(pages[u % PAGES][:].indirect(slots), y_sb[:], wgo_sb[:, users], MULT)
+            nc.vector.tensor_tensor(pages[u][:].indirect(slots), y_sb[:], wgo_sb[:, users], MULT)
             if half == HALVES - 1:
-                nc.sync.dma_start(out=out[u * P : (u + 1) * P, :], in_=pages[u % PAGES][:])
+                nc.sync.dma_start(out=out[u * P : (u + 1) * P, :], in_=pages[u][:])
 
-        first_stage(0, 0)
-        first_stage(0, 1)
-        first_stage(1, 0)
-        second_stage(0, 0, ROWS_AT[0])
-        first_stage(1, 1)
-        order = [(0, 1), (0, 2), (1, 0), (1, 1), (1, 2), (0, 3), (1, 3)]
-        for n, (half, u) in enumerate(order):
-            at = ROWS_AT[1] + n * 4 * HALF if n < 4 else ROWS_AT[0] + (n - 3) * 4 * HALF
-            second_stage(half, u, at)
+        for a in range(BLOCKS):
+            for b in range(BLOCKS):
+                feedback(a, b, 0)
+        close_tiles(0, 0, range(PACK))
+        w1_mx.append(quantize("w1b", w1_grouped[1]))
+        feedback(0, 0, 1)
+        close_tiles(1, 0, range(PACK))
+        c_mx[1, 1] = quantize("c11", c_grouped[1, 1])
+        h_mx[0, 0] = quantize("h00", interleave("h00", h_rows[0, 0][:], XS[0]))
+        h10_grouped = interleave("h10", h_rows[1, 0][:], XS[3])
+        feedback(0, 1, 1)
+        feedback(1, 0, 1)
+        close_tiles(0, 1, range(PACK))
+        h_mx[1, 0] = quantize("h10", h10_grouped)
+        feedback(1, 1, 1)
+        close_tiles(1, 1, range(2))
+        for b in range(BLOCKS):
+            w2_mx[b, 0] = quantize("w2_%d0" % b, cast_w2(b, 0, (GROUPED[1], PAGE3 - KIB)[b]), COLS)
+        w2a_high = cast_w2(0, 1, rows_at[1, 0])
+        close_tiles(1, 1, range(2, PACK))
+        for u in (2, 3):
+            pages.append(placed([P, T2], F32, "page%d" % u, (PAGE2, PAGE3)[u - 2]))
+            nc.gpsimd.memset(pages[u][:], 0.0)
+        second_stage(0, 0, GROUPED[2])
+        w2b_high = cast_w2(1, 1, SLOT[4] + 4 * KIB)
+        w2_mx[0, 1] = quantize("w2_01", w2a_high, COLS)
+        w2_mx[1, 1] = quantize("w2_11", w2b_high, COLS)
+        second_stage(0, 1, BASE)
+        h_mx[0, 1] = quantize("h01", interleave("h01", h_rows[0, 1][:], SLOT[4] + 6 * KIB))
+        second_stage(0, 2, XS[2])
+        h_mx[1, 1] = quantize("h11", interleave("h11", h_rows[1, 1][:], XS[5]))
+        second_stage(0, 3, rows_at[1, 1])
+        for u in range(NT):
+            second_stage(1, u, ROWS[0] + u * 2 * KIB)

@@ -112,6 +112,8 @@ def tile_list_handover_gradient_kernel(
         nc.gpsimd.memset(tab_s[32:64, :].bitcast(I32), 0)
         nc.gpsimd.memset(tab_s[64:P, :].bitcast(I32), 0)
         nc.gpsimd.memset(pages[0][:], 0.0)
+        last_page = placed([P, T2], F32, "page2")
+        nc.gpsimd.memset(last_page[:], 0.0)
 
         nc.sync.dma_start(idx[:], offs)
         nc.sync.dma_start(
@@ -141,6 +143,8 @@ def tile_list_handover_gradient_kernel(
             nc.sync.dma_start(out=v_s[r:P:32, :].bitcast(I32), in_=v_s_raw[2 * r : 32 : 8, :].bitcast(I32))
         pages.append(placed([P, T2], F32, "page1", PAGE1))
         nc.gpsimd.memset(pages[1][:], 0.0)
+        pages.append(last_page)
+        pages.append(pages[0])
 
         x_at = [XS[0], XS[1], XS[2], XS[3], XS[4], XS[5], XS[0], XS[2]]
         xs = {}
@@ -313,17 +317,15 @@ def tile_list_handover_gradient_kernel(
             w2_mx[b, 0] = quantize("w2_%d0" % b, cast_w2(b, 0, (GROUPED[1], PAGE3 - KIB)[b]), COLS)
         w2a_high = cast_w2(0, 1, rows_at[1, 0])
         close_tiles(1, 1, range(2, PACK))
-        for u in (2, 3):
-            pages.append(placed([P, T2], F32, "page%d" % u, (PAGE2, PAGE3)[u - 2]))
-            nc.gpsimd.memset(pages[u][:], 0.0)
         second_stage(0, 0, GROUPED[2])
         w2b_high = cast_w2(1, 1, SLOT[4] + 4 * KIB)
         w2_mx[0, 1] = quantize("w2_01", w2a_high, COLS)
         w2_mx[1, 1] = quantize("w2_11", w2b_high, COLS)
         second_stage(0, 1, BASE)
         h_mx[0, 1] = quantize("h01", interleave("h01", h_rows[0, 1][:], SLOT[4] + 6 * KIB))
-        second_stage(0, 2, XS[2])
         h_mx[1, 1] = quantize("h11", interleave("h11", h_rows[1, 1][:], XS[5]))
-        second_stage(0, 3, rows_at[1, 1])
-        for u in range(NT):
+        second_stage(0, 2, rows_at[1, 1])
+        for u in range(NT - 1):
             second_stage(1, u, ROWS[0] + u * 2 * KIB)
+        second_stage(0, NT - 1, XS[2])
+        second_stage(1, NT - 1, XS[2] + 2 * KIB)

@@ -38,7 +38,7 @@ XS = [BASE + (68 + 4 * g) * KIB for g in range(6)]
 PAGE1 = BASE + 92 * KIB
 PAGE2 = BASE + 100 * KIB
 PAGE3 = BASE + 108 * KIB
-SCALAR_PLANES = 4
+SCALAR_PLANES = 3
 
 
 def tile_list_handover_gradient_kernel(
@@ -75,8 +75,8 @@ def tile_list_handover_gradient_kernel(
         def interleave_w1(name, raw, at=None):
             grouped = placed([P, HALF * PACK], BF16, name + "_g", at)
             nc.scalar.copy(
-                out=grouped[:].rearrange("p (t m j) -> p m t j", t=PACK, j=PACK),
-                in_=raw[:].rearrange("p j (m t) -> p m t j", t=PACK),
+                out=grouped[:].rearrange("p (t m j) -> p m j t", t=PACK, j=PACK),
+                in_=raw[:].rearrange("p j (m t) -> p m j t", t=PACK),
             )
             return grouped
 
@@ -173,10 +173,11 @@ def tile_list_handover_gradient_kernel(
             for half in range(width // HALF):
                 slope[k, first + half] = tile[:, half * HALF : (half + 1) * HALF]
 
-        def vector_slope(k, at):
-            tile = placed([P, S], F32, "slope%d" % k, at)
-            nc.vector.scalar_tensor_tensor(out=tile[:], in0=xs[k][:], scalar=1.0, in1=xs[k][:], op0=SUB, op1=MULT)
-            for half in range(HALVES):
+        def vector_slope(k, width, at):
+            x = xs[k][:, 0:width]
+            tile = placed([P, width], F32, "slope%d" % k, at)
+            nc.vector.scalar_tensor_tensor(out=tile[:], in0=x, scalar=1.0, in1=x, op0=SUB, op1=MULT)
+            for half in range(width // HALF):
                 slope[k, half] = tile[:, half * HALF : (half + 1) * HALF]
 
         for k in range(PLANES):
@@ -187,8 +188,8 @@ def tile_list_handover_gradient_kernel(
             nc.vector.tensor_copy(xs[k][:], planes[k][:].indirect(idx[:]))
             if t == 0:
                 c_rows[b] = placed([P, HALVES, PACK, HALF], BF16, "c_rows%d" % b, ROWS[b])
-            if k < PLANES - 2:
-                pool_slope(k, 0, S if k < PLANES - 3 else HALF)
+            if k < PLANES - 3:
+                pool_slope(k, 0, S)
             if k < PLANES - 1:
                 price_rows(k, [0, 1])
             if k == PACK - 1:
@@ -197,7 +198,7 @@ def tile_list_handover_gradient_kernel(
 
         c_mx = {}
         c_mx[0, 0] = quantize("c00", c_grouped[0, 0], at=SLOT[2])
-        pool_slope(PLANES - 3, 1, HALF, GROUPED[0])
+        pool_slope(PLANES - 3, 0, HALF, GROUPED[0])
 
         wf_raw1 = load_wf(1, XS[1])
         tab_w = placed([P, T], I32, "tab_w", SLOT[3])
@@ -220,16 +221,17 @@ def tile_list_handover_gradient_kernel(
 
         after = SLOT[3]
         wf_w.append(deal_wf(1, wf_raw1, after + 4 * KIB))
-        c_mx[1, 0] = quantize("c10", c_grouped[1, 0], at=after)
         c_mx[0, 1] = quantize("c01", c_grouped[0, 1], at=after + HALF)
-        vector_slope(PLANES - 2, GROUPED[2])
+        c_mx[1, 0] = quantize("c10", c_grouped[1, 0], at=after)
+        vector_slope(PLANES - 2, S, GROUPED[1])
         w1_mx = [quantize("w1a", w1_grouped[0])]
-        vector_slope(PLANES - 1, SLOT[4] + 4 * KIB)
+        vector_slope(PLANES - 1, HALF, SLOT[4])
+        w1_mx.append(quantize("w1b", w1_grouped[1]))
 
         h_rows = {}
         h_mx = {}
         w2_mx = {}
-        rows_at = {(0, 0): ROWS[0], (1, 0): ROWS[0] + 4 * KIB, (0, 1): ROWS[1], (1, 1): ROWS[1] + 4 * KIB}
+        rows_at = {(0, 0): SLOT[0] + 4 * KIB, (1, 0): ROWS[0], (0, 1): SLOT[0] + 4 * KIB, (1, 1): ROWS[0]}
 
         def feedback_pass(d, a, k, half):
             nc.tensor.matmul_mx(
@@ -276,6 +278,18 @@ def tile_list_handover_gradient_kernel(
         def cast_w2(b, part, at):
             return interleave("w2_%d%d" % (b, part), w2_raw[b][:, :, part * COLS : (part + 1) * COLS], at, COLS)
 
+        def pool_cast_w2(b, part, at):
+            grouped = placed([P, COLS * PACK], BF16, "w2_%d%d_g" % (b, part), at)
+            nc.gpsimd.tensor_scalar(
+                grouped[:].rearrange("p (c i t) -> p c t i", i=4, t=PACK),
+                w2_raw[b][:, :, part * COLS : (part + 1) * COLS].rearrange("p t (c i) -> p c t i", i=4),
+                1.0,
+                0.0,
+                MULT,
+                ADD,
+            )
+            return grouped
+
         def second_stage(half, u, at):
             users = slice(half * HALF, (half + 1) * HALF)
             slots = idx2[:, half * HALF // 16 : (half + 1) * HALF // 16]
@@ -300,32 +314,33 @@ def tile_list_handover_gradient_kernel(
         for a in range(BLOCKS):
             for b in range(BLOCKS):
                 feedback(a, b, 0)
+        pool_slope(PLANES - 3, 1, HALF, PAGE3 + 4 * KIB)
+        w2_low = [pool_cast_w2(0, 0, PAGE3 + 6 * KIB), cast_w2(1, 0, PAGE3)]
         close_tiles(0, 0, range(PACK))
-        w1_mx.append(quantize("w1b", w1_grouped[1]))
+        h00_grouped = interleave("h00", h_rows[0, 0][:], XS[0])
         feedback(0, 0, 1)
         close_tiles(1, 0, range(PACK))
-        c_mx[1, 1] = quantize("c11", c_grouped[1, 1])
-        h_mx[0, 0] = quantize("h00", interleave("h00", h_rows[0, 0][:], XS[0]))
         h10_grouped = interleave("h10", h_rows[1, 0][:], XS[3])
+        c_mx[1, 1] = quantize("c11", c_grouped[1, 1])
+        for b in range(BLOCKS):
+            w2_mx[b, 0] = quantize("w2_%d0" % b, w2_low[b], COLS)
+        h_mx[0, 0] = quantize("h00", h00_grouped)
+        pool_slope(PLANES - 1, 1, HALF, XS[0])
         feedback(0, 1, 1)
         feedback(1, 0, 1)
         close_tiles(0, 1, range(PACK))
         h_mx[1, 0] = quantize("h10", h10_grouped)
+        w2_high = [cast_w2(b, 1, SLOT[0] + b * 2 * KIB) for b in range(BLOCKS)]
         feedback(1, 1, 1)
-        close_tiles(1, 1, range(2))
+        close_tiles(1, 1, range(PACK))
         for b in range(BLOCKS):
-            w2_mx[b, 0] = quantize("w2_%d0" % b, cast_w2(b, 0, (GROUPED[1], PAGE3 - KIB)[b]), COLS)
-        w2a_high = cast_w2(0, 1, rows_at[1, 0])
-        close_tiles(1, 1, range(2, PACK))
-        second_stage(0, 0, GROUPED[2])
-        w2b_high = cast_w2(1, 1, SLOT[4] + 4 * KIB)
-        w2_mx[0, 1] = quantize("w2_01", w2a_high, COLS)
-        w2_mx[1, 1] = quantize("w2_11", w2b_high, COLS)
-        second_stage(0, 1, BASE)
-        h_mx[0, 1] = quantize("h01", interleave("h01", h_rows[0, 1][:], SLOT[4] + 6 * KIB))
-        h_mx[1, 1] = quantize("h11", interleave("h11", h_rows[1, 1][:], XS[5]))
+            w2_mx[b, 1] = quantize("w2_%d1" % b, w2_high[b], COLS)
+        second_stage(0, 0, GROUPED[1])
+        second_stage(0, 1, GROUPED[1] + 2 * KIB)
+        h_mx[0, 1] = quantize("h01", interleave("h01", h_rows[0, 1][:], XS[0]))
+        h_mx[1, 1] = quantize("h11", interleave("h11", h_rows[1, 1][:], ROWS[1]))
         second_stage(0, 2, rows_at[1, 1])
         for u in range(NT - 1):
-            second_stage(1, u, ROWS[0] + u * 2 * KIB)
-        second_stage(0, NT - 1, XS[2])
-        second_stage(1, NT - 1, XS[2] + 2 * KIB)
+            second_stage(1, u, SLOT[4] + (u + 1) * 2 * KIB)
+        second_stage(0, NT - 1, PAGE2)
+        second_stage(1, NT - 1, PAGE2 + 2 * KIB)

@@ -105,48 +105,45 @@ def tile_list_handover_gradient_kernel(
             nc.sync.dma_start(out=plane[:], in_=s_rows[k // PACK, k % PACK])
             return plane
 
-        wf_s_raw = placed([P, H], U8, "wf_s_raw", PAGE1)
-        tab_s = placed([P, T], U8, "tab_s", PRICE_AT)
-        pages = [placed([P, T2], F32, "page0")]
-        nc.gpsimd.memset(wf_s_raw[:].bitcast(I32), 0)
-        nc.gpsimd.memset(tab_s[32:64, :].bitcast(I32), 0)
-        nc.gpsimd.memset(tab_s[64:P, :].bitcast(I32), 0)
-        nc.gpsimd.memset(pages[0][:], 0.0)
-        last_page = placed([P, T2], F32, "page2")
-        nc.gpsimd.memset(last_page[:], 0.0)
+        wf_s_raw = placed([P, H + 4], U8, "wf_s_raw", PAGE1)
+        tab_s = placed([P, T + 4], U8, "tab_s", PRICE_AT)
+        pages = [placed([P, T2], F32, "page%d" % u) for u in range(2)]
+        nc.vector.memset(wf_s_raw[:].bitcast(I32), 0)
+        nc.vector.memset(tab_s[32:64, :].bitcast(I32), 0)
+        nc.vector.memset(tab_s[64:P, :].bitcast(I32), 0)
+        for page in pages:
+            nc.gpsimd.memset(page[:], 0.0)
 
         nc.sync.dma_start(idx[:], offs)
         nc.sync.dma_start(
-            out=tab_s[0:32, :].bitcast(I32),
+            out=tab_s[0:32, 0:T].bitcast(I32),
             in_=tab_scales[0].bitcast(I32).unsqueeze(1).to_broadcast([16, 2, T // 4]),
         )
         wf_raw0 = load_wf(0, SLOT[4] - 2 * KIB)
         planes = [load_plane(0), load_plane(1)]
         for q in range(4):
             nc.scalar.dma_start(
-                out=wf_s_raw[32 * q : 32 * q + 4 * BLOCKS, :].bitcast(I32),
+                out=wf_s_raw[32 * q : 32 * q + 4 * BLOCKS, 0:H].bitcast(I32),
                 in_=wf_scales.bitcast(I32)[:, 4 * q : 4 * q + 4, :],
             )
 
         v_s_raw = placed([P, S], U8, "v_s_raw")
-        nc.vector.tensor_copy(v_s_raw[:], tab_s[:].indirect(idx[:]))
+        nc.vector.tensor_copy(v_s_raw[:], tab_s[:, 0:T].indirect(idx[:]))
         wf_w = [deal_wf(0, wf_raw0)]
         wf_s = placed([P, H], U8, "wf_s")
         nc.vector.tensor_copy(
             out=wf_s[:].rearrange("p (b t m) -> p b t m", t=PACK, m=P),
-            in_=wf_s_raw[:].rearrange("p (b m t) -> p b t m", t=PACK, m=P),
+            in_=wf_s_raw[:, 0:H].rearrange("p (b m t) -> p b t m", t=PACK, m=P),
         )
         price_sb = placed([P, BLOCKS, PACK], F32, "price_sb", PRICE_AT)
         nc.sync.dma_start(out=price_sb[:], in_=price.rearrange("(b p t) -> p b t", p=P, t=PACK))
         v_s = placed([P, S], U8, "v_s")
         for r in range(4):
             nc.sync.dma_start(out=v_s[r:P:32, :].bitcast(I32), in_=v_s_raw[2 * r : 32 : 8, :].bitcast(I32))
-        pages.append(placed([P, T2], F32, "page1", PAGE1))
-        nc.gpsimd.memset(pages[1][:], 0.0)
-        pages.append(last_page)
-        pages.append(pages[0])
+        pages.append(placed([P, T2], F32, "page2", PAGE1))
+        nc.gpsimd.memset(pages[2][:], 0.0)
 
-        x_at = [XS[0], XS[1], XS[2], XS[3], XS[4], XS[5], XS[0], XS[2]]
+        x_at = [XS[0], XS[1], XS[2], XS[3], XS[4], XS[5], XS[0], XS[1]]
         xs = {}
         slope = {}
         c_rows = {}
@@ -200,7 +197,7 @@ def tile_list_handover_gradient_kernel(
         c_mx[0, 0] = quantize("c00", c_grouped[0, 0], at=SLOT[2])
         pool_slope(PLANES - 3, 0, HALF, GROUPED[0])
 
-        wf_raw1 = load_wf(1, XS[1])
+        wf_raw1 = load_wf(1, XS[2])
         tab_w = placed([P, T], I32, "tab_w", SLOT[3])
         nc.sync.dma_start(out=tab_w[:], in_=tab_words[0].rearrange("p n t -> p (n t)").bitcast(I32))
         w1_raw = [load_raw("w1_raw0", w1[:, 0:PASS], SLOT[4]), load_raw("w1_raw1", w1[:, PASS:H], SLOT[0])]
@@ -215,7 +212,7 @@ def tile_list_handover_gradient_kernel(
         price_rows(PLANES - 1, [0])
         c_grouped[1, 0] = interleave("c10", c_rows[1][:, 0, :, :], GROUPED[2])
         w1_grouped = [interleave_w1("w1a", w1_raw[0], PAGE2)]
-        w1_grouped.append(interleave_w1("w1b", w1_raw[1], PAGE3 + 4 * KIB))
+        w1_grouped.append(interleave_w1("w1b", w1_raw[1], PAGE3 + 7 * KIB))
         price_rows(PLANES - 1, [1])
         c_grouped[1, 1] = interleave("c11", c_rows[1][:, 1, :, :], SLOT[0])
 
@@ -278,18 +275,6 @@ def tile_list_handover_gradient_kernel(
         def cast_w2(b, part, at):
             return interleave("w2_%d%d" % (b, part), w2_raw[b][:, :, part * COLS : (part + 1) * COLS], at, COLS)
 
-        def pool_cast_w2(b, part, at):
-            grouped = placed([P, COLS * PACK], BF16, "w2_%d%d_g" % (b, part), at)
-            nc.gpsimd.tensor_scalar(
-                grouped[:].rearrange("p (c i t) -> p c t i", i=4, t=PACK),
-                w2_raw[b][:, :, part * COLS : (part + 1) * COLS].rearrange("p t (c i) -> p c t i", i=4),
-                1.0,
-                0.0,
-                MULT,
-                ADD,
-            )
-            return grouped
-
         def second_stage(half, u, at):
             users = slice(half * HALF, (half + 1) * HALF)
             slots = idx2[:, half * HALF // 16 : (half + 1) * HALF // 16]
@@ -314,22 +299,24 @@ def tile_list_handover_gradient_kernel(
         for a in range(BLOCKS):
             for b in range(BLOCKS):
                 feedback(a, b, 0)
-        pool_slope(PLANES - 3, 1, HALF, PAGE3 + 4 * KIB)
-        w2_low = [pool_cast_w2(0, 0, PAGE3 + 6 * KIB), cast_w2(1, 0, PAGE3)]
+        pool_slope(PLANES - 3, 1, HALF, PAGE3 + 8 * KIB)
+        pages.append(placed([P, T2], F32, "page3", PAGE3))
+        nc.gpsimd.memset(pages[3][:], 0.0)
+        w2_low = cast_w2(0, 0, PAGE3 + 12 * KIB)
         close_tiles(0, 0, range(PACK))
         h00_grouped = interleave("h00", h_rows[0, 0][:], XS[0])
         feedback(0, 0, 1)
         close_tiles(1, 0, range(PACK))
         h10_grouped = interleave("h10", h_rows[1, 0][:], XS[3])
         c_mx[1, 1] = quantize("c11", c_grouped[1, 1])
-        for b in range(BLOCKS):
-            w2_mx[b, 0] = quantize("w2_%d0" % b, w2_low[b], COLS)
+        w2_mx[0, 0] = quantize("w2_00", w2_low, COLS)
         h_mx[0, 0] = quantize("h00", h00_grouped)
         pool_slope(PLANES - 1, 1, HALF, XS[0])
         feedback(0, 1, 1)
         feedback(1, 0, 1)
         close_tiles(0, 1, range(PACK))
         h_mx[1, 0] = quantize("h10", h10_grouped)
+        w2_mx[1, 0] = quantize("w2_10", cast_w2(1, 0, PAGE3 + 12 * KIB), COLS)
         w2_high = [cast_w2(b, 1, SLOT[0] + b * 2 * KIB) for b in range(BLOCKS)]
         feedback(1, 1, 1)
         close_tiles(1, 1, range(PACK))
@@ -340,7 +327,6 @@ def tile_list_handover_gradient_kernel(
         h_mx[0, 1] = quantize("h01", interleave("h01", h_rows[0, 1][:], XS[0]))
         h_mx[1, 1] = quantize("h11", interleave("h11", h_rows[1, 1][:], ROWS[1]))
         second_stage(0, 2, rows_at[1, 1])
-        for u in range(NT - 1):
-            second_stage(1, u, SLOT[4] + (u + 1) * 2 * KIB)
-        second_stage(0, NT - 1, PAGE2)
-        second_stage(1, NT - 1, PAGE2 + 2 * KIB)
+        second_stage(0, 3, rows_at[1, 1] + 2 * KIB)
+        for u in range(NT):
+            second_stage(1, u, SLOT[3] + KIB + u * 2 * KIB if u == 0 else SLOT[4] + u * 2 * KIB)

@@ -29,15 +29,16 @@ NT = N // P
 COLS = N // 2
 
 KIB = 1024
-PRICE_AT = 0
-BASE = KIB
-SLOT = [BASE + 8 * KIB, BASE + 16 * KIB, 64, BASE + 24 * KIB, BASE + 32 * KIB]
-ROWS = [BASE + 40 * KIB, BASE + 48 * KIB]
-GROUPED = [BASE + (56 + 4 * g) * KIB for g in range(3)]
-XS = [BASE + (68 + 4 * g) * KIB for g in range(6)]
-PAGE1 = BASE + 92 * KIB
-PAGE2 = BASE + 100 * KIB
-PAGE3 = BASE + 108 * KIB
+BASE = 3 * KIB
+SLOT = [BASE + 8 * KIB, BASE + 16 * KIB, 0, BASE + 24 * KIB, BASE + 36 * KIB]
+LAST_PLANE = KIB
+TABLE = SLOT[3] + 4 * KIB
+ROWS = [BASE + 44 * KIB, BASE + 52 * KIB]
+GROUPED = [BASE + (60 + 4 * g) * KIB for g in range(3)]
+XS = [BASE + (72 + 4 * g) * KIB for g in range(PLANES)]
+PAGE1 = BASE + 104 * KIB
+PAGE2 = BASE + 112 * KIB
+PAGE3 = BASE + 116 * KIB
 SCALAR_PLANES = 3
 
 
@@ -101,14 +102,12 @@ def tile_list_handover_gradient_kernel(
         s_rows = sT.rearrange("(b p t) n -> b t p n", p=P, t=PACK)
 
         def load_plane(k):
-            plane = placed([P, T], F32, "plane%d" % k, SLOT[k % 5])
+            plane = placed([P, T], F32, "plane%d" % k, LAST_PLANE if k == PLANES - 1 else SLOT[k % 5])
             nc.sync.dma_start(out=plane[:], in_=s_rows[k // PACK, k % PACK])
             return plane
 
-        wf_s_raw = placed([P, H + 4], U8, "wf_s_raw", PAGE1)
-        tab_s = placed([P, T + 4], U8, "tab_s", PRICE_AT)
+        tab_s = placed([P, T + 4], U8, "tab_s")
         pages = [placed([P, T2], F32, "page%d" % u) for u in range(2)]
-        nc.vector.memset(wf_s_raw[:].bitcast(I32), 0)
         nc.vector.memset(tab_s[32:64, :].bitcast(I32), 0)
         nc.vector.memset(tab_s[64:P, :].bitcast(I32), 0)
         for page in pages:
@@ -119,31 +118,17 @@ def tile_list_handover_gradient_kernel(
             out=tab_s[0:32, 0:T].bitcast(I32),
             in_=tab_scales[0].bitcast(I32).unsqueeze(1).to_broadcast([16, 2, T // 4]),
         )
-        wf_raw0 = load_wf(0, SLOT[4] - 2 * KIB)
-        planes = [load_plane(0), load_plane(1)]
-        for q in range(4):
-            nc.scalar.dma_start(
-                out=wf_s_raw[32 * q : 32 * q + 4 * BLOCKS, 0:H].bitcast(I32),
-                in_=wf_scales.bitcast(I32)[:, 4 * q : 4 * q + 4, :],
-            )
+        wf_raw0 = load_wf(0, PAGE1)
+        price_sb = placed([P, BLOCKS, PACK], F32, "price_sb")
+        nc.scalar.dma_start(out=price_sb[:], in_=price.rearrange("(b p t) -> p b t", p=P, t=PACK))
 
         v_s_raw = placed([P, S], U8, "v_s_raw")
         nc.vector.tensor_copy(v_s_raw[:], tab_s[:, 0:T].indirect(idx[:]))
         wf_w = [deal_wf(0, wf_raw0)]
-        wf_s = placed([P, H], U8, "wf_s")
-        nc.vector.tensor_copy(
-            out=wf_s[:].rearrange("p (b t m) -> p b t m", t=PACK, m=P),
-            in_=wf_s_raw[:, 0:H].rearrange("p (b m t) -> p b t m", t=PACK, m=P),
-        )
-        price_sb = placed([P, BLOCKS, PACK], F32, "price_sb", PRICE_AT)
-        nc.sync.dma_start(out=price_sb[:], in_=price.rearrange("(b p t) -> p b t", p=P, t=PACK))
-        v_s = placed([P, S], U8, "v_s")
-        for r in range(4):
-            nc.sync.dma_start(out=v_s[r:P:32, :].bitcast(I32), in_=v_s_raw[2 * r : 32 : 8, :].bitcast(I32))
         pages.append(placed([P, T2], F32, "page2", PAGE1))
         nc.gpsimd.memset(pages[2][:], 0.0)
 
-        x_at = [XS[0], XS[1], XS[2], XS[3], XS[4], XS[5], XS[0], XS[1]]
+        planes = []
         xs = {}
         slope = {}
         c_rows = {}
@@ -179,9 +164,8 @@ def tile_list_handover_gradient_kernel(
 
         for k in range(PLANES):
             b, t = divmod(k, PACK)
-            if k >= 2:
-                planes.append(load_plane(k))
-            xs[k] = placed([P, S], F32, "x%d" % k, x_at[k])
+            planes.append(load_plane(k))
+            xs[k] = placed([P, S], F32, "x%d" % k, XS[k])
             nc.vector.tensor_copy(xs[k][:], planes[k][:].indirect(idx[:]))
             if t == 0:
                 c_rows[b] = placed([P, HALVES, PACK, HALF], BF16, "c_rows%d" % b, ROWS[b])
@@ -189,21 +173,35 @@ def tile_list_handover_gradient_kernel(
                 pool_slope(k, 0, S)
             if k < PLANES - 1:
                 price_rows(k, [0, 1])
+            if k == 2:
+                wf_s_raw = placed([P, H], U8, "wf_s_raw", SLOT[2])
+                nc.gpsimd.memset(wf_s_raw[:].bitcast(I32), 0)
             if k == PACK - 1:
                 for half in range(HALVES):
                     c_grouped[0, half] = interleave("c0%d" % half, c_rows[0][:, half, :, :], GROUPED[half])
 
+        for q in range(4):
+            nc.sync.dma_start(
+                out=wf_s_raw[32 * q : 32 * q + 4 * BLOCKS, :].bitcast(I32),
+                in_=wf_scales.bitcast(I32)[:, 4 * q : 4 * q + 4, :],
+            )
+        v_s = placed([P, S], U8, "v_s")
+        for r in range(4):
+            nc.sync.dma_start(out=v_s[r:P:32, :].bitcast(I32), in_=v_s_raw[2 * r : 32 : 8, :].bitcast(I32))
+        wf_s = placed([P, H], U8, "wf_s", LAST_PLANE + HALF)
+        nc.vector.tensor_copy(
+            out=wf_s[:].rearrange("p (b t m) -> p b t m", t=PACK, m=P),
+            in_=wf_s_raw[:].rearrange("p (b m t) -> p b t m", t=PACK, m=P),
+        )
         c_mx = {}
-        c_mx[0, 0] = quantize("c00", c_grouped[0, 0], at=SLOT[2])
+        c_mx[0, 0] = quantize("c00", c_grouped[0, 0], at=LAST_PLANE)
         pool_slope(PLANES - 3, 0, HALF, GROUPED[0])
 
-        wf_raw1 = load_wf(1, XS[2])
-        tab_w = placed([P, T], I32, "tab_w", SLOT[3])
+        tab_w = placed([P, T], I32, "tab_w", TABLE)
         nc.sync.dma_start(out=tab_w[:], in_=tab_words[0].rearrange("p n t -> p (n t)").bitcast(I32))
+        wf_raw1 = load_wf(1, SLOT[3])
         w1_raw = [load_raw("w1_raw0", w1[:, 0:PASS], SLOT[4]), load_raw("w1_raw1", w1[:, PASS:H], SLOT[0])]
         w2_raw = [load_raw("w2_raw0", w2[0:PASS, :], SLOT[1]), load_raw("w2_raw1", w2[PASS:H, :], BASE)]
-        wgo_sb = placed([P, S], F32, "wgo_sb", XS[4])
-        nc.sync.dma_start(out=wgo_sb[:], in_=wgo)
         nc.sync.dma_start(idx2[:], offs2)
 
         v_w = placed([P, S], U32, "v_w")
@@ -216,12 +214,14 @@ def tile_list_handover_gradient_kernel(
         price_rows(PLANES - 1, [1])
         c_grouped[1, 1] = interleave("c11", c_rows[1][:, 1, :, :], SLOT[0])
 
-        after = SLOT[3]
+        after = TABLE
         wf_w.append(deal_wf(1, wf_raw1, after + 4 * KIB))
         c_mx[0, 1] = quantize("c01", c_grouped[0, 1], at=after + HALF)
         c_mx[1, 0] = quantize("c10", c_grouped[1, 0], at=after)
         vector_slope(PLANES - 2, S, GROUPED[1])
         w1_mx = [quantize("w1a", w1_grouped[0])]
+        wgo_sb = placed([P, S], F32, "wgo_sb", PAGE2)
+        nc.sync.dma_start(out=wgo_sb[:], in_=wgo)
         vector_slope(PLANES - 1, HALF, SLOT[4])
         w1_mx.append(quantize("w1b", w1_grouped[1]))
 
@@ -329,4 +329,4 @@ def tile_list_handover_gradient_kernel(
         second_stage(0, 2, rows_at[1, 1])
         second_stage(0, 3, rows_at[1, 1] + 2 * KIB)
         for u in range(NT):
-            second_stage(1, u, SLOT[3] + KIB + u * 2 * KIB if u == 0 else SLOT[4] + u * 2 * KIB)
+            second_stage(1, u, SLOT[1] + u * 2 * KIB)

@@ -39,6 +39,7 @@ XS = [BASE + (72 + 4 * g) * KIB for g in range(PLANES)]
 PAGE1 = BASE + 104 * KIB
 PAGE2 = BASE + 112 * KIB
 PAGE3 = BASE + 116 * KIB
+SPARE = BASE + 124 * KIB
 SCALAR_PLANES = 3
 
 
@@ -134,18 +135,23 @@ def tile_list_handover_gradient_kernel(
         c_rows = {}
         c_grouped = {}
 
+        def x_of(k, first, width):
+            if k == PLANES - 1:
+                return xs[k, first][:]
+            return xs[k][:, first * HALF : first * HALF + width]
+
         def price_rows(k, halves):
             b, t = divmod(k, PACK)
             lo, hi = halves[0], halves[-1] + 1
             nc.scalar.activation(
                 out=c_rows[b][:, lo:hi, t, :],
-                in_=xs[k][:, lo * HALF : hi * HALF].rearrange("p (h j) -> p h j", j=HALF),
+                in_=x_of(k, lo, (hi - lo) * HALF).rearrange("p (h j) -> p h j", j=HALF),
                 func=COPY,
                 scale=price_sb[:, b, t : t + 1],
             )
 
         def pool_slope(k, first, width, at=None):
-            x = xs[k][:, first * HALF : first * HALF + width]
+            x = x_of(k, first, width)
             tile = placed([P, width], F32, "slope%d_%d" % (k, first), at)
             if k < SCALAR_PLANES:
                 nc.scalar.activation(out=tile[:], in_=x, func=COPY, bias=-1.0)
@@ -156,7 +162,7 @@ def tile_list_handover_gradient_kernel(
                 slope[k, first + half] = tile[:, half * HALF : (half + 1) * HALF]
 
         def vector_slope(k, width, at):
-            x = xs[k][:, 0:width]
+            x = x_of(k, 0, width)
             tile = placed([P, width], F32, "slope%d" % k, at)
             nc.vector.scalar_tensor_tensor(out=tile[:], in0=x, scalar=1.0, in1=x, op0=SUB, op1=MULT)
             for half in range(width // HALF):
@@ -165,11 +171,20 @@ def tile_list_handover_gradient_kernel(
         for k in range(PLANES):
             b, t = divmod(k, PACK)
             planes.append(load_plane(k))
-            xs[k] = placed([P, S], F32, "x%d" % k, XS[k])
-            nc.vector.tensor_copy(xs[k][:], planes[k][:].indirect(idx[:]))
+            if k < PLANES - 1:
+                xs[k] = placed([P, S], F32, "x%d" % k, XS[k])
+                nc.vector.tensor_copy(xs[k][:], planes[k][:].indirect(idx[:]))
+            else:
+                for half in range(HALVES):
+                    xs[k, half] = placed([P, HALF], F32, "x%d_%d" % (k, half), XS[k] + half * 2 * KIB)
+                    picks = idx[:, half * HALF // 16 : (half + 1) * HALF // 16]
+                    nc.vector.tensor_copy(xs[k, half][:], planes[k][:].indirect(picks))
             if t == 0:
                 c_rows[b] = placed([P, HALVES, PACK, HALF], BF16, "c_rows%d" % b, ROWS[b])
-            if k < PLANES - 3:
+            if k == 1:
+                pool_slope(k, 0, HALF, SPARE)
+                pool_slope(k, 1, HALF)
+            elif k < PLANES - 3:
                 pool_slope(k, 0, S)
             if k < PLANES - 1:
                 price_rows(k, [0, 1])
@@ -178,7 +193,7 @@ def tile_list_handover_gradient_kernel(
                 nc.gpsimd.memset(wf_s_raw[:].bitcast(I32), 0)
             if k == PACK - 1:
                 for half in range(HALVES):
-                    c_grouped[0, half] = interleave("c0%d" % half, c_rows[0][:, half, :, :], GROUPED[half])
+                    c_grouped[0, half] = interleave("c0%d" % half, c_rows[0][:, half, :, :], (PAGE3, GROUPED[1])[half])
 
         for q in range(4):
             nc.sync.dma_start(
@@ -195,7 +210,8 @@ def tile_list_handover_gradient_kernel(
         )
         c_mx = {}
         c_mx[0, 0] = quantize("c00", c_grouped[0, 0], at=LAST_PLANE)
-        pool_slope(PLANES - 3, 0, HALF, GROUPED[0])
+        pages.append(placed([P, T2], F32, "page3", PAGE3))
+        nc.gpsimd.memset(pages[3][:], 0.0)
 
         tab_w = placed([P, T], I32, "tab_w", TABLE)
         nc.sync.dma_start(out=tab_w[:], in_=tab_words[0].rearrange("p n t -> p (n t)").bitcast(I32))
@@ -210,7 +226,7 @@ def tile_list_handover_gradient_kernel(
         price_rows(PLANES - 1, [0])
         c_grouped[1, 0] = interleave("c10", c_rows[1][:, 0, :, :], GROUPED[2])
         w1_grouped = [interleave_w1("w1a", w1_raw[0], PAGE2)]
-        w1_grouped.append(interleave_w1("w1b", w1_raw[1], PAGE3 + 7 * KIB))
+        w1_grouped.append(interleave_w1("w1b", w1_raw[1], GROUPED[0]))
         price_rows(PLANES - 1, [1])
         c_grouped[1, 1] = interleave("c11", c_rows[1][:, 1, :, :], SLOT[0])
 
@@ -223,12 +239,12 @@ def tile_list_handover_gradient_kernel(
         wgo_sb = placed([P, S], F32, "wgo_sb", PAGE2)
         nc.sync.dma_start(out=wgo_sb[:], in_=wgo)
         vector_slope(PLANES - 1, HALF, SLOT[4])
-        w1_mx.append(quantize("w1b", w1_grouped[1]))
+        pool_slope(PLANES - 3, 0, HALF, XS[PLANES - 1])
 
         h_rows = {}
         h_mx = {}
         w2_mx = {}
-        rows_at = {(0, 0): SLOT[0] + 4 * KIB, (1, 0): ROWS[0], (0, 1): SLOT[0] + 4 * KIB, (1, 1): ROWS[0]}
+        rows_at = {(0, 0): ROWS[0] + 4 * KIB, (1, 0): ROWS[0], (0, 1): ROWS[0] + 4 * KIB, (1, 1): ROWS[0]}
 
         def feedback_pass(d, a, k, half):
             nc.tensor.matmul_mx(
@@ -259,7 +275,7 @@ def tile_list_handover_gradient_kernel(
         def feedback(a, b, half):
             if a == 0:
                 h_rows[b, half] = placed([P, PACK, HALF], BF16, "h_rows%d%d" % (b, half), rows_at[b, half])
-                banks[b, half] = [psum.tile([P, HALF], F32, name="acc", bufs=8) for t in range(PACK)]
+                banks[b, half] = [psum.tile([P, HALF], F32, name="acc%d" % b, bufs=PACK) for t in range(PACK)]
             for t in range(PACK):
                 feedback_pass(banks[b, half][t], a, b * PACK + t, half)
 
@@ -267,6 +283,8 @@ def tile_list_handover_gradient_kernel(
             for t in tiles:
                 k = b * PACK + t
                 d = banks[b, half][t]
+                if half == 1:
+                    feedback_pass(d, 1, k, half)
                 table_pass(d, k, half)
                 nc.vector.scalar_tensor_tensor(
                     out=h_rows[b, half][:, t, :], in0=slope[k, half], scalar=-1.0, in1=d[:], op0=MULT, op1=MULT
@@ -279,7 +297,7 @@ def tile_list_handover_gradient_kernel(
             users = slice(half * HALF, (half + 1) * HALF)
             slots = idx2[:, half * HALF // 16 : (half + 1) * HALF // 16]
             part, col = divmod(u * P, COLS)
-            y = psum.tile([P, HALF], F32, name="acc", bufs=8)
+            y = psum.tile([P, HALF], F32, name="acc%d" % (1 - half), bufs=PACK)
             for b in range(BLOCKS):
                 nc.tensor.matmul_mx(
                     out=y[:],
@@ -299,31 +317,30 @@ def tile_list_handover_gradient_kernel(
         for a in range(BLOCKS):
             for b in range(BLOCKS):
                 feedback(a, b, 0)
-        pool_slope(PLANES - 3, 1, HALF, PAGE3 + 8 * KIB)
-        pages.append(placed([P, T2], F32, "page3", PAGE3))
-        nc.gpsimd.memset(pages[3][:], 0.0)
-        w2_low = cast_w2(0, 0, PAGE3 + 12 * KIB)
-        close_tiles(0, 0, range(PACK))
+        close_tiles(0, 0, range(PACK - 1))
+        w1_mx.append(quantize("w1b", w1_grouped[1], at=SPARE))
+        pool_slope(PLANES - 3, 1, HALF, GROUPED[0])
+        close_tiles(0, 0, [PACK - 1])
         h00_grouped = interleave("h00", h_rows[0, 0][:], XS[0])
         feedback(0, 0, 1)
         close_tiles(1, 0, range(PACK))
         h10_grouped = interleave("h10", h_rows[1, 0][:], XS[3])
         c_mx[1, 1] = quantize("c11", c_grouped[1, 1])
-        w2_mx[0, 0] = quantize("w2_00", w2_low, COLS)
         h_mx[0, 0] = quantize("h00", h00_grouped)
         pool_slope(PLANES - 1, 1, HALF, XS[0])
         feedback(0, 1, 1)
-        feedback(1, 0, 1)
         close_tiles(0, 1, range(PACK))
         h_mx[1, 0] = quantize("h10", h10_grouped)
-        w2_mx[1, 0] = quantize("w2_10", cast_w2(1, 0, PAGE3 + 12 * KIB), COLS)
-        w2_high = [cast_w2(b, 1, SLOT[0] + b * 2 * KIB) for b in range(BLOCKS)]
-        feedback(1, 1, 1)
-        close_tiles(1, 1, range(PACK))
+        w2_low = [cast_w2(b, 0, SLOT[0] + b * 2 * KIB) for b in range(BLOCKS)]
+        w2_mx[0, 0] = quantize("w2_00", w2_low[0], COLS)
+        w2_high = [cast_w2(b, 1, XS[3] + b * 2 * KIB) for b in range(BLOCKS)]
+        close_tiles(1, 1, range(2))
+        w2_mx[1, 0] = quantize("w2_10", w2_low[1], COLS)
+        close_tiles(1, 1, range(2, PACK))
         for b in range(BLOCKS):
             w2_mx[b, 1] = quantize("w2_%d1" % b, w2_high[b], COLS)
-        second_stage(0, 0, GROUPED[1])
-        second_stage(0, 1, GROUPED[1] + 2 * KIB)
+        second_stage(0, 0, SLOT[4] + 4 * KIB)
+        second_stage(0, 1, SLOT[4] + 6 * KIB)
         h_mx[0, 1] = quantize("h01", interleave("h01", h_rows[0, 1][:], XS[0]))
         h_mx[1, 1] = quantize("h11", interleave("h11", h_rows[1, 1][:], ROWS[1]))
         second_stage(0, 2, rows_at[1, 1])

@@ -29,17 +29,18 @@ NT = N // P
 COLS = N // 2
 
 KIB = 1024
-BASE = 3 * KIB
-SLOT = [BASE + 8 * KIB, BASE + 16 * KIB, 0, BASE + 24 * KIB, BASE + 36 * KIB]
-LAST_PLANE = KIB
+BASE = 15 * KIB
+SLOT = [BASE + 8 * KIB, BASE + 16 * KIB, 4 * KIB, BASE + 24 * KIB, BASE + 36 * KIB]
+LAST_PLANE = 9 * KIB
+RESTART = SLOT[2] - HALF
 TABLE = SLOT[3] + 4 * KIB
-ROWS = [BASE + 44 * KIB, BASE + 52 * KIB]
-GROUPED = [BASE + (60 + 4 * g) * KIB for g in range(3)]
-XS = [BASE + (72 + 4 * g) * KIB for g in range(PLANES)]
-PAGE1 = BASE + 104 * KIB
-PAGE2 = BASE + 112 * KIB
-PAGE3 = BASE + 116 * KIB
-SPARE = BASE + 124 * KIB
+W1A = SLOT[4] + KIB
+SPARE = BASE + 117 * KIB
+ROWS = [BASE + 45 * KIB, BASE + 53 * KIB]
+GROUPED = [0, SPARE + 2 * KIB, BASE + 69 * KIB]
+XS = [BASE + (73 + 4 * g) * KIB for g in range(PLANES)]
+PAGE2 = BASE + 105 * KIB
+PAGE3 = BASE + 109 * KIB
 SCALAR_PLANES = 3
 
 
@@ -63,7 +64,7 @@ def tile_list_handover_gradient_kernel(
         def quantize(name, grouped, width=HALF, at=None):
             codes = placed([P, width], U32, name + "_w")
             scales = placed([P, width], U8, name + "_s", at)
-            nc.vector.quantize_mx(out=codes[:].bitcast(E4), scales=scales[:], in_=grouped[:])
+            nc.vector.quantize_mx(out=codes[:].bitcast(E4), scales=scales[:], in_=grouped)
             return codes, scales
 
         def interleave(name, rows, at=None, width=HALF):
@@ -72,7 +73,7 @@ def tile_list_handover_gradient_kernel(
                 out=grouped[:].rearrange("p (c i t) -> p c t i", i=4, t=PACK),
                 in_=rows.rearrange("p t (c i) -> p c t i", i=4),
             )
-            return grouped
+            return grouped[:]
 
         def interleave_w1(name, raw, at=None):
             grouped = placed([P, HALF * PACK], BF16, name + "_g", at)
@@ -80,7 +81,7 @@ def tile_list_handover_gradient_kernel(
                 out=grouped[:].rearrange("p (t m j) -> p m j t", t=PACK, j=PACK),
                 in_=raw[:].rearrange("p j (m t) -> p m j t", t=PACK),
             )
-            return grouped
+            return grouped[:]
 
         def load_raw(name, rows, at):
             raw = placed([P, PACK, HALF], F32, name, at)
@@ -108,7 +109,7 @@ def tile_list_handover_gradient_kernel(
             return plane
 
         tab_s = placed([P, T + 4], U8, "tab_s")
-        pages = [placed([P, T2], F32, "page%d" % u) for u in range(2)]
+        pages = [placed([P, T2], F32, "page%d" % u) for u in range(NT - 1)]
         nc.vector.memset(tab_s[32:64, :].bitcast(I32), 0)
         nc.vector.memset(tab_s[64:P, :].bitcast(I32), 0)
         for page in pages:
@@ -119,15 +120,11 @@ def tile_list_handover_gradient_kernel(
             out=tab_s[0:32, 0:T].bitcast(I32),
             in_=tab_scales[0].bitcast(I32).unsqueeze(1).to_broadcast([16, 2, T // 4]),
         )
-        wf_raw0 = load_wf(0, PAGE1)
         price_sb = placed([P, BLOCKS, PACK], F32, "price_sb")
         nc.scalar.dma_start(out=price_sb[:], in_=price.rearrange("(b p t) -> p b t", p=P, t=PACK))
 
         v_s_raw = placed([P, S], U8, "v_s_raw")
         nc.vector.tensor_copy(v_s_raw[:], tab_s[:, 0:T].indirect(idx[:]))
-        wf_w = [deal_wf(0, wf_raw0)]
-        pages.append(placed([P, T2], F32, "page2", PAGE1))
-        nc.gpsimd.memset(pages[2][:], 0.0)
 
         planes = []
         xs = {}
@@ -193,16 +190,15 @@ def tile_list_handover_gradient_kernel(
                 nc.gpsimd.memset(wf_s_raw[:].bitcast(I32), 0)
             if k == PACK - 1:
                 for half in range(HALVES):
-                    c_grouped[0, half] = interleave("c0%d" % half, c_rows[0][:, half, :, :], (PAGE3, GROUPED[1])[half])
+                    c_grouped[0, half] = interleave("c0%d" % half, c_rows[0][:, half, :, :], GROUPED[half])
 
+        wf_raw0 = load_wf(0, SLOT[2] + KIB)
         for q in range(4):
             nc.sync.dma_start(
                 out=wf_s_raw[32 * q : 32 * q + 4 * BLOCKS, :].bitcast(I32),
                 in_=wf_scales.bitcast(I32)[:, 4 * q : 4 * q + 4, :],
             )
-        v_s = placed([P, S], U8, "v_s")
-        for r in range(4):
-            nc.sync.dma_start(out=v_s[r:P:32, :].bitcast(I32), in_=v_s_raw[2 * r : 32 : 8, :].bitcast(I32))
+        wf_w = [deal_wf(0, wf_raw0, LAST_PLANE + 3 * HALF)]
         wf_s = placed([P, H], U8, "wf_s", LAST_PLANE + HALF)
         nc.vector.tensor_copy(
             out=wf_s[:].rearrange("p (b t m) -> p b t m", t=PACK, m=P),
@@ -210,13 +206,18 @@ def tile_list_handover_gradient_kernel(
         )
         c_mx = {}
         c_mx[0, 0] = quantize("c00", c_grouped[0, 0], at=LAST_PLANE)
-        pages.append(placed([P, T2], F32, "page3", PAGE3))
-        nc.gpsimd.memset(pages[3][:], 0.0)
+        pool_slope(PLANES - 3, 0, HALF, RESTART)
 
         tab_w = placed([P, T], I32, "tab_w", TABLE)
         nc.sync.dma_start(out=tab_w[:], in_=tab_words[0].rearrange("p n t -> p (n t)").bitcast(I32))
         wf_raw1 = load_wf(1, SLOT[3])
-        w1_raw = [load_raw("w1_raw0", w1[:, 0:PASS], SLOT[4]), load_raw("w1_raw1", w1[:, PASS:H], SLOT[0])]
+        w1_raw = [load_raw("w1_raw0", w1[:, 0:PASS], W1A)]
+        v_s = placed([P, S], U8, "v_s", SLOT[4])
+        for q in range(4):
+            nc.sync.dma_start(
+                out=v_s[32 * q : 32 * q + 4, :].bitcast(I32), in_=v_s_raw[8 * q : 8 * q + 8 : 2, :].bitcast(I32)
+            )
+        w1_raw.append(load_raw("w1_raw1", w1[:, PASS:H], SLOT[0]))
         w2_raw = [load_raw("w2_raw0", w2[0:PASS, :], SLOT[1]), load_raw("w2_raw1", w2[PASS:H, :], BASE)]
         nc.sync.dma_start(idx2[:], offs2)
 
@@ -226,20 +227,20 @@ def tile_list_handover_gradient_kernel(
         price_rows(PLANES - 1, [0])
         c_grouped[1, 0] = interleave("c10", c_rows[1][:, 0, :, :], GROUPED[2])
         w1_grouped = [interleave_w1("w1a", w1_raw[0], PAGE2)]
-        w1_grouped.append(interleave_w1("w1b", w1_raw[1], GROUPED[0]))
+        w1_grouped.append(interleave_w1("w1b", w1_raw[1], PAGE3))
         price_rows(PLANES - 1, [1])
         c_grouped[1, 1] = interleave("c11", c_rows[1][:, 1, :, :], SLOT[0])
 
         after = TABLE
         wf_w.append(deal_wf(1, wf_raw1, after + 4 * KIB))
-        c_mx[0, 1] = quantize("c01", c_grouped[0, 1], at=after + HALF)
         c_mx[1, 0] = quantize("c10", c_grouped[1, 0], at=after)
-        vector_slope(PLANES - 2, S, GROUPED[1])
         w1_mx = [quantize("w1a", w1_grouped[0])]
+        c_mx[0, 1] = quantize("c01", c_grouped[0, 1], at=W1A + 2 * KIB)
         wgo_sb = placed([P, S], F32, "wgo_sb", PAGE2)
         nc.sync.dma_start(out=wgo_sb[:], in_=wgo)
-        vector_slope(PLANES - 1, HALF, SLOT[4])
-        pool_slope(PLANES - 3, 0, HALF, XS[PLANES - 1])
+        vector_slope(PLANES - 1, HALF, W1A)
+        vector_slope(PLANES - 2, S, W1A + 4 * KIB)
+        pool_slope(PLANES - 3, 1, HALF, XS[PLANES - 2])
 
         h_rows = {}
         h_mx = {}
@@ -279,19 +280,23 @@ def tile_list_handover_gradient_kernel(
             for t in range(PACK):
                 feedback_pass(banks[b, half][t], a, b * PACK + t, half)
 
-        def close_tiles(b, half, tiles):
-            for t in tiles:
+        def close_tiles(b, half):
+            for t in range(PACK):
                 k = b * PACK + t
                 d = banks[b, half][t]
-                if half == 1:
-                    feedback_pass(d, 1, k, half)
                 table_pass(d, k, half)
                 nc.vector.scalar_tensor_tensor(
                     out=h_rows[b, half][:, t, :], in0=slope[k, half], scalar=-1.0, in1=d[:], op0=MULT, op1=MULT
                 )
 
-        def cast_w2(b, part, at):
-            return interleave("w2_%d%d" % (b, part), w2_raw[b][:, :, part * COLS : (part + 1) * COLS], at, COLS)
+        def cast_w2(part, at):
+            grouped = placed([P, BLOCKS, COLS * PACK], BF16, "w2_%d_g" % part, at)
+            for b in range(BLOCKS):
+                nc.scalar.copy(
+                    out=grouped[:, b, :].rearrange("p (c i t) -> p c t i", i=4, t=PACK),
+                    in_=w2_raw[b][:, :, part * COLS : (part + 1) * COLS].rearrange("p t (c i) -> p c t i", i=4),
+                )
+            return grouped[:].rearrange("p b n -> p (b n)")
 
         def second_stage(half, u, at):
             users = slice(half * HALF, (half + 1) * HALF)
@@ -301,8 +306,8 @@ def tile_list_handover_gradient_kernel(
             for b in range(BLOCKS):
                 nc.tensor.matmul_mx(
                     out=y[:],
-                    lhsT=w2_mx[b, part][0][:, col : col + P].bitcast(E4),
-                    lhsT_scale=w2_mx[b, part][1][:, col : col + P],
+                    lhsT=w2_mx[part][0][:, b * COLS + col : b * COLS + col + P].bitcast(E4),
+                    lhsT_scale=w2_mx[part][1][:, b * COLS + col : b * COLS + col + P],
                     rhs=h_mx[b, half][0][:].bitcast(E4),
                     rhs_scale=h_mx[b, half][1][:],
                     start=(b == 0),
@@ -314,34 +319,34 @@ def tile_list_handover_gradient_kernel(
             if half == HALVES - 1:
                 nc.sync.dma_start(out=out[u * P : (u + 1) * P, :], in_=pages[u][:])
 
-        for a in range(BLOCKS):
-            for b in range(BLOCKS):
-                feedback(a, b, 0)
-        close_tiles(0, 0, range(PACK - 1))
+        feedback(0, 0, 0)
+        feedback(0, 1, 0)
+        feedback(1, 0, 0)
+        w2_low = cast_w2(0, XS[1])
+        close_tiles(0, 0)
+        feedback(1, 1, 0)
         w1_mx.append(quantize("w1b", w1_grouped[1], at=SPARE))
-        pool_slope(PLANES - 3, 1, HALF, GROUPED[0])
-        close_tiles(0, 0, [PACK - 1])
+        pages.append(placed([P, T2], F32, "page3", PAGE3))
+        nc.gpsimd.memset(pages[3][:], 0.0)
         h00_grouped = interleave("h00", h_rows[0, 0][:], XS[0])
         feedback(0, 0, 1)
-        close_tiles(1, 0, range(PACK))
+        close_tiles(1, 0)
         h10_grouped = interleave("h10", h_rows[1, 0][:], XS[3])
-        c_mx[1, 1] = quantize("c11", c_grouped[1, 1])
+        c_mx[1, 1] = quantize("c11", c_grouped[1, 1], at=RESTART)
+        feedback(1, 0, 1)
+        w2_mx[0] = quantize("w2_0", w2_low, at=RESTART + HALF)
         h_mx[0, 0] = quantize("h00", h00_grouped)
-        pool_slope(PLANES - 1, 1, HALF, XS[0])
+        pool_slope(PLANES - 1, 1, HALF, XS[1] - KIB)
+        close_tiles(0, 1)
         feedback(0, 1, 1)
-        close_tiles(0, 1, range(PACK))
+        feedback(1, 1, 1)
         h_mx[1, 0] = quantize("h10", h10_grouped)
-        w2_low = [cast_w2(b, 0, SLOT[0] + b * 2 * KIB) for b in range(BLOCKS)]
-        w2_mx[0, 0] = quantize("w2_00", w2_low[0], COLS)
-        w2_high = [cast_w2(b, 1, XS[3] + b * 2 * KIB) for b in range(BLOCKS)]
-        close_tiles(1, 1, range(2))
-        w2_mx[1, 0] = quantize("w2_10", w2_low[1], COLS)
-        close_tiles(1, 1, range(2, PACK))
-        for b in range(BLOCKS):
-            w2_mx[b, 1] = quantize("w2_%d1" % b, w2_high[b], COLS)
-        second_stage(0, 0, SLOT[4] + 4 * KIB)
-        second_stage(0, 1, SLOT[4] + 6 * KIB)
-        h_mx[0, 1] = quantize("h01", interleave("h01", h_rows[0, 1][:], XS[0]))
+        w2_high = cast_w2(1, XS[0] - KIB)
+        close_tiles(1, 1)
+        w2_mx[1] = quantize("w2_1", w2_high)
+        second_stage(0, 0, GROUPED[1])
+        second_stage(0, 1, GROUPED[1] + 2 * KIB)
+        h_mx[0, 1] = quantize("h01", interleave("h01", h_rows[0, 1][:], XS[1]))
         h_mx[1, 1] = quantize("h11", interleave("h11", h_rows[1, 1][:], ROWS[1]))
         second_stage(0, 2, rows_at[1, 1])
         second_stage(0, 3, rows_at[1, 1] + 2 * KIB)

@@ -37,7 +37,7 @@ TABLE = SLOT[3] + 4 * KIB
 W1A = SLOT[4] + KIB
 SPARE = BASE + 117 * KIB
 ROWS = [BASE + 45 * KIB, BASE + 53 * KIB]
-GROUPED = [0, SPARE + 2 * KIB, BASE + 69 * KIB]
+GROUPED = [0, BASE + 113 * KIB, BASE + 69 * KIB]
 XS = [BASE + (73 + 4 * g) * KIB for g in range(PLANES)]
 PAGE2 = BASE + 105 * KIB
 PAGE3 = BASE + 109 * KIB
@@ -93,13 +93,18 @@ def tile_list_handover_gradient_kernel(
             nc.sync.dma_start(out=raw[:], in_=wf_words[a].rearrange("p n t -> p (n t)").bitcast(I32))
             return raw
 
-        def deal_wf(a, raw, at=None):
-            words = placed([P, H], I32, "wf_w%d" % a, at)
+        wf_w = {}
+
+        def deal_wf(a, raw, first, count, at):
+            words = placed([P, count * PASS], I32, "wf_w%d%d" % (a, first), at)
             nc.vector.tensor_copy(
                 out=words[:].rearrange("p (b t c i) -> p b c t i", t=PACK, c=32, i=4),
-                in_=raw[:].rearrange("p (b c i t) -> p b c t i", t=PACK, c=32, i=4),
+                in_=raw[:, first * PASS : (first + count) * PASS].rearrange(
+                    "p (b c i t) -> p b c t i", t=PACK, c=32, i=4
+                ),
             )
-            return words
+            for b in range(count):
+                wf_w[a, first + b] = words[:, b * PASS : (b + 1) * PASS]
 
         s_rows = sT.rearrange("(b p t) n -> b t p n", p=P, t=PACK)
 
@@ -111,7 +116,7 @@ def tile_list_handover_gradient_kernel(
         tab_s = placed([P, T + 4], U8, "tab_s")
         pages = [placed([P, T2], F32, "page%d" % u) for u in range(NT - 1)]
         nc.vector.memset(tab_s[32:64, :].bitcast(I32), 0)
-        nc.vector.memset(tab_s[64:P, :].bitcast(I32), 0)
+        nc.gpsimd.memset(tab_s[64:P, :].bitcast(I32), 0)
         for page in pages:
             nc.gpsimd.memset(page[:], 0.0)
 
@@ -198,7 +203,7 @@ def tile_list_handover_gradient_kernel(
                 out=wf_s_raw[32 * q : 32 * q + 4 * BLOCKS, :].bitcast(I32),
                 in_=wf_scales.bitcast(I32)[:, 4 * q : 4 * q + 4, :],
             )
-        wf_w = [deal_wf(0, wf_raw0, LAST_PLANE + 3 * HALF)]
+        deal_wf(0, wf_raw0, 0, BLOCKS, LAST_PLANE + 3 * HALF)
         wf_s = placed([P, H], U8, "wf_s", LAST_PLANE + HALF)
         nc.vector.tensor_copy(
             out=wf_s[:].rearrange("p (b t m) -> p b t m", t=PACK, m=P),
@@ -232,12 +237,12 @@ def tile_list_handover_gradient_kernel(
         c_grouped[1, 1] = interleave("c11", c_rows[1][:, 1, :, :], SLOT[0])
 
         after = TABLE
-        wf_w.append(deal_wf(1, wf_raw1, after + 4 * KIB))
+        deal_wf(1, wf_raw1, 0, 1, after + 4 * KIB)
         c_mx[1, 0] = quantize("c10", c_grouped[1, 0], at=after)
         w1_mx = [quantize("w1a", w1_grouped[0])]
-        c_mx[0, 1] = quantize("c01", c_grouped[0, 1], at=W1A + 2 * KIB)
         wgo_sb = placed([P, S], F32, "wgo_sb", PAGE2)
         nc.sync.dma_start(out=wgo_sb[:], in_=wgo)
+        deal_wf(1, wf_raw1, 1, 1, W1A + 2 * KIB)
         vector_slope(PLANES - 1, HALF, W1A)
         vector_slope(PLANES - 2, S, W1A + 4 * KIB)
         pool_slope(PLANES - 3, 1, HALF, XS[PLANES - 2])
@@ -250,7 +255,7 @@ def tile_list_handover_gradient_kernel(
         def feedback_pass(d, a, k, half):
             nc.tensor.matmul_mx(
                 out=d[:],
-                lhsT=wf_w[a][:, k * P : (k + 1) * P].bitcast(E4),
+                lhsT=wf_w[a, k // PACK][:, k % PACK * P : (k % PACK + 1) * P].bitcast(E4),
                 lhsT_scale=wf_s[4 * a : P, k * P : (k + 1) * P],
                 rhs=c_mx[a, half][0][:].bitcast(E4),
                 rhs_scale=c_mx[a, half][1][:],
@@ -280,10 +285,12 @@ def tile_list_handover_gradient_kernel(
             for t in range(PACK):
                 feedback_pass(banks[b, half][t], a, b * PACK + t, half)
 
-        def close_tiles(b, half):
-            for t in range(PACK):
+        def close_tiles(b, half, tiles=range(PACK)):
+            for t in tiles:
                 k = b * PACK + t
                 d = banks[b, half][t]
+                if half == 1:
+                    feedback_pass(d, 1, k, half)
                 table_pass(d, k, half)
                 nc.vector.scalar_tensor_tensor(
                     out=h_rows[b, half][:, t, :], in0=slope[k, half], scalar=-1.0, in1=d[:], op0=MULT, op1=MULT
@@ -322,32 +329,32 @@ def tile_list_handover_gradient_kernel(
         feedback(0, 0, 0)
         feedback(0, 1, 0)
         feedback(1, 0, 0)
-        w2_low = cast_w2(0, XS[1])
         close_tiles(0, 0)
         feedback(1, 1, 0)
         w1_mx.append(quantize("w1b", w1_grouped[1], at=SPARE))
+        c_mx[0, 1] = quantize("c01", c_grouped[0, 1], at=SLOT[0] + 4 * KIB)
         pages.append(placed([P, T2], F32, "page3", PAGE3))
         nc.gpsimd.memset(pages[3][:], 0.0)
-        h00_grouped = interleave("h00", h_rows[0, 0][:], XS[0])
-        feedback(0, 0, 1)
+        h00_grouped = interleave("h00", h_rows[0, 0][:], ROWS[1])
         close_tiles(1, 0)
         h10_grouped = interleave("h10", h_rows[1, 0][:], XS[3])
-        c_mx[1, 1] = quantize("c11", c_grouped[1, 1], at=RESTART)
-        feedback(1, 0, 1)
-        w2_mx[0] = quantize("w2_0", w2_low, at=RESTART + HALF)
-        h_mx[0, 0] = quantize("h00", h00_grouped)
-        pool_slope(PLANES - 1, 1, HALF, XS[1] - KIB)
-        close_tiles(0, 1)
+        feedback(0, 0, 1)
         feedback(0, 1, 1)
-        feedback(1, 1, 1)
+        c_mx[1, 1] = quantize("c11", c_grouped[1, 1], at=RESTART)
+        h_mx[0, 0] = quantize("h00", h00_grouped)
+        pool_slope(PLANES - 1, 1, HALF, ROWS[1] + 3 * KIB)
+        close_tiles(0, 1)
         h_mx[1, 0] = quantize("h10", h10_grouped)
-        w2_high = cast_w2(1, XS[0] - KIB)
-        close_tiles(1, 1)
+        w2_low = cast_w2(0, XS[1])
+        w2_high = cast_w2(1, XS[3])
+        close_tiles(1, 1, range(1))
+        w2_mx[0] = quantize("w2_0", w2_low)
+        close_tiles(1, 1, range(1, PACK))
         w2_mx[1] = quantize("w2_1", w2_high)
-        second_stage(0, 0, GROUPED[1])
-        second_stage(0, 1, GROUPED[1] + 2 * KIB)
-        h_mx[0, 1] = quantize("h01", interleave("h01", h_rows[0, 1][:], XS[1]))
-        h_mx[1, 1] = quantize("h11", interleave("h11", h_rows[1, 1][:], ROWS[1]))
+        second_stage(0, 0, SPARE + 2 * KIB)
+        second_stage(0, 1, SPARE + 4 * KIB)
+        h_mx[0, 1] = quantize("h01", interleave("h01", h_rows[0, 1][:], ROWS[1] + 4 * KIB))
+        h_mx[1, 1] = quantize("h11", interleave("h11", h_rows[1, 1][:], XS[0]))
         second_stage(0, 2, rows_at[1, 1])
         second_stage(0, 3, rows_at[1, 1] + 2 * KIB)
         for u in range(NT):

@@ -32,7 +32,6 @@ KIB = 1024
 BASE = 15 * KIB
 SLOT = [BASE + 8 * KIB, BASE + 16 * KIB, 4 * KIB, BASE + 24 * KIB, BASE + 36 * KIB]
 LAST_PLANE = 9 * KIB
-RESTART = SLOT[2] - HALF
 TABLE = SLOT[3] + 4 * KIB
 W1A = SLOT[4] + KIB
 SPARE = BASE + 117 * KIB
@@ -211,7 +210,8 @@ def tile_list_handover_gradient_kernel(
         )
         c_mx = {}
         c_mx[0, 0] = quantize("c00", c_grouped[0, 0], at=LAST_PLANE)
-        pool_slope(PLANES - 3, 0, HALF, RESTART)
+        pages.append(placed([P, T2], F32, "page3", GROUPED[0]))
+        nc.gpsimd.memset(pages[3][:], 0.0)
 
         tab_w = placed([P, T], I32, "tab_w", TABLE)
         nc.sync.dma_start(out=tab_w[:], in_=tab_words[0].rearrange("p n t -> p (n t)").bitcast(I32))
@@ -237,15 +237,15 @@ def tile_list_handover_gradient_kernel(
         c_grouped[1, 1] = interleave("c11", c_rows[1][:, 1, :, :], SLOT[0])
 
         after = TABLE
-        deal_wf(1, wf_raw1, 0, 1, after + 4 * KIB)
+        deal_wf(1, wf_raw1, 0, 1, after + HALF)
         c_mx[1, 0] = quantize("c10", c_grouped[1, 0], at=after)
+        vector_slope(PLANES - 2, S, after + 4 * KIB)
         w1_mx = [quantize("w1a", w1_grouped[0])]
         wgo_sb = placed([P, S], F32, "wgo_sb", PAGE2)
         nc.sync.dma_start(out=wgo_sb[:], in_=wgo)
         deal_wf(1, wf_raw1, 1, 1, W1A + 2 * KIB)
         vector_slope(PLANES - 1, HALF, W1A)
-        vector_slope(PLANES - 2, S, W1A + 4 * KIB)
-        pool_slope(PLANES - 3, 1, HALF, XS[PLANES - 2])
+        pool_slope(PLANES - 3, 0, HALF, XS[PLANES - 1])
 
         h_rows = {}
         h_mx = {}
@@ -333,29 +333,27 @@ def tile_list_handover_gradient_kernel(
         feedback(1, 1, 0)
         w1_mx.append(quantize("w1b", w1_grouped[1], at=SPARE))
         c_mx[0, 1] = quantize("c01", c_grouped[0, 1], at=SLOT[0] + 4 * KIB)
-        pages.append(placed([P, T2], F32, "page3", PAGE3))
-        nc.gpsimd.memset(pages[3][:], 0.0)
-        h00_grouped = interleave("h00", h_rows[0, 0][:], ROWS[1])
+        pool_slope(PLANES - 3, 1, HALF, PAGE3 + 3 * KIB)
+        h00_grouped = interleave("h00", h_rows[0, 0][:], ROWS[1] + 4 * KIB)
         close_tiles(1, 0)
         h10_grouped = interleave("h10", h_rows[1, 0][:], XS[3])
         feedback(0, 0, 1)
         feedback(0, 1, 1)
-        c_mx[1, 1] = quantize("c11", c_grouped[1, 1], at=RESTART)
+        c_mx[1, 1] = quantize("c11", c_grouped[1, 1], at=XS[PLANES - 1])
         h_mx[0, 0] = quantize("h00", h00_grouped)
-        pool_slope(PLANES - 1, 1, HALF, ROWS[1] + 3 * KIB)
+        pool_slope(PLANES - 1, 1, HALF, ROWS[1] + 7 * KIB)
         close_tiles(0, 1)
         h_mx[1, 0] = quantize("h10", h10_grouped)
         w2_low = cast_w2(0, XS[1])
-        w2_high = cast_w2(1, XS[3])
         close_tiles(1, 1, range(1))
         w2_mx[0] = quantize("w2_0", w2_low)
         close_tiles(1, 1, range(1, PACK))
-        w2_mx[1] = quantize("w2_1", w2_high)
         second_stage(0, 0, SPARE + 2 * KIB)
-        second_stage(0, 1, SPARE + 4 * KIB)
-        h_mx[0, 1] = quantize("h01", interleave("h01", h_rows[0, 1][:], ROWS[1] + 4 * KIB))
-        h_mx[1, 1] = quantize("h11", interleave("h11", h_rows[1, 1][:], XS[0]))
-        second_stage(0, 2, rows_at[1, 1])
-        second_stage(0, 3, rows_at[1, 1] + 2 * KIB)
+        w2_mx[1] = quantize("w2_1", cast_w2(1, ROWS[1] + 8 * KIB))
+        second_stage(0, 1, BASE)
+        h_mx[0, 1] = quantize("h01", interleave("h01", h_rows[0, 1][:], ROWS[1] + 5 * KIB))
+        second_stage(0, 2, XS[0])
+        h_mx[1, 1] = quantize("h11", interleave("h11", h_rows[1, 1][:], ROWS[1] + 11 * KIB))
+        second_stage(0, 3, rows_at[1, 1])
         for u in range(NT):
             second_stage(1, u, SLOT[1] + u * 2 * KIB)

@@ -32,6 +32,7 @@ KIB = 1024
 BASE = 15 * KIB
 SLOT = [BASE + 8 * KIB, BASE + 16 * KIB, 4 * KIB, BASE + 24 * KIB, BASE + 36 * KIB]
 LAST_PLANE = 9 * KIB
+RESTART = SLOT[2] - HALF
 TABLE = SLOT[3] + 4 * KIB
 W1A = SLOT[4] + KIB
 SPARE = BASE + 117 * KIB
@@ -113,9 +114,9 @@ def tile_list_handover_gradient_kernel(
             return plane
 
         tab_s = placed([P, T + 4], U8, "tab_s")
-        pages = [placed([P, T2], F32, "page%d" % u) for u in range(NT - 1)]
+        pages = [placed([P, T2], F32, "page%d" % u) for u in range(NT)]
         nc.vector.memset(tab_s[32:64, :].bitcast(I32), 0)
-        nc.gpsimd.memset(tab_s[64:P, :].bitcast(I32), 0)
+        nc.vector.memset(tab_s[64:P, :].bitcast(I32), 0)
         for page in pages:
             nc.gpsimd.memset(page[:], 0.0)
 
@@ -210,8 +211,7 @@ def tile_list_handover_gradient_kernel(
         )
         c_mx = {}
         c_mx[0, 0] = quantize("c00", c_grouped[0, 0], at=LAST_PLANE)
-        pages.append(placed([P, T2], F32, "page3", GROUPED[0]))
-        nc.gpsimd.memset(pages[3][:], 0.0)
+        pool_slope(PLANES - 3, 0, HALF, RESTART)
 
         tab_w = placed([P, T], I32, "tab_w", TABLE)
         nc.sync.dma_start(out=tab_w[:], in_=tab_words[0].rearrange("p n t -> p (n t)").bitcast(I32))
@@ -239,13 +239,13 @@ def tile_list_handover_gradient_kernel(
         after = TABLE
         deal_wf(1, wf_raw1, 0, 1, after + HALF)
         c_mx[1, 0] = quantize("c10", c_grouped[1, 0], at=after)
-        vector_slope(PLANES - 2, S, after + 4 * KIB)
+        vector_slope(PLANES - 2, HALF, after + 4 * KIB)
         w1_mx = [quantize("w1a", w1_grouped[0])]
         wgo_sb = placed([P, S], F32, "wgo_sb", PAGE2)
         nc.sync.dma_start(out=wgo_sb[:], in_=wgo)
         deal_wf(1, wf_raw1, 1, 1, W1A + 2 * KIB)
         vector_slope(PLANES - 1, HALF, W1A)
-        pool_slope(PLANES - 3, 0, HALF, XS[PLANES - 1])
+        pool_slope(PLANES - 3, 1, HALF, XS[PLANES - 1])
 
         h_rows = {}
         h_mx = {}
@@ -333,13 +333,13 @@ def tile_list_handover_gradient_kernel(
         feedback(1, 1, 0)
         w1_mx.append(quantize("w1b", w1_grouped[1], at=SPARE))
         c_mx[0, 1] = quantize("c01", c_grouped[0, 1], at=SLOT[0] + 4 * KIB)
-        pool_slope(PLANES - 3, 1, HALF, PAGE3 + 3 * KIB)
+        pool_slope(PLANES - 2, 1, HALF, PAGE3 + 3 * KIB)
         h00_grouped = interleave("h00", h_rows[0, 0][:], ROWS[1] + 4 * KIB)
         close_tiles(1, 0)
         h10_grouped = interleave("h10", h_rows[1, 0][:], XS[3])
         feedback(0, 0, 1)
         feedback(0, 1, 1)
-        c_mx[1, 1] = quantize("c11", c_grouped[1, 1], at=XS[PLANES - 1])
+        c_mx[1, 1] = quantize("c11", c_grouped[1, 1], at=RESTART)
         h_mx[0, 0] = quantize("h00", h00_grouped)
         pool_slope(PLANES - 1, 1, HALF, ROWS[1] + 7 * KIB)
         close_tiles(0, 1)

@@ -30,17 +30,17 @@ COLS = N // 2
 
 KIB = 1024
 BASE = 15 * KIB
-SLOT = [BASE + 8 * KIB, BASE + 16 * KIB, 4 * KIB, BASE + 24 * KIB, BASE + 36 * KIB]
+SLOT = [BASE + 8 * KIB, BASE + 16 * KIB, 4 * KIB, BASE + 28 * KIB, BASE + 42 * KIB]
 LAST_PLANE = 9 * KIB
 RESTART = SLOT[2] - HALF
-TABLE = SLOT[3] + 4 * KIB
-W1A = SLOT[4] + KIB
-SPARE = BASE + 117 * KIB
-ROWS = [BASE + 45 * KIB, BASE + 53 * KIB]
-GROUPED = [0, BASE + 113 * KIB, BASE + 69 * KIB]
-XS = [BASE + (73 + 4 * g) * KIB for g in range(PLANES)]
-PAGE2 = BASE + 105 * KIB
-PAGE3 = BASE + 109 * KIB
+TABLE = SLOT[3] + 6 * KIB
+W1A = SLOT[3] - 4 * KIB
+SPARE = BASE + 122 * KIB
+ROWS = [BASE + 50 * KIB, BASE + 58 * KIB]
+GROUPED = [0, BASE + 118 * KIB, BASE + 74 * KIB]
+XS = [BASE + (78 + 4 * g) * KIB for g in range(PLANES)]
+PAGE2 = BASE + 110 * KIB
+PAGE3 = BASE + 114 * KIB
 SCALAR_PLANES = 3
 
 
@@ -88,9 +88,10 @@ def tile_list_handover_gradient_kernel(
             nc.sync.dma_start(out=raw[:], in_=rows.rearrange("(p j) c -> p j c", j=PACK))
             return raw
 
-        def load_wf(a, at):
-            raw = placed([P, H], I32, "wf_raw%d" % a, at)
-            nc.sync.dma_start(out=raw[:], in_=wf_words[a].rearrange("p n t -> p (n t)").bitcast(I32))
+        def load_wf(a, first, count, at):
+            raw = placed([P, count * PASS], I32, "wf_raw%d%d" % (a, first), at)
+            words = wf_words[a].rearrange("p n t -> p (n t)").bitcast(I32)
+            nc.sync.dma_start(out=raw[:], in_=words[:, first * PASS : (first + count) * PASS])
             return raw
 
         wf_w = {}
@@ -99,9 +100,7 @@ def tile_list_handover_gradient_kernel(
             words = placed([P, count * PASS], I32, "wf_w%d%d" % (a, first), at)
             nc.vector.tensor_copy(
                 out=words[:].rearrange("p (b t c i) -> p b c t i", t=PACK, c=32, i=4),
-                in_=raw[:, first * PASS : (first + count) * PASS].rearrange(
-                    "p (b c i t) -> p b c t i", t=PACK, c=32, i=4
-                ),
+                in_=raw[:].rearrange("p (b c i t) -> p b c t i", t=PACK, c=32, i=4),
             )
             for b in range(count):
                 wf_w[a, first + b] = words[:, b * PASS : (b + 1) * PASS]
@@ -121,12 +120,9 @@ def tile_list_handover_gradient_kernel(
             nc.gpsimd.memset(page[:], 0.0)
 
         nc.sync.dma_start(idx[:], offs)
-        nc.sync.dma_start(
-            out=tab_s[0:32, 0:T].bitcast(I32),
-            in_=tab_scales[0].bitcast(I32).unsqueeze(1).to_broadcast([16, 2, T // 4]),
-        )
+        for first in (0, 16):
+            nc.sync.dma_start(out=tab_s[first : first + 16, 0:T].bitcast(I32), in_=tab_scales[0].bitcast(I32))
         price_sb = placed([P, BLOCKS, PACK], F32, "price_sb")
-        nc.scalar.dma_start(out=price_sb[:], in_=price.rearrange("(b p t) -> p b t", p=P, t=PACK))
 
         v_s_raw = placed([P, S], U8, "v_s_raw")
         nc.vector.tensor_copy(v_s_raw[:], tab_s[:, 0:T].indirect(idx[:]))
@@ -173,6 +169,8 @@ def tile_list_handover_gradient_kernel(
         for k in range(PLANES):
             b, t = divmod(k, PACK)
             planes.append(load_plane(k))
+            if k == 0:
+                nc.sync.dma_start(out=price_sb[:], in_=price.rearrange("(b p t) -> p b t", p=P, t=PACK))
             if k < PLANES - 1:
                 xs[k] = placed([P, S], F32, "x%d" % k, XS[k])
                 nc.vector.tensor_copy(xs[k][:], planes[k][:].indirect(idx[:]))
@@ -197,7 +195,7 @@ def tile_list_handover_gradient_kernel(
                 for half in range(HALVES):
                     c_grouped[0, half] = interleave("c0%d" % half, c_rows[0][:, half, :, :], GROUPED[half])
 
-        wf_raw0 = load_wf(0, SLOT[2] + KIB)
+        wf_raw0 = load_wf(0, 0, BLOCKS, SLOT[2] + KIB)
         for q in range(4):
             nc.sync.dma_start(
                 out=wf_s_raw[32 * q : 32 * q + 4 * BLOCKS, :].bitcast(I32),
@@ -215,12 +213,13 @@ def tile_list_handover_gradient_kernel(
 
         tab_w = placed([P, T], I32, "tab_w", TABLE)
         nc.sync.dma_start(out=tab_w[:], in_=tab_words[0].rearrange("p n t -> p (n t)").bitcast(I32))
-        wf_raw1 = load_wf(1, SLOT[3])
+        wf_raw1 = [load_wf(1, 0, 1, SLOT[3] + 4 * KIB)]
         w1_raw = [load_raw("w1_raw0", w1[:, 0:PASS], W1A)]
+        wf_raw1.append(load_wf(1, 1, 1, SLOT[4] + KIB))
         v_s = placed([P, S], U8, "v_s", SLOT[4])
         for q in range(4):
             nc.sync.dma_start(
-                out=v_s[32 * q : 32 * q + 4, :].bitcast(I32), in_=v_s_raw[8 * q : 8 * q + 8 : 2, :].bitcast(I32)
+                out=v_s[32 * q : 32 * q + 4, :].bitcast(I32), in_=v_s_raw[4 * q : 4 * q + 4, :].bitcast(I32)
             )
         w1_raw.append(load_raw("w1_raw1", w1[:, PASS:H], SLOT[0]))
         w2_raw = [load_raw("w2_raw0", w2[0:PASS, :], SLOT[1]), load_raw("w2_raw1", w2[PASS:H, :], BASE)]
@@ -237,13 +236,13 @@ def tile_list_handover_gradient_kernel(
         c_grouped[1, 1] = interleave("c11", c_rows[1][:, 1, :, :], SLOT[0])
 
         after = TABLE
-        deal_wf(1, wf_raw1, 0, 1, after + HALF)
+        deal_wf(1, wf_raw1[0], 0, 1, after + HALF)
         c_mx[1, 0] = quantize("c10", c_grouped[1, 0], at=after)
         vector_slope(PLANES - 2, HALF, after + 4 * KIB)
         w1_mx = [quantize("w1a", w1_grouped[0])]
         wgo_sb = placed([P, S], F32, "wgo_sb", PAGE2)
         nc.sync.dma_start(out=wgo_sb[:], in_=wgo)
-        deal_wf(1, wf_raw1, 1, 1, W1A + 2 * KIB)
+        deal_wf(1, wf_raw1[1], 1, 1, W1A + 2 * KIB)
         vector_slope(PLANES - 1, HALF, W1A)
         pool_slope(PLANES - 3, 1, HALF, XS[PLANES - 1])
 

@@ -320,8 +320,8 @@ def tile_list_handover_gradient_kernel(
                     stop=(b == BLOCKS - 1),
                 )
             y_sb = placed([P, HALF], F32, "y%d%d" % (half, u), at)
-            nc.scalar.copy(out=y_sb[:], in_=y[:])
-            nc.vector.tensor_tensor(pages[u][:].indirect(slots), y_sb[:], wgo_sb[:, users], MULT)
+            nc.vector.tensor_tensor(y_sb[:], wgo_sb[:, users], y[:], MULT)
+            nc.vector.tensor_copy(pages[u][:].indirect(slots), y_sb[:])
             if half == HALVES - 1:
                 nc.sync.dma_start(out=out[u * P : (u + 1) * P, :], in_=pages[u][:])
 

@@ -22,26 +22,23 @@ P = 128
 PACK = 4
 PASS = P * PACK
 HALF = 512
+QUARTER = 256
 BLOCKS = H // PASS
-HALVES = S // HALF
 PLANES = BLOCKS * PACK
 NT = N // P
 COLS = N // 2
+BANK = 2048
 
 KIB = 1024
-BASE = 15 * KIB
-SLOT = [BASE + 8 * KIB, BASE + 16 * KIB, 4 * KIB, BASE + 28 * KIB, BASE + 42 * KIB]
-LAST_PLANE = 9 * KIB
-RESTART = SLOT[2] - HALF
-TABLE = SLOT[3] + 6 * KIB
-W1A = SLOT[3] - 4 * KIB
-SPARE = BASE + 122 * KIB
-ROWS = [BASE + 50 * KIB, BASE + 58 * KIB]
-GROUPED = [0, BASE + 118 * KIB, BASE + 74 * KIB]
-XS = [BASE + (78 + 4 * g) * KIB for g in range(PLANES)]
-PAGE2 = BASE + 110 * KIB
-PAGE3 = BASE + 114 * KIB
-SCALAR_PLANES = 3
+SLOT = [0, 9 * KIB, 17 * KIB, 31 * KIB, 39 * KIB]
+LAST_PLANE = 22 * KIB
+TABLE = 43 * KIB
+ROWS01 = 51 * KIB
+ROWS00 = 56 * KIB + HALF
+ROWS10 = 76 * KIB
+ROWS11 = ROWS01
+CG00, CG01, CG10, WG1A, WG1B, WF0, W2HI = (k * KIB for k in (64, 68, 72, 106, 80, 84, 88))
+Y00, Y01, Y10, Y_LAST = (k * KIB for k in (91, 92, 96, 97))
 
 
 def tile_list_handover_gradient_kernel(
@@ -67,50 +64,77 @@ def tile_list_handover_gradient_kernel(
             nc.vector.quantize_mx(out=codes[:].bitcast(E4), scales=scales[:], in_=grouped)
             return codes, scales
 
-        def interleave(name, rows, at=None, width=HALF):
-            grouped = placed([P, width * PACK], BF16, name + "_g", at)
+        def interleave(name, rows, at):
+            grouped = placed([P, HALF * PACK], BF16, name + "_g", at)
             nc.scalar.copy(
                 out=grouped[:].rearrange("p (c i t) -> p c t i", i=4, t=PACK),
                 in_=rows.rearrange("p t (c i) -> p c t i", i=4),
             )
             return grouped[:]
 
-        def interleave_w1(name, raw, at=None):
-            grouped = placed([P, HALF * PACK], BF16, name + "_g", at)
-            nc.scalar.copy(
-                out=grouped[:].rearrange("p (t m j) -> p m j t", t=PACK, j=PACK),
-                in_=raw[:].rearrange("p j (m t) -> p m j t", t=PACK),
-            )
+        def load_w1(b, at, parts):
+            width = PASS // parts
+            raws = []
+            for part in range(parts):
+                raw = placed([P, PACK, width], F32, "w1_raw%d%d" % (b, part), at + part * width * PACK * 4)
+                cols = w1[:, b * PASS + part * width : b * PASS + (part + 1) * width]
+                nc.sync.dma_start(out=raw[:], in_=cols.rearrange("(p j) c -> p j c", j=PACK))
+                raws.append(raw)
+            return raws
+
+        def cast_w1(b, raws, at):
+            grouped = placed([P, PASS * PACK], BF16, "w1_g%d" % b, at)
+            dealt = grouped[:].rearrange("p (t m j) -> p m j t", t=PACK, j=PACK)
+            width = P // len(raws)
+            for part, raw in enumerate(raws):
+                nc.scalar.copy(
+                    out=dealt[:, part * width : (part + 1) * width, :, :],
+                    in_=raw[:].rearrange("p j (m t) -> p m j t", t=PACK),
+                )
             return grouped[:]
 
-        def load_raw(name, rows, at):
-            raw = placed([P, PACK, HALF], F32, name, at)
-            nc.sync.dma_start(out=raw[:], in_=rows.rearrange("(p j) c -> p j c", j=PACK))
-            return raw
+        def load_w2(part, at):
+            raws = []
+            for b in range(BLOCKS):
+                raw = placed([P, PACK, COLS], F32, "w2_raw%d%d" % (part, b), at + b * 4 * KIB)
+                rows = w2[b * PASS : (b + 1) * PASS, part * COLS : (part + 1) * COLS]
+                nc.sync.dma_start(out=raw[:], in_=rows.rearrange("(p j) c -> p j c", j=PACK))
+                raws.append(raw)
+            return raws
 
-        def load_wf(a, first, count, at):
-            raw = placed([P, count * PASS], I32, "wf_raw%d%d" % (a, first), at)
-            words = wf_words[a].rearrange("p n t -> p (n t)").bitcast(I32)
-            nc.sync.dma_start(out=raw[:], in_=words[:, first * PASS : (first + count) * PASS])
-            return raw
+        def cast_w2(part, raws, at):
+            grouped = placed([P, BLOCKS, COLS * PACK], BF16, "w2_g%d" % part, at)
+            for b in range(BLOCKS):
+                nc.scalar.copy(
+                    out=grouped[:, b, :].rearrange("p (c i t) -> p c t i", i=4, t=PACK),
+                    in_=raws[b][:].rearrange("p t (c i) -> p c t i", i=4),
+                )
+            return grouped[:].rearrange("p b n -> p (b n)")
 
+        wf_raw = {}
         wf_w = {}
+        wf_s = {}
 
-        def deal_wf(a, raw, first, count, at):
-            words = placed([P, count * PASS], I32, "wf_w%d%d" % (a, first), at)
-            nc.vector.tensor_copy(
-                out=words[:].rearrange("p (b t c i) -> p b c t i", t=PACK, c=32, i=4),
-                in_=raw[:].rearrange("p (b c i t) -> p b c t i", t=PACK, c=32, i=4),
+        def load_wf(a, b, at):
+            wf_raw[a, b] = placed([P, PASS], I32, "wf_raw%d%d" % (a, b), at)
+            words = wf_words[a].rearrange("p n t -> p (n t)").bitcast(I32)
+            nc.sync.dma_start(out=wf_raw[a, b][:], in_=words[:, b * PASS : (b + 1) * PASS])
+
+        def deal_wf(a, b, at, copy=nc.vector.tensor_copy):
+            wf_w[a, b] = placed([P, PASS], U32, "wf_w%d%d" % (a, b), at)
+            copy(
+                out=wf_w[a, b][:].rearrange("p (t c i) -> p c t i", t=PACK, i=4),
+                in_=wf_raw[a, b][:].bitcast(U32).rearrange("p (c i t) -> p c t i", t=PACK, i=4),
             )
-            for b in range(count):
-                wf_w[a, first + b] = words[:, b * PASS : (b + 1) * PASS]
+
+        def deal_scales(b, at=None):
+            wf_s[b] = placed([P, PASS], U8, "wf_s%d" % b, at)
+            nc.vector.tensor_copy(
+                out=wf_s[b][:].rearrange("p (t m) -> p t m", t=PACK),
+                in_=wf_s_raw[:, b * PASS : (b + 1) * PASS].rearrange("p (m t) -> p t m", t=PACK),
+            )
 
         s_rows = sT.rearrange("(b p t) n -> b t p n", p=P, t=PACK)
-
-        def load_plane(k):
-            plane = placed([P, T], F32, "plane%d" % k, LAST_PLANE if k == PLANES - 1 else SLOT[k % 5])
-            nc.sync.dma_start(out=plane[:], in_=s_rows[k // PACK, k % PACK])
-            return plane
 
         tab_s = placed([P, T + 4], U8, "tab_s")
         pages = [placed([P, T2], F32, "page%d" % u) for u in range(NT)]
@@ -127,232 +151,241 @@ def tile_list_handover_gradient_kernel(
         v_s_raw = placed([P, S], U8, "v_s_raw")
         nc.vector.tensor_copy(v_s_raw[:], tab_s[:, 0:T].indirect(idx[:]))
 
-        planes = []
-        xs = {}
-        slope = {}
-        c_rows = {}
+        xs = [placed([P, PACK, S], F32, "x%d" % b) for b in range(BLOCKS)]
+        slope0 = placed([P, PACK, S], F32, "slope0")
+        less10 = placed([P, PACK, 3 * P], F32, "less10")
+        rows00 = placed([P, PACK, HALF], BF16, "rows00", ROWS00)
+        rows01 = placed([P, PACK, HALF], BF16, "rows01", ROWS01)
+        wf_s_raw = placed([P, H], U8, "wf_s_raw")
+        rows10 = placed([P, PACK, HALF], BF16, "rows10", ROWS10)
+
+        def priced(dst, src, b, t):
+            nc.scalar.activation(out=dst, in_=src, func=COPY, scale=price_sb[:, b, t : t + 1])
+
+        def vector_slope(g, at):
+            slope = placed([P, PACK, P], F32, "slope%d" % g, at)
+            x = xs[1][:, :, g * P : (g + 1) * P]
+            nc.vector.scalar_tensor_tensor(out=slope[:], in0=x, scalar=1.0, in1=x, op0=SUB, op1=MULT)
+            return slope[:]
+
+        nc.gpsimd.memset(wf_s_raw[:].bitcast(I32), 0)
         c_grouped = {}
-
-        def x_of(k, first, width):
-            if k == PLANES - 1:
-                return xs[k, first][:]
-            return xs[k][:, first * HALF : first * HALF + width]
-
-        def price_rows(k, halves):
-            b, t = divmod(k, PACK)
-            lo, hi = halves[0], halves[-1] + 1
-            nc.scalar.activation(
-                out=c_rows[b][:, lo:hi, t, :],
-                in_=x_of(k, lo, (hi - lo) * HALF).rearrange("p (h j) -> p h j", j=HALF),
-                func=COPY,
-                scale=price_sb[:, b, t : t + 1],
-            )
-
-        def pool_slope(k, first, width, at=None):
-            x = x_of(k, first, width)
-            tile = placed([P, width], F32, "slope%d_%d" % (k, first), at)
-            if k < SCALAR_PLANES:
-                nc.scalar.activation(out=tile[:], in_=x, func=COPY, bias=-1.0)
-            else:
-                nc.gpsimd.tensor_scalar(tile[:], x, 1.0, -1.0, MULT, ADD)
-            nc.gpsimd.tensor_tensor(tile[:], tile[:], x, MULT)
-            for half in range(width // HALF):
-                slope[k, first + half] = tile[:, half * HALF : (half + 1) * HALF]
-
-        def vector_slope(k, width, at):
-            x = x_of(k, 0, width)
-            tile = placed([P, width], F32, "slope%d" % k, at)
-            nc.vector.scalar_tensor_tensor(out=tile[:], in0=x, scalar=1.0, in1=x, op0=SUB, op1=MULT)
-            for half in range(width // HALF):
-                slope[k, half] = tile[:, half * HALF : (half + 1) * HALF]
-
         for k in range(PLANES):
             b, t = divmod(k, PACK)
-            planes.append(load_plane(k))
+            plane = placed([P, T], F32, "plane%d" % k, LAST_PLANE if k == PLANES - 1 else SLOT[k % 5])
+            nc.sync.dma_start(out=plane[:], in_=s_rows[b, t])
             if k == 0:
                 nc.sync.dma_start(out=price_sb[:], in_=price.rearrange("(b p t) -> p b t", p=P, t=PACK))
+            x = xs[b][:, t, :]
             if k < PLANES - 1:
-                xs[k] = placed([P, S], F32, "x%d" % k, XS[k])
-                nc.vector.tensor_copy(xs[k][:], planes[k][:].indirect(idx[:]))
+                nc.vector.tensor_copy(x, plane[:].indirect(idx[:]))
             else:
-                for half in range(HALVES):
-                    xs[k, half] = placed([P, HALF], F32, "x%d_%d" % (k, half), XS[k] + half * 2 * KIB)
+                for half in range(2):
                     picks = idx[:, half * HALF // 16 : (half + 1) * HALF // 16]
-                    nc.vector.tensor_copy(xs[k, half][:], planes[k][:].indirect(picks))
-            if t == 0:
-                c_rows[b] = placed([P, HALVES, PACK, HALF], BF16, "c_rows%d" % b, ROWS[b])
-            if k == 1:
-                pool_slope(k, 0, HALF, SPARE)
-                pool_slope(k, 1, HALF)
-            elif k < PLANES - 3:
-                pool_slope(k, 0, S)
-            if k < PLANES - 1:
-                price_rows(k, [0, 1])
-            if k == 2:
-                wf_s_raw = placed([P, H], U8, "wf_s_raw", SLOT[2])
-                nc.gpsimd.memset(wf_s_raw[:].bitcast(I32), 0)
+                    nc.vector.tensor_copy(x[:, half * HALF : (half + 1) * HALF], plane[:].indirect(picks))
+            if k < PACK - 1:
+                nc.scalar.activation(out=slope0[:, t, :], in_=x, func=COPY, bias=-1.0)
+                nc.gpsimd.tensor_tensor(slope0[:, t, :], slope0[:, t, :], x, MULT)
+            elif k == PACK - 1:
+                nc.gpsimd.tensor_scalar(slope0[:, t, :], x, 1.0, -1.0, MULT, ADD)
+                nc.gpsimd.tensor_tensor(slope0[:, t, :], slope0[:, t, :], x, MULT)
+            elif k < PLANES - 1:
+                nc.gpsimd.tensor_scalar(less10[:, t, :], x[:, 0 : 3 * P], 1.0, -1.0, MULT, ADD)
+            priced((rows00, rows10)[b][:, t, :], x[:, 0:HALF], b, t)
+            if b == 0:
+                priced(rows01[:, t, :], x[:, HALF:S], b, t)
             if k == PACK - 1:
-                for half in range(HALVES):
-                    c_grouped[0, half] = interleave("c0%d" % half, c_rows[0][:, half, :, :], GROUPED[half])
+                c_grouped[0, 0] = interleave("c00", rows00[:], CG00)
 
-        wf_raw0 = load_wf(0, 0, BLOCKS, SLOT[2] + KIB)
+        load_wf(0, 0, SLOT[2] + KIB)
         for q in range(4):
             nc.sync.dma_start(
                 out=wf_s_raw[32 * q : 32 * q + 4 * BLOCKS, :].bitcast(I32),
                 in_=wf_scales.bitcast(I32)[:, 4 * q : 4 * q + 4, :],
             )
-        deal_wf(0, wf_raw0, 0, BLOCKS, LAST_PLANE + 3 * HALF)
-        wf_s = placed([P, H], U8, "wf_s", LAST_PLANE + HALF)
-        nc.vector.tensor_copy(
-            out=wf_s[:].rearrange("p (b t m) -> p b t m", t=PACK, m=P),
-            in_=wf_s_raw[:].rearrange("p (b m t) -> p b t m", t=PACK, m=P),
-        )
-        c_mx = {}
-        c_mx[0, 0] = quantize("c00", c_grouped[0, 0], at=LAST_PLANE)
-        pool_slope(PLANES - 3, 0, HALF, RESTART)
-
+        load_wf(1, 0, SLOT[2] + 3 * KIB)
+        w1_raw = [load_w1(0, SLOT[3], 1)]
+        load_wf(0, 1, SLOT[4])
         tab_w = placed([P, T], I32, "tab_w", TABLE)
         nc.sync.dma_start(out=tab_w[:], in_=tab_words[0].rearrange("p n t -> p (n t)").bitcast(I32))
-        wf_raw1 = [load_wf(1, 0, 1, SLOT[3] + 4 * KIB)]
-        w1_raw = [load_raw("w1_raw0", w1[:, 0:PASS], W1A)]
-        wf_raw1.append(load_wf(1, 1, 1, SLOT[4] + KIB))
-        v_s = placed([P, S], U8, "v_s", SLOT[4])
+        load_wf(1, 1, SLOT[4] + 2 * KIB)
+        v_s = placed([P, S], U8, "v_s", SLOT[0])
         for q in range(4):
             nc.sync.dma_start(
                 out=v_s[32 * q : 32 * q + 4, :].bitcast(I32), in_=v_s_raw[4 * q : 4 * q + 4, :].bitcast(I32)
             )
-        w1_raw.append(load_raw("w1_raw1", w1[:, PASS:H], SLOT[0]))
-        w2_raw = [load_raw("w2_raw0", w2[0:PASS, :], SLOT[1]), load_raw("w2_raw1", w2[PASS:H, :], BASE)]
+        w1_raw.append(load_w1(1, SLOT[0] + KIB, 2))
+        w2_raw = [load_w2(0, SLOT[1])]
         nc.sync.dma_start(idx2[:], offs2)
 
-        v_w = placed([P, S], U32, "v_w")
-        nc.vector.tensor_copy(v_w[:], tab_w[:].bitcast(U32).indirect(idx[:]))
-
-        price_rows(PLANES - 1, [0])
-        c_grouped[1, 0] = interleave("c10", c_rows[1][:, 0, :, :], GROUPED[2])
-        w1_grouped = [interleave_w1("w1a", w1_raw[0], PAGE2)]
-        w1_grouped.append(interleave_w1("w1b", w1_raw[1], PAGE3))
-        price_rows(PLANES - 1, [1])
-        c_grouped[1, 1] = interleave("c11", c_rows[1][:, 1, :, :], SLOT[0])
-
-        after = TABLE
-        deal_wf(1, wf_raw1[0], 0, 1, after + HALF)
-        c_mx[1, 0] = quantize("c10", c_grouped[1, 0], at=after)
-        vector_slope(PLANES - 2, HALF, after + 4 * KIB)
-        w1_mx = [quantize("w1a", w1_grouped[0])]
-        wgo_sb = placed([P, S], F32, "wgo_sb", PAGE2)
+        deal_wf(0, 0, WF0)
+        deal_scales(0, LAST_PLANE)
+        c_mx = {}
+        c_mx[0, 0] = quantize("c00", c_grouped[0, 0], at=LAST_PLANE + HALF)
+        deal_wf(1, 0, WF0 + 2 * KIB)
+        deal_scales(1, SLOT[2] + 2 * KIB)
+        wgo_sb = placed([P, S], F32, "wgo_sb", SLOT[3])
         nc.sync.dma_start(out=wgo_sb[:], in_=wgo)
-        deal_wf(1, wf_raw1[1], 1, 1, W1A + 2 * KIB)
-        vector_slope(PLANES - 1, HALF, W1A)
-        pool_slope(PLANES - 3, 1, HALF, XS[PLANES - 1])
+        w2_raw.append(load_w2(1, LAST_PLANE + KIB))
 
-        h_rows = {}
-        h_mx = {}
-        w2_mx = {}
-        rows_at = {(0, 0): ROWS[0] + 4 * KIB, (1, 0): ROWS[0], (0, 1): ROWS[0] + 4 * KIB, (1, 1): ROWS[0]}
-
-        def feedback_pass(d, a, k, half):
-            nc.tensor.matmul_mx(
-                out=d[:],
-                lhsT=wf_w[a, k // PACK][:, k % PACK * P : (k % PACK + 1) * P].bitcast(E4),
-                lhsT_scale=wf_s[4 * a : P, k * P : (k + 1) * P],
-                rhs=c_mx[a, half][0][:].bitcast(E4),
-                rhs_scale=c_mx[a, half][1][:],
-                start=(a == 0),
-                stop=False,
-            )
-
-        def table_pass(d, k, half):
-            b, t = divmod(k, PACK)
-            users = slice(half * HALF, (half + 1) * HALF)
-            nc.tensor.matmul_mx(
-                out=d[:],
-                lhsT=w1_mx[b][0][:, t * P : (t + 1) * P].bitcast(E4),
-                lhsT_scale=w1_mx[b][1][:, t * P : (t + 1) * P],
-                rhs=v_w[:, users].bitcast(E5),
-                rhs_scale=v_s[:, users],
-                start=False,
-                stop=True,
-            )
+        c_grouped[1, 0] = interleave("c10", rows10[:], CG10)
+        w1_grouped = [cast_w1(0, w1_raw[0], WG1A)]
+        nc.scalar.activation(out=less10[:, PACK - 1, :], in_=xs[1][:, PACK - 1, 0 : 3 * P], func=COPY, bias=-1.0)
+        c_mx[1, 0] = quantize("c10", c_grouped[1, 0])
+        deal_wf(0, 1, ROWS10 + 2 * KIB)
+        slopes1 = {3: vector_slope(3, SLOT[2]), 4: vector_slope(4, ROWS10)}
+        codes, scales = quantize("w1a", w1_grouped[0])
+        w1_mx = {(0, t): (codes[:, t * P : (t + 1) * P], scales[:, t * P : (t + 1) * P]) for t in range(PACK)}
+        v_w = []
+        for half in range(2):
+            v_w.append(placed([P, HALF], U32, "v_w%d" % half, SLOT[3] + (4 + 2 * half) * KIB))
+            picks = idx[:, half * HALF // 16 : (half + 1) * HALF // 16]
+            nc.vector.tensor_copy(v_w[half][:], tab_w[:].bitcast(U32).indirect(picks))
+        slope10 = placed([P, 3, PACK, P], F32, "slope10", WG1A - KIB)
+        for g in range(3):
+            cols = slice(g * P, (g + 1) * P)
+            nc.gpsimd.tensor_tensor(slope10[:, g, :, :], less10[:, :, cols], xs[1][:, :, cols], MULT)
+            slopes1[g] = slope10[:, g, :, :]
 
         banks = {}
 
-        def feedback(a, b, half):
-            if a == 0:
-                h_rows[b, half] = placed([P, PACK, HALF], BF16, "h_rows%d%d" % (b, half), rows_at[b, half])
-                banks[b, half] = [psum.tile([P, HALF], F32, name="acc%d" % b, bufs=PACK) for t in range(PACK)]
+        def open_bank(b, g, bank):
+            banks[b, g] = [psum.tile([P, PACK, P], F32, name="d%d%d" % (b, g), offset=bank * BANK), 0]
+
+        def passes(b, g, kind):
+            half, first = divmod(g * P, HALF)
             for t in range(PACK):
-                feedback_pass(banks[b, half][t], a, b * PACK + t, half)
-
-        def close_tiles(b, half, tiles=range(PACK)):
-            for t in tiles:
-                k = b * PACK + t
-                d = banks[b, half][t]
-                if half == 1:
-                    feedback_pass(d, 1, k, half)
-                table_pass(d, k, half)
-                nc.vector.scalar_tensor_tensor(
-                    out=h_rows[b, half][:, t, :], in0=slope[k, half], scalar=-1.0, in1=d[:], op0=MULT, op1=MULT
-                )
-
-        def cast_w2(part, at):
-            grouped = placed([P, BLOCKS, COLS * PACK], BF16, "w2_%d_g" % part, at)
-            for b in range(BLOCKS):
-                nc.scalar.copy(
-                    out=grouped[:, b, :].rearrange("p (c i t) -> p c t i", i=4, t=PACK),
-                    in_=w2_raw[b][:, :, part * COLS : (part + 1) * COLS].rearrange("p t (c i) -> p c t i", i=4),
-                )
-            return grouped[:].rearrange("p b n -> p (b n)")
-
-        def second_stage(half, u, at):
-            users = slice(half * HALF, (half + 1) * HALF)
-            slots = idx2[:, half * HALF // 16 : (half + 1) * HALF // 16]
-            part, col = divmod(u * P, COLS)
-            y = psum.tile([P, HALF], F32, name="acc%d" % (1 - half), bufs=PACK)
-            for b in range(BLOCKS):
+                d, done = banks[b, g]
+                if kind == "table":
+                    lhs = w1_mx[b, t][0].bitcast(E4)
+                    lhs_scale = w1_mx[b, t][1]
+                    rhs = v_w[half][:, first : first + P].bitcast(E5)
+                    rhs_scale = v_s[:, g * P : (g + 1) * P]
+                else:
+                    lhs = wf_w[kind, b][:, t * P : (t + 1) * P].bitcast(E4)
+                    lhs_scale = wf_s[b][4 * kind : P, t * P : (t + 1) * P]
+                    rhs = c_mx[kind, half][0][:, first : first + P].bitcast(E4)
+                    rhs_scale = c_mx[kind, half][1][:, first : first + P]
                 nc.tensor.matmul_mx(
-                    out=y[:],
-                    lhsT=w2_mx[part][0][:, b * COLS + col : b * COLS + col + P].bitcast(E4),
-                    lhsT_scale=w2_mx[part][1][:, b * COLS + col : b * COLS + col + P],
-                    rhs=h_mx[b, half][0][:].bitcast(E4),
-                    rhs_scale=h_mx[b, half][1][:],
-                    start=(b == 0),
-                    stop=(b == BLOCKS - 1),
+                    out=d[:, t, :], lhsT=lhs, lhsT_scale=lhs_scale, rhs=rhs, rhs_scale=rhs_scale,
+                    start=(done == 0), stop=(done == 3 * PACK - 1),
                 )
-            y_sb = placed([P, HALF], F32, "y%d%d" % (half, u), at)
-            nc.vector.tensor_tensor(y_sb[:], wgo_sb[:, users], y[:], MULT)
-            nc.vector.tensor_copy(pages[u][:].indirect(slots), y_sb[:])
-            if half == HALVES - 1:
-                nc.sync.dma_start(out=out[u * P : (u + 1) * P, :], in_=pages[u][:])
+                banks[b, g][1] = done + 1
 
-        feedback(0, 0, 0)
-        feedback(0, 1, 0)
-        feedback(1, 0, 0)
-        close_tiles(0, 0)
-        feedback(1, 1, 0)
-        w1_mx.append(quantize("w1b", w1_grouped[1], at=SPARE))
-        c_mx[0, 1] = quantize("c01", c_grouped[0, 1], at=SLOT[0] + 4 * KIB)
-        pool_slope(PLANES - 2, 1, HALF, PAGE3 + 3 * KIB)
-        h00_grouped = interleave("h00", h_rows[0, 0][:], ROWS[1] + 4 * KIB)
-        close_tiles(1, 0)
-        h10_grouped = interleave("h10", h_rows[1, 0][:], XS[3])
-        feedback(0, 0, 1)
-        feedback(0, 1, 1)
-        c_mx[1, 1] = quantize("c11", c_grouped[1, 1], at=RESTART)
-        h_mx[0, 0] = quantize("h00", h00_grouped)
-        pool_slope(PLANES - 1, 1, HALF, ROWS[1] + 7 * KIB)
-        close_tiles(0, 1)
-        h_mx[1, 0] = quantize("h10", h10_grouped)
-        w2_low = cast_w2(0, XS[1])
-        close_tiles(1, 1, range(1))
+        def product(b, g, slope, grouped):
+            nc.vector.tensor_tensor(
+                grouped.rearrange("p (c i t) -> p c t i", i=2, t=PACK),
+                slope.rearrange("p t (c i) -> p c t i", i=2),
+                banks[b, g][0][:].rearrange("p t (c i) -> p c t i", i=2),
+                MULT,
+            )
+
+        for g in range(4):
+            open_bank(0, g, g)
+            passes(0, g, 0)
+        for g in range(4):
+            passes(0, g, 1)
+        for g in range(4):
+            open_bank(1, g, 4 + g)
+            passes(1, g, 0)
+        h00 = placed([P, HALF * PACK], BF16, "h00_g", CG01)
+        for g in range(4):
+            passes(0, g, "table")
+            product(0, g, slope0[:, :, g * P : (g + 1) * P], h00[:, g * PASS : (g + 1) * PASS])
+
+        w1_grouped.append(cast_w1(1, w1_raw[1], WG1B))
+        deal_wf(1, 1, SLOT[0] + 6 * KIB, nc.scalar.copy)
+        for g in range(4):
+            passes(1, g, 1)
+        for pair in range(2):
+            codes, scales = quantize("w1b%d" % pair, w1_grouped[1][:, pair * KIB : (pair + 1) * KIB], QUARTER)
+            for t in range(2):
+                w1_mx[1, 2 * pair + t] = (codes[:, t * P : (t + 1) * P], scales[:, t * P : (t + 1) * P])
+        h_mx = {}
+        h_mx[0, 0] = quantize("h00", h00[:], at=SLOT[0] + 8 * KIB + HALF)
+        w2_low = cast_w2(0, w2_raw[0], CG00)
+        c_grouped[0, 1] = interleave("c01", rows01[:], SLOT[1] + 4 * KIB)
+
+        w2_mx = {}
+        h10 = [placed([P, QUARTER * PACK], BF16, "h10_g%d" % q, CG10 + 2 * q * KIB) for q in range(2)]
+        h10_mx = {}
+
+        def close_second(g):
+            passes(1, g, "table")
+            product(1, g, slopes1[g], h10[g // 2][:, g % 2 * PASS : (g % 2 + 1) * PASS])
+
+        def second_stage(name, u, first, pieces, bank, at):
+            part, col = divmod(u * P, COLS)
+            width = sum(w for w, operands in pieces)
+            y = psum.tile([P, width], F32, name="y" + name, offset=bank * BANK)
+            lo = 0
+            for w, operands in pieces:
+                for b in range(BLOCKS):
+                    (codes, scales), start = operands[b]
+                    nc.tensor.matmul_mx(
+                        out=y[:, lo : lo + w],
+                        lhsT=w2_mx[part][0][:, b * COLS + col : b * COLS + col + P].bitcast(E4),
+                        lhsT_scale=w2_mx[part][1][:, b * COLS + col : b * COLS + col + P],
+                        rhs=codes[:, start : start + w].bitcast(E4),
+                        rhs_scale=scales[:, start : start + w],
+                        start=(b == 0),
+                        stop=(b == BLOCKS - 1),
+                    )
+                lo += w
+            y_sb = placed([P, width], F32, "y_sb" + name, at)
+            nc.scalar.activation(out=y_sb[:], in_=y[:], func=COPY, scale=-1.0)
+            slots = idx2[:, first // 16 : (first + width) // 16]
+            nc.vector.tensor_tensor(pages[u][:].indirect(slots), y_sb[:], wgo_sb[:, first : first + width], MULT)
+
+        def quarter(q):
+            return (QUARTER, [(h_mx[0, 0], q * QUARTER), (h10_mx[q], 0)])
+
+        close_second(0)
+        close_second(1)
         w2_mx[0] = quantize("w2_0", w2_low)
-        close_tiles(1, 1, range(1, PACK))
-        second_stage(0, 0, SPARE + 2 * KIB)
-        w2_mx[1] = quantize("w2_1", cast_w2(1, ROWS[1] + 8 * KIB))
-        second_stage(0, 1, BASE)
-        h_mx[0, 1] = quantize("h01", interleave("h01", h_rows[0, 1][:], ROWS[1] + 5 * KIB))
-        second_stage(0, 2, XS[0])
-        h_mx[1, 1] = quantize("h11", interleave("h11", h_rows[1, 1][:], ROWS[1] + 11 * KIB))
-        second_stage(0, 3, rows_at[1, 1])
+        h10_mx[0] = quantize("h10a", h10[0][:], QUARTER)
+        close_second(2)
+        close_second(3)
+        second_stage("00", 0, 0, [quarter(0)], 0, Y00)
+        h10_mx[1] = quantize("h10b", h10[1][:], QUARTER)
+        second_stage("01", 1, 0, [quarter(0)], 1, Y01)
+        second_stage("10", 0, QUARTER, [quarter(1)], 2, Y10)
+        w2_mx[1] = quantize("w2_1", cast_w2(1, w2_raw[1], W2HI))
+        second_stage("11", 1, QUARTER, [quarter(1)], 3, LAST_PLANE + 7 * KIB)
+        rows11 = placed([P, PACK, HALF], BF16, "rows11", ROWS11)
+        for t in range(PACK):
+            priced(rows11[:, t, :], xs[1][:, t, HALF:S], 1, t)
+        c_mx[0, 1] = quantize("c01", c_grouped[0, 1])
+        for g in range(4, 8):
+            open_bank(0, g, g)
+            passes(0, g, "table")
+            passes(0, g, 0)
+        c_mx[1, 1] = quantize("c11", interleave("c11", rows11[:], Y01))
+        second_stage("2", 2, 0, [quarter(0), quarter(1)], 0, ROWS11 + 3 * KIB)
+        less_late = placed([P, 3, PACK, P], F32, "less_late", Y01 + KIB)
+        for g in range(5, 8):
+            nc.scalar.activation(out=less_late[:, g - 5, :, :], in_=xs[1][:, :, g * P : (g + 1) * P], func=COPY, bias=-1.0)
+        for g in range(4, 8):
+            open_bank(1, g, (g - 3) % 4)
+            passes(1, g, "table")
+            passes(1, g, 0)
+        slope_late = placed([P, 3, PACK, P], F32, "slope_late", ROWS11 + 4 * KIB)
+        for g in range(5, 8):
+            nc.gpsimd.tensor_tensor(
+                slope_late[:, g - 5, :, :], less_late[:, g - 5, :, :], xs[1][:, :, g * P : (g + 1) * P], MULT
+            )
+        h01 = placed([P, HALF * PACK], BF16, "h01_g", TABLE)
+        h11 = placed([P, HALF * PACK], BF16, "h11_g", TABLE + 4 * KIB)
+        for g in range(4, 8):
+            passes(0, g, 1)
+            product(0, g, slope0[:, :, g * P : (g + 1) * P], h01[:, (g - 4) * PASS : (g - 3) * PASS])
+        for g in range(4, 8):
+            passes(1, g, 1)
+            slope = slopes1[4] if g == 4 else slope_late[:, g - 5, :, :]
+            product(1, g, slope, h11[:, (g - 4) * PASS : (g - 3) * PASS])
+        h_mx[0, 1] = quantize("h01", h01[:])
+        h_mx[1, 1] = quantize("h11", h11[:])
+        second_stage("3", 3, 0, [quarter(0), quarter(1)], 4, ROWS11 + 6 * KIB)
         for u in range(NT):
-            second_stage(1, u, SLOT[1] + u * 2 * KIB)
+            second_stage("l%d" % u, u, HALF, [(HALF, [(h_mx[0, 1], 0), (h_mx[1, 1], 0)])], (5, 6, 7, 1)[u], Y_LAST + u * 2 * KIB)
+            nc.sync.dma_start(out=out[u * P : (u + 1) * P, :], in_=pages[u][:])

@@ -32,13 +32,14 @@ BANK = 2048
 KIB = 1024
 SLOT = [0, 9 * KIB, 17 * KIB, 31 * KIB, 39 * KIB]
 LAST_PLANE = 22 * KIB
-TABLE = 43 * KIB
+W2LO = [13 * KIB, 23 * KIB]
+W2HI = [27 * KIB, 45 * KIB]
 ROWS01 = 51 * KIB
 ROWS00 = 56 * KIB + HALF
 ROWS10 = 76 * KIB
 ROWS11 = ROWS01
-CG00, CG01, CG10, WG1A, WG1B, WF0, W2HI = (k * KIB for k in (64, 68, 72, 106, 80, 84, 88))
-Y00, Y01, Y10, Y_LAST = (k * KIB for k in (91, 92, 96, 97))
+CG00, CG01, CG10, WG1A, WG1B, WF0 = (k * KIB for k in (64, 68, 72, 106, 80, 84))
+Y00, Y01, CG11, Y_LAST = (k * KIB for k in (91, 92, 93, 97))
 
 
 def tile_list_handover_gradient_kernel(
@@ -96,7 +97,7 @@ def tile_list_handover_gradient_kernel(
         def load_w2(part, at):
             raws = []
             for b in range(BLOCKS):
-                raw = placed([P, PACK, COLS], F32, "w2_raw%d%d" % (part, b), at + b * 4 * KIB)
+                raw = placed([P, PACK, COLS], F32, "w2_raw%d%d" % (part, b), at[b])
                 rows = w2[b * PASS : (b + 1) * PASS, part * COLS : (part + 1) * COLS]
                 nc.sync.dma_start(out=raw[:], in_=rows.rearrange("(p j) c -> p j c", j=PACK))
                 raws.append(raw)
@@ -113,7 +114,6 @@ def tile_list_handover_gradient_kernel(
 
         wf_raw = {}
         wf_w = {}
-        wf_s = {}
 
         def load_wf(a, b, at):
             wf_raw[a, b] = placed([P, PASS], I32, "wf_raw%d%d" % (a, b), at)
@@ -127,12 +127,6 @@ def tile_list_handover_gradient_kernel(
                 in_=wf_raw[a, b][:].bitcast(U32).rearrange("p (c i t) -> p c t i", t=PACK, i=4),
             )
 
-        def deal_scales(b, at=None):
-            wf_s[b] = placed([P, PASS], U8, "wf_s%d" % b, at)
-            nc.vector.tensor_copy(
-                out=wf_s[b][:].rearrange("p (t m) -> p t m", t=PACK),
-                in_=wf_s_raw[:, b * PASS : (b + 1) * PASS].rearrange("p (m t) -> p t m", t=PACK),
-            )
 
         s_rows = sT.rearrange("(b p t) n -> b t p n", p=P, t=PACK)
 
@@ -140,6 +134,8 @@ def tile_list_handover_gradient_kernel(
         pages = [placed([P, T2], F32, "page%d" % u) for u in range(NT)]
         nc.vector.memset(tab_s[32:64, :].bitcast(I32), 0)
         nc.vector.memset(tab_s[64:P, :].bitcast(I32), 0)
+        wf_s_raw = placed([P, PASS + 4], U8, "wf_s_raw")
+        nc.vector.memset(wf_s_raw[:].bitcast(I32), 0)
         for page in pages:
             nc.gpsimd.memset(page[:], 0.0)
 
@@ -156,7 +152,6 @@ def tile_list_handover_gradient_kernel(
         less10 = placed([P, PACK, 3 * P], F32, "less10")
         rows00 = placed([P, PACK, HALF], BF16, "rows00", ROWS00)
         rows01 = placed([P, PACK, HALF], BF16, "rows01", ROWS01)
-        wf_s_raw = placed([P, H], U8, "wf_s_raw")
         rows10 = placed([P, PACK, HALF], BF16, "rows10", ROWS10)
 
         def priced(dst, src, b, t):
@@ -168,7 +163,6 @@ def tile_list_handover_gradient_kernel(
             nc.vector.scalar_tensor_tensor(out=slope[:], in0=x, scalar=1.0, in1=x, op0=SUB, op1=MULT)
             return slope[:]
 
-        nc.gpsimd.memset(wf_s_raw[:].bitcast(I32), 0)
         c_grouped = {}
         for k in range(PLANES):
             b, t = divmod(k, PACK)
@@ -176,6 +170,13 @@ def tile_list_handover_gradient_kernel(
             nc.sync.dma_start(out=plane[:], in_=s_rows[b, t])
             if k == 0:
                 nc.sync.dma_start(out=price_sb[:], in_=price.rearrange("(b p t) -> p b t", p=P, t=PACK))
+            if 1 <= k <= 4:
+                for block in range(BLOCKS):
+                    row = 32 * (k - 1) + 8 * block
+                    nc.sync.dma_start(
+                        out=wf_s_raw[row : row + 8, 0:PASS].bitcast(I32),
+                        in_=wf_scales[:, 4 * (k - 1) : 4 * k, block * PASS : (block + 1) * PASS].bitcast(I32),
+                    )
             x = xs[b][:, t, :]
             if k < PLANES - 1:
                 nc.vector.tensor_copy(x, plane[:].indirect(idx[:]))
@@ -189,7 +190,7 @@ def tile_list_handover_gradient_kernel(
             elif k == PACK - 1:
                 nc.gpsimd.tensor_scalar(slope0[:, t, :], x, 1.0, -1.0, MULT, ADD)
                 nc.gpsimd.tensor_tensor(slope0[:, t, :], slope0[:, t, :], x, MULT)
-            elif k < PLANES - 1:
+            else:
                 nc.gpsimd.tensor_scalar(less10[:, t, :], x[:, 0 : 3 * P], 1.0, -1.0, MULT, ADD)
             priced((rows00, rows10)[b][:, t, :], x[:, 0:HALF], b, t)
             if b == 0:
@@ -198,54 +199,53 @@ def tile_list_handover_gradient_kernel(
                 c_grouped[0, 0] = interleave("c00", rows00[:], CG00)
 
         load_wf(0, 0, SLOT[2] + KIB)
-        for q in range(4):
-            nc.sync.dma_start(
-                out=wf_s_raw[32 * q : 32 * q + 4 * BLOCKS, :].bitcast(I32),
-                in_=wf_scales.bitcast(I32)[:, 4 * q : 4 * q + 4, :],
-            )
         load_wf(1, 0, SLOT[2] + 3 * KIB)
-        w1_raw = [load_w1(0, SLOT[3], 1)]
-        load_wf(0, 1, SLOT[4])
-        tab_w = placed([P, T], I32, "tab_w", TABLE)
+        tab_w = placed([P, T], I32, "tab_w", SLOT[3])
         nc.sync.dma_start(out=tab_w[:], in_=tab_words[0].rearrange("p n t -> p (n t)").bitcast(I32))
-        load_wf(1, 1, SLOT[4] + 2 * KIB)
+        w1_raw = [load_w1(0, SLOT[4], 2)]
         v_s = placed([P, S], U8, "v_s", SLOT[0])
         for q in range(4):
             nc.sync.dma_start(
                 out=v_s[32 * q : 32 * q + 4, :].bitcast(I32), in_=v_s_raw[4 * q : 4 * q + 4, :].bitcast(I32)
             )
         w1_raw.append(load_w1(1, SLOT[0] + KIB, 2))
-        w2_raw = [load_w2(0, SLOT[1])]
+        load_wf(0, 1, SLOT[1])
+        load_wf(1, 1, SLOT[1] + 2 * KIB)
+        w2_raw = [load_w2(0, W2LO)]
         nc.sync.dma_start(idx2[:], offs2)
 
         deal_wf(0, 0, WF0)
-        deal_scales(0, LAST_PLANE)
+        wf_s = placed([P, PASS], U8, "wf_s", LAST_PLANE)
+        nc.vector.tensor_copy(
+            out=wf_s[:].rearrange("p (t m) -> p t m", t=PACK), in_=wf_s_raw[:, 0:PASS].rearrange("p (m t) -> p t m", t=PACK)
+        )
         c_mx = {}
         c_mx[0, 0] = quantize("c00", c_grouped[0, 0], at=LAST_PLANE + HALF)
         deal_wf(1, 0, WF0 + 2 * KIB)
-        deal_scales(1, SLOT[2] + 2 * KIB)
-        wgo_sb = placed([P, S], F32, "wgo_sb", SLOT[3])
+        wgo_sb = placed([P, S], F32, "wgo_sb", SLOT[4])
         nc.sync.dma_start(out=wgo_sb[:], in_=wgo)
-        w2_raw.append(load_w2(1, LAST_PLANE + KIB))
+        w2_raw.append(load_w2(1, W2HI))
 
         c_grouped[1, 0] = interleave("c10", rows10[:], CG10)
         w1_grouped = [cast_w1(0, w1_raw[0], WG1A)]
-        nc.scalar.activation(out=less10[:, PACK - 1, :], in_=xs[1][:, PACK - 1, 0 : 3 * P], func=COPY, bias=-1.0)
+        slopes1 = {3: vector_slope(3, SLOT[2]), 4: vector_slope(4, SLOT[2] + 2 * KIB)}
         c_mx[1, 0] = quantize("c10", c_grouped[1, 0])
-        deal_wf(0, 1, ROWS10 + 2 * KIB)
-        slopes1 = {3: vector_slope(3, SLOT[2]), 4: vector_slope(4, ROWS10)}
-        codes, scales = quantize("w1a", w1_grouped[0])
-        w1_mx = {(0, t): (codes[:, t * P : (t + 1) * P], scales[:, t * P : (t + 1) * P]) for t in range(PACK)}
-        v_w = []
-        for half in range(2):
-            v_w.append(placed([P, HALF], U32, "v_w%d" % half, SLOT[3] + (4 + 2 * half) * KIB))
+        v_w = {}
+
+        def gather_table(half, at):
+            v_w[half] = placed([P, HALF], U32, "v_w%d" % half, at)
             picks = idx[:, half * HALF // 16 : (half + 1) * HALF // 16]
             nc.vector.tensor_copy(v_w[half][:], tab_w[:].bitcast(U32).indirect(picks))
-        slope10 = placed([P, 3, PACK, P], F32, "slope10", WG1A - KIB)
-        for g in range(3):
+
+        gather_table(0, ROWS10 + 2 * KIB)
+        codes, scales = quantize("w1a", w1_grouped[0])
+        w1_mx = {(0, t): (codes[:, t * P : (t + 1) * P], scales[:, t * P : (t + 1) * P]) for t in range(PACK)}
+        gather_table(1, SLOT[4] + 4 * KIB)
+        for g, at in enumerate((CG10 + 2 * KIB, WG1A, WG1A + 2 * KIB)):
             cols = slice(g * P, (g + 1) * P)
-            nc.gpsimd.tensor_tensor(slope10[:, g, :, :], less10[:, :, cols], xs[1][:, :, cols], MULT)
-            slopes1[g] = slope10[:, g, :, :]
+            slope = placed([P, PACK, P], F32, "slope1%d" % g, at)
+            nc.gpsimd.tensor_tensor(slope[:], less10[:, :, cols], xs[1][:, :, cols], MULT)
+            slopes1[g] = slope[:]
 
         banks = {}
 
@@ -263,7 +263,7 @@ def tile_list_handover_gradient_kernel(
                     rhs_scale = v_s[:, g * P : (g + 1) * P]
                 else:
                     lhs = wf_w[kind, b][:, t * P : (t + 1) * P].bitcast(E4)
-                    lhs_scale = wf_s[b][4 * kind : P, t * P : (t + 1) * P]
+                    lhs_scale = wf_s[8 * b + 4 * kind : P, t * P : (t + 1) * P]
                     rhs = c_mx[kind, half][0][:, first : first + P].bitcast(E4)
                     rhs_scale = c_mx[kind, half][1][:, first : first + P]
                 nc.tensor.matmul_mx(
@@ -285,16 +285,17 @@ def tile_list_handover_gradient_kernel(
             passes(0, g, 0)
         for g in range(4):
             passes(0, g, 1)
-        for g in range(4):
-            open_bank(1, g, 4 + g)
-            passes(1, g, 0)
         h00 = placed([P, HALF * PACK], BF16, "h00_g", CG01)
         for g in range(4):
             passes(0, g, "table")
             product(0, g, slope0[:, :, g * P : (g + 1) * P], h00[:, g * PASS : (g + 1) * PASS])
 
         w1_grouped.append(cast_w1(1, w1_raw[1], WG1B))
+        deal_wf(0, 1, SLOT[0] + 4 * KIB, nc.scalar.copy)
         deal_wf(1, 1, SLOT[0] + 6 * KIB, nc.scalar.copy)
+        for g in range(4):
+            open_bank(1, g, 4 + g)
+            passes(1, g, 0)
         for g in range(4):
             passes(1, g, 1)
         for pair in range(2):
@@ -304,7 +305,7 @@ def tile_list_handover_gradient_kernel(
         h_mx = {}
         h_mx[0, 0] = quantize("h00", h00[:], at=SLOT[0] + 8 * KIB + HALF)
         w2_low = cast_w2(0, w2_raw[0], CG00)
-        c_grouped[0, 1] = interleave("c01", rows01[:], SLOT[1] + 4 * KIB)
+        c_grouped[0, 1] = interleave("c01", rows01[:], W2LO[1])
 
         w2_mx = {}
         h10 = [placed([P, QUARTER * PACK], BF16, "h10_g%d" % q, CG10 + 2 * q * KIB) for q in range(2)]
@@ -349,43 +350,39 @@ def tile_list_handover_gradient_kernel(
         second_stage("00", 0, 0, [quarter(0)], 0, Y00)
         h10_mx[1] = quantize("h10b", h10[1][:], QUARTER)
         second_stage("01", 1, 0, [quarter(0)], 1, Y01)
-        second_stage("10", 0, QUARTER, [quarter(1)], 2, Y10)
-        w2_mx[1] = quantize("w2_1", cast_w2(1, w2_raw[1], W2HI))
-        second_stage("11", 1, QUARTER, [quarter(1)], 3, LAST_PLANE + 7 * KIB)
         rows11 = placed([P, PACK, HALF], BF16, "rows11", ROWS11)
         for t in range(PACK):
             priced(rows11[:, t, :], xs[1][:, t, HALF:S], 1, t)
         c_mx[0, 1] = quantize("c01", c_grouped[0, 1])
-        for g in range(4, 8):
-            open_bank(0, g, g)
-            passes(0, g, "table")
-            passes(0, g, 0)
-        c_mx[1, 1] = quantize("c11", interleave("c11", rows11[:], Y01))
-        second_stage("2", 2, 0, [quarter(0), quarter(1)], 0, ROWS11 + 3 * KIB)
-        less_late = placed([P, 3, PACK, P], F32, "less_late", Y01 + KIB)
+        c_mx[1, 1] = quantize("c11", interleave("c11", rows11[:], CG11))
+        second_stage("10", 0, QUARTER, [quarter(1)], 2, ROWS11)
+        second_stage("11", 1, QUARTER, [quarter(1)], 3, ROWS11 + 2 * KIB)
+        less_late = placed([P, 3, PACK, P], F32, "less_late", CG11 - 4 * KIB)
         for g in range(5, 8):
             nc.scalar.activation(out=less_late[:, g - 5, :, :], in_=xs[1][:, :, g * P : (g + 1) * P], func=COPY, bias=-1.0)
-        for g in range(4, 8):
-            open_bank(1, g, (g - 3) % 4)
-            passes(1, g, "table")
-            passes(1, g, 0)
-        slope_late = placed([P, 3, PACK, P], F32, "slope_late", ROWS11 + 4 * KIB)
+        w2_high = cast_w2(1, w2_raw[1], CG11 + 2 * KIB)
+        for b in range(BLOCKS):
+            for g in range(4, 8):
+                open_bank(b, g, g - 4 * b)
+                for kind in ("table", 0, 1):
+                    passes(b, g, kind)
+        slope5 = placed([P, PACK, P], F32, "slope5", ROWS11 + HALF)
+        slope67 = placed([P, 2, PACK, P], F32, "slope67", ROWS11 + 5 * HALF)
+        slopes1.update({5: slope5[:], 6: slope67[:, 0, :, :], 7: slope67[:, 1, :, :]})
         for g in range(5, 8):
-            nc.gpsimd.tensor_tensor(
-                slope_late[:, g - 5, :, :], less_late[:, g - 5, :, :], xs[1][:, :, g * P : (g + 1) * P], MULT
-            )
-        h01 = placed([P, HALF * PACK], BF16, "h01_g", TABLE)
-        h11 = placed([P, HALF * PACK], BF16, "h11_g", TABLE + 4 * KIB)
+            nc.gpsimd.tensor_tensor(slopes1[g], less_late[:, g - 5, :, :], xs[1][:, :, g * P : (g + 1) * P], MULT)
+        h01 = placed([P, HALF * PACK], BF16, "h01_g", SLOT[3])
+        h11 = placed([P, HALF * PACK], BF16, "h11_g", CG01)
         for g in range(4, 8):
-            passes(0, g, 1)
             product(0, g, slope0[:, :, g * P : (g + 1) * P], h01[:, (g - 4) * PASS : (g - 3) * PASS])
         for g in range(4, 8):
-            passes(1, g, 1)
-            slope = slopes1[4] if g == 4 else slope_late[:, g - 5, :, :]
-            product(1, g, slope, h11[:, (g - 4) * PASS : (g - 3) * PASS])
-        h_mx[0, 1] = quantize("h01", h01[:])
+            if g == 7:
+                w2_mx[1] = quantize("w2_1", w2_high, at=ROWS11 + KIB)
+            product(1, g, slopes1[g], h11[:, (g - 4) * PASS : (g - 3) * PASS])
+        h_mx[0, 1] = quantize("h01", h01[:], at=ROWS11 + 3 * HALF)
         h_mx[1, 1] = quantize("h11", h11[:])
-        second_stage("3", 3, 0, [quarter(0), quarter(1)], 4, ROWS11 + 6 * KIB)
+        for u in (2, 3):
+            second_stage("0_%d" % u, u, 0, [quarter(0), quarter(1)], 2 + u, ROWS00 + (2 * u - 3) * KIB)
         for u in range(NT):
-            second_stage("l%d" % u, u, HALF, [(HALF, [(h_mx[0, 1], 0), (h_mx[1, 1], 0)])], (5, 6, 7, 1)[u], Y_LAST + u * 2 * KIB)
+            second_stage("l%d" % u, u, HALF, [(HALF, [(h_mx[0, 1], 0), (h_mx[1, 1], 0)])], (6, 7, 0, 1)[u], Y_LAST + u * 2 * KIB)
             nc.sync.dma_start(out=out[u * P : (u + 1) * P, :], in_=pages[u][:])

@@ -28,17 +28,20 @@ PLANES = BLOCKS * PACK
 NT = N // P
 COLS = N // 2
 BANK = 2048
+WARM_UPS = 5
 
 KIB = 1024
 SLOT = [0, 9 * KIB, 17 * KIB, 31 * KIB, 39 * KIB]
-LAST_PLANE = 22 * KIB
-W2LO = [13 * KIB, 23 * KIB]
-W2HI = [27 * KIB, 45 * KIB]
+LAST_PLANE = 21 * KIB
+TABLE = 33 * KIB
+W1A = 41 * KIB
+W2LO = [11 * KIB, 15 * KIB]
+W2HI = [37 * KIB, 47 * KIB]
 ROWS01 = 51 * KIB
 ROWS00 = 56 * KIB + HALF
 ROWS10 = 76 * KIB
-ROWS11 = ROWS01
-CG00, CG01, CG10, WG1A, WG1B, WF0 = (k * KIB for k in (64, 68, 72, 106, 80, 84))
+ROWS11 = 13 * KIB
+CG00, CG01, CG10, WG1A, WG1B = (k * KIB for k in (64, 68, 72, 106, 80))
 Y00, Y01, CG11, Y_LAST = (k * KIB for k in (91, 92, 93, 97))
 
 
@@ -197,38 +200,48 @@ def tile_list_handover_gradient_kernel(
                 priced(rows01[:, t, :], x[:, HALF:S], b, t)
             if k == PACK - 1:
                 c_grouped[0, 0] = interleave("c00", rows00[:], CG00)
+            if k == PACK + 1:
+                c_grouped[0, 1] = interleave("c01", rows01[:], 84 * KIB)
 
-        load_wf(0, 0, SLOT[2] + KIB)
-        load_wf(1, 0, SLOT[2] + 3 * KIB)
-        tab_w = placed([P, T], I32, "tab_w", SLOT[3])
+        load_wf(0, 0, SLOT[2])
+        load_wf(1, 0, SLOT[2] + 2 * KIB)
+        load_wf(0, 1, SLOT[3])
+        tab_w = placed([P, T], I32, "tab_w", TABLE)
         nc.sync.dma_start(out=tab_w[:], in_=tab_words[0].rearrange("p n t -> p (n t)").bitcast(I32))
-        w1_raw = [load_w1(0, SLOT[4], 2)]
+        w1_raw = [load_w1(0, W1A, 2)]
         v_s = placed([P, S], U8, "v_s", SLOT[0])
         for q in range(4):
             nc.sync.dma_start(
                 out=v_s[32 * q : 32 * q + 4, :].bitcast(I32), in_=v_s_raw[4 * q : 4 * q + 4, :].bitcast(I32)
             )
         w1_raw.append(load_w1(1, SLOT[0] + KIB, 2))
-        load_wf(0, 1, SLOT[1])
-        load_wf(1, 1, SLOT[1] + 2 * KIB)
+        load_wf(1, 1, SLOT[1])
         w2_raw = [load_w2(0, W2LO)]
         nc.sync.dma_start(idx2[:], offs2)
 
-        deal_wf(0, 0, WF0)
+        warm = psum.tile([P, PASS], F32, name="warm", offset=7 * BANK)
+        for step in range(WARM_UPS):
+            nc.tensor.matmul_mx(
+                out=warm[:], lhsT=wf_raw[1, 0][:, 0:P].bitcast(E4), lhsT_scale=wf_s_raw[:, 0:P],
+                rhs=wf_raw[1, 0][:].bitcast(E4), rhs_scale=wf_s_raw[:, 0:PASS], start=True, stop=True,
+            )
+        deal_wf(0, 0, LAST_PLANE + KIB)
         wf_s = placed([P, PASS], U8, "wf_s", LAST_PLANE)
         nc.vector.tensor_copy(
             out=wf_s[:].rearrange("p (t m) -> p t m", t=PACK), in_=wf_s_raw[:, 0:PASS].rearrange("p (m t) -> p t m", t=PACK)
         )
         c_mx = {}
         c_mx[0, 0] = quantize("c00", c_grouped[0, 0], at=LAST_PLANE + HALF)
-        deal_wf(1, 0, WF0 + 2 * KIB)
-        wgo_sb = placed([P, S], F32, "wgo_sb", SLOT[4])
+        deal_wf(1, 0, LAST_PLANE + 3 * KIB)
+        deal_wf(0, 1, LAST_PLANE + 5 * KIB)
+        wgo_sb = placed([P, S], F32, "wgo_sb", W1A)
         nc.sync.dma_start(out=wgo_sb[:], in_=wgo)
         w2_raw.append(load_w2(1, W2HI))
 
         c_grouped[1, 0] = interleave("c10", rows10[:], CG10)
         w1_grouped = [cast_w1(0, w1_raw[0], WG1A)]
-        slopes1 = {3: vector_slope(3, SLOT[2]), 4: vector_slope(4, SLOT[2] + 2 * KIB)}
+        slopes1 = {3: vector_slope(3, LAST_PLANE + 7 * KIB)}
+        c_mx[0, 1] = quantize("c01", c_grouped[0, 1], at=SLOT[2] + 2 * KIB)
         c_mx[1, 0] = quantize("c10", c_grouped[1, 0])
         v_w = {}
 
@@ -240,7 +253,7 @@ def tile_list_handover_gradient_kernel(
         gather_table(0, ROWS10 + 2 * KIB)
         codes, scales = quantize("w1a", w1_grouped[0])
         w1_mx = {(0, t): (codes[:, t * P : (t + 1) * P], scales[:, t * P : (t + 1) * P]) for t in range(PACK)}
-        gather_table(1, SLOT[4] + 4 * KIB)
+        gather_table(1, W1A + 4 * KIB)
         for g, at in enumerate((CG10 + 2 * KIB, WG1A, WG1A + 2 * KIB)):
             cols = slice(g * P, (g + 1) * P)
             slope = placed([P, PACK, P], F32, "slope1%d" % g, at)
@@ -272,11 +285,11 @@ def tile_list_handover_gradient_kernel(
                 )
                 banks[b, g][1] = done + 1
 
-        def product(b, g, slope, grouped):
+        def product(b, g, slope, grouped, cols=slice(0, P)):
             nc.vector.tensor_tensor(
                 grouped.rearrange("p (c i t) -> p c t i", i=2, t=PACK),
                 slope.rearrange("p t (c i) -> p c t i", i=2),
-                banks[b, g][0][:].rearrange("p t (c i) -> p c t i", i=2),
+                banks[b, g][0][:, :, cols].rearrange("p t (c i) -> p c t i", i=2),
                 MULT,
             )
 
@@ -285,17 +298,16 @@ def tile_list_handover_gradient_kernel(
             passes(0, g, 0)
         for g in range(4):
             passes(0, g, 1)
+        for g in range(4):
+            open_bank(1, g, 4 + g)
+            passes(1, g, 0)
         h00 = placed([P, HALF * PACK], BF16, "h00_g", CG01)
         for g in range(4):
             passes(0, g, "table")
             product(0, g, slope0[:, :, g * P : (g + 1) * P], h00[:, g * PASS : (g + 1) * PASS])
 
         w1_grouped.append(cast_w1(1, w1_raw[1], WG1B))
-        deal_wf(0, 1, SLOT[0] + 4 * KIB, nc.scalar.copy)
         deal_wf(1, 1, SLOT[0] + 6 * KIB, nc.scalar.copy)
-        for g in range(4):
-            open_bank(1, g, 4 + g)
-            passes(1, g, 0)
         for g in range(4):
             passes(1, g, 1)
         for pair in range(2):
@@ -305,7 +317,16 @@ def tile_list_handover_gradient_kernel(
         h_mx = {}
         h_mx[0, 0] = quantize("h00", h00[:], at=SLOT[0] + 8 * KIB + HALF)
         w2_low = cast_w2(0, w2_raw[0], CG00)
-        c_grouped[0, 1] = interleave("c01", rows01[:], W2LO[1])
+        less4 = placed([P, PACK, P], F32, "less4", W2LO[1] + 2 * KIB)
+        nc.scalar.activation(out=less4[:], in_=xs[1][:, :, HALF : HALF + P], func=COPY, bias=-1.0)
+        slope4 = []
+
+        def pool_slope4(part, at):
+            slope4.append(placed([P, PACK, P // 2], F32, "slope4%d" % part, at))
+            cols = slice(part * P // 2, (part + 1) * P // 2)
+            nc.gpsimd.tensor_tensor(slope4[part][:], less4[:, :, cols], xs[1][:, :, HALF : HALF + P][:, :, cols], MULT)
+
+        pool_slope4(0, CG01)
 
         w2_mx = {}
         h10 = [placed([P, QUARTER * PACK], BF16, "h10_g%d" % q, CG10 + 2 * q * KIB) for q in range(2)]
@@ -345,6 +366,7 @@ def tile_list_handover_gradient_kernel(
         close_second(1)
         w2_mx[0] = quantize("w2_0", w2_low)
         h10_mx[0] = quantize("h10a", h10[0][:], QUARTER)
+        pool_slope4(1, CG10)
         close_second(2)
         close_second(3)
         second_stage("00", 0, 0, [quarter(0)], 0, Y00)
@@ -353,7 +375,6 @@ def tile_list_handover_gradient_kernel(
         rows11 = placed([P, PACK, HALF], BF16, "rows11", ROWS11)
         for t in range(PACK):
             priced(rows11[:, t, :], xs[1][:, t, HALF:S], 1, t)
-        c_mx[0, 1] = quantize("c01", c_grouped[0, 1])
         c_mx[1, 1] = quantize("c11", interleave("c11", rows11[:], CG11))
         second_stage("10", 0, QUARTER, [quarter(1)], 2, ROWS11)
         second_stage("11", 1, QUARTER, [quarter(1)], 3, ROWS11 + 2 * KIB)
@@ -366,23 +387,27 @@ def tile_list_handover_gradient_kernel(
                 open_bank(b, g, g - 4 * b)
                 for kind in ("table", 0, 1):
                     passes(b, g, kind)
-        slope5 = placed([P, PACK, P], F32, "slope5", ROWS11 + HALF)
-        slope67 = placed([P, 2, PACK, P], F32, "slope67", ROWS11 + 5 * HALF)
+        slope5 = placed([P, PACK, P], F32, "slope5", ROWS11 + 5 * HALF)
+        slope67 = placed([P, 2, PACK, P], F32, "slope67", ROWS11 - 3 * HALF)
         slopes1.update({5: slope5[:], 6: slope67[:, 0, :, :], 7: slope67[:, 1, :, :]})
         for g in range(5, 8):
             nc.gpsimd.tensor_tensor(slopes1[g], less_late[:, g - 5, :, :], xs[1][:, :, g * P : (g + 1) * P], MULT)
-        h01 = placed([P, HALF * PACK], BF16, "h01_g", SLOT[3])
-        h11 = placed([P, HALF * PACK], BF16, "h11_g", CG01)
+        h01 = placed([P, HALF * PACK], BF16, "h01_g", TABLE)
+        h11 = placed([P, HALF * PACK], BF16, "h11_g", 84 * KIB)
         for g in range(4, 8):
             product(0, g, slope0[:, :, g * P : (g + 1) * P], h01[:, (g - 4) * PASS : (g - 3) * PASS])
-        for g in range(4, 8):
+        for part in range(2):
+            cols = slice(part * P // 2, (part + 1) * P // 2)
+            product(1, 4, slope4[part][:], h11[:, part * QUARTER : (part + 1) * QUARTER], cols)
+        for g in range(5, 8):
             if g == 7:
-                w2_mx[1] = quantize("w2_1", w2_high, at=ROWS11 + KIB)
+                w2_mx[1] = quantize("w2_1", w2_high, at=ROWS11 + 3 * KIB)
             product(1, g, slopes1[g], h11[:, (g - 4) * PASS : (g - 3) * PASS])
-        h_mx[0, 1] = quantize("h01", h01[:], at=ROWS11 + 3 * HALF)
+        h_mx[0, 1] = quantize("h01", h01[:], at=ROWS11 + 7 * HALF)
         h_mx[1, 1] = quantize("h11", h11[:])
-        for u in (2, 3):
-            second_stage("0_%d" % u, u, 0, [quarter(0), quarter(1)], 2 + u, ROWS00 + (2 * u - 3) * KIB)
+        for q in range(2):
+            second_stage("2%d" % q, 2, q * QUARTER, [quarter(q)], 4 + q, ROWS00 + (1 + q) * KIB)
+        second_stage("3", 3, 0, [quarter(0), quarter(1)], 6, ROWS00 + 3 * KIB)
         for u in range(NT):
-            second_stage("l%d" % u, u, HALF, [(HALF, [(h_mx[0, 1], 0), (h_mx[1, 1], 0)])], (6, 7, 0, 1)[u], Y_LAST + u * 2 * KIB)
+            second_stage("l%d" % u, u, HALF, [(HALF, [(h_mx[0, 1], 0), (h_mx[1, 1], 0)])], (7, 0, 1, 2)[u], Y_LAST + u * 2 * KIB)
             nc.sync.dma_start(out=out[u * P : (u + 1) * P, :], in_=pages[u][:])

@@ -28,7 +28,6 @@ PLANES = BLOCKS * PACK
 NT = N // P
 COLS = N // 2
 BANK = 2048
-WARM_UPS = 5
 
 KIB = 1024
 SLOT = [0, 9 * KIB, 17 * KIB, 31 * KIB, 39 * KIB]
@@ -219,12 +218,6 @@ def tile_list_handover_gradient_kernel(
         w2_raw = [load_w2(0, W2LO)]
         nc.sync.dma_start(idx2[:], offs2)
 
-        warm = psum.tile([P, PASS], F32, name="warm", offset=7 * BANK)
-        for step in range(WARM_UPS):
-            nc.tensor.matmul_mx(
-                out=warm[:], lhsT=wf_raw[1, 0][:, 0:P].bitcast(E4), lhsT_scale=wf_s_raw[:, 0:P],
-                rhs=wf_raw[1, 0][:].bitcast(E4), rhs_scale=wf_s_raw[:, 0:PASS], start=True, stop=True,
-            )
         deal_wf(0, 0, LAST_PLANE + KIB)
         wf_s = placed([P, PASS], U8, "wf_s", LAST_PLANE)
         nc.vector.tensor_copy(

@@ -32,10 +32,11 @@ BANK = 2048
 KIB = 1024
 SLOT = [0, 9 * KIB, 17 * KIB, 31 * KIB, 39 * KIB]
 LAST_PLANE = 21 * KIB
-TABLE = 33 * KIB
-W1A = 41 * KIB
+TABLE = 43 * KIB
+W1A = 31 * KIB
+WF1 = 39 * KIB
 W2LO = [11 * KIB, 15 * KIB]
-W2HI = [37 * KIB, 47 * KIB]
+W2HI = [43 * KIB, 47 * KIB]
 ROWS01 = 51 * KIB
 ROWS00 = 56 * KIB + HALF
 ROWS10 = 76 * KIB
@@ -117,16 +118,15 @@ def tile_list_handover_gradient_kernel(
         wf_raw = {}
         wf_w = {}
 
-        def load_wf(a, b, at):
-            wf_raw[a, b] = placed([P, PASS], I32, "wf_raw%d%d" % (a, b), at)
-            words = wf_words[a].rearrange("p n t -> p (n t)").bitcast(I32)
-            nc.sync.dma_start(out=wf_raw[a, b][:], in_=words[:, b * PASS : (b + 1) * PASS])
+        def load_wf(a, at):
+            wf_raw[a] = placed([P, H], I32, "wf_raw%d" % a, at)
+            nc.sync.dma_start(out=wf_raw[a][:], in_=wf_words[a].rearrange("p n t -> p (n t)").bitcast(I32))
 
         def deal_wf(a, b, at, copy=nc.vector.tensor_copy):
             wf_w[a, b] = placed([P, PASS], U32, "wf_w%d%d" % (a, b), at)
             copy(
                 out=wf_w[a, b][:].rearrange("p (t c i) -> p c t i", t=PACK, i=4),
-                in_=wf_raw[a, b][:].bitcast(U32).rearrange("p (c i t) -> p c t i", t=PACK, i=4),
+                in_=wf_raw[a][:, b * PASS : (b + 1) * PASS].bitcast(U32).rearrange("p (c i t) -> p c t i", t=PACK, i=4),
             )
 
 
@@ -202,19 +202,17 @@ def tile_list_handover_gradient_kernel(
             if k == PACK + 1:
                 c_grouped[0, 1] = interleave("c01", rows01[:], 84 * KIB)
 
-        load_wf(0, 0, SLOT[2])
-        load_wf(1, 0, SLOT[2] + 2 * KIB)
-        load_wf(0, 1, SLOT[3])
+        load_wf(0, SLOT[2])
+        w1_raw = [load_w1(0, W1A, 1)]
+        load_wf(1, WF1)
         tab_w = placed([P, T], I32, "tab_w", TABLE)
         nc.sync.dma_start(out=tab_w[:], in_=tab_words[0].rearrange("p n t -> p (n t)").bitcast(I32))
-        w1_raw = [load_w1(0, W1A, 2)]
         v_s = placed([P, S], U8, "v_s", SLOT[0])
         for q in range(4):
             nc.sync.dma_start(
                 out=v_s[32 * q : 32 * q + 4, :].bitcast(I32), in_=v_s_raw[4 * q : 4 * q + 4, :].bitcast(I32)
             )
         w1_raw.append(load_w1(1, SLOT[0] + KIB, 2))
-        load_wf(1, 1, SLOT[1])
         w2_raw = [load_w2(0, W2LO)]
         nc.sync.dma_start(idx2[:], offs2)
 
@@ -225,16 +223,16 @@ def tile_list_handover_gradient_kernel(
         )
         c_mx = {}
         c_mx[0, 0] = quantize("c00", c_grouped[0, 0], at=LAST_PLANE + HALF)
-        deal_wf(1, 0, LAST_PLANE + 3 * KIB)
         deal_wf(0, 1, LAST_PLANE + 5 * KIB)
-        wgo_sb = placed([P, S], F32, "wgo_sb", W1A)
+        wgo_sb = placed([P, S], F32, "wgo_sb", W1A + 4 * KIB)
         nc.sync.dma_start(out=wgo_sb[:], in_=wgo)
         w2_raw.append(load_w2(1, W2HI))
 
         c_grouped[1, 0] = interleave("c10", rows10[:], CG10)
         w1_grouped = [cast_w1(0, w1_raw[0], WG1A)]
-        slopes1 = {3: vector_slope(3, LAST_PLANE + 7 * KIB)}
+        slopes1 = {3: vector_slope(3, LAST_PLANE + 7 * KIB), 4: vector_slope(4, None)}
         c_mx[0, 1] = quantize("c01", c_grouped[0, 1], at=SLOT[2] + 2 * KIB)
+        deal_wf(1, 0, LAST_PLANE + 3 * KIB)
         c_mx[1, 0] = quantize("c10", c_grouped[1, 0])
         v_w = {}
 
@@ -243,11 +241,11 @@ def tile_list_handover_gradient_kernel(
             picks = idx[:, half * HALF // 16 : (half + 1) * HALF // 16]
             nc.vector.tensor_copy(v_w[half][:], tab_w[:].bitcast(U32).indirect(picks))
 
-        gather_table(0, ROWS10 + 2 * KIB)
         codes, scales = quantize("w1a", w1_grouped[0])
         w1_mx = {(0, t): (codes[:, t * P : (t + 1) * P], scales[:, t * P : (t + 1) * P]) for t in range(PACK)}
-        gather_table(1, W1A + 4 * KIB)
-        for g, at in enumerate((CG10 + 2 * KIB, WG1A, WG1A + 2 * KIB)):
+        gather_table(0, W1A)
+        gather_table(1, W1A + 2 * KIB)
+        for g, at in enumerate((WG1A - KIB, WG1A + KIB, WG1A + 3 * KIB)):
             cols = slice(g * P, (g + 1) * P)
             slope = placed([P, PACK, P], F32, "slope1%d" % g, at)
             nc.gpsimd.tensor_tensor(slope[:], less10[:, :, cols], xs[1][:, :, cols], MULT)
@@ -278,11 +276,11 @@ def tile_list_handover_gradient_kernel(
                 )
                 banks[b, g][1] = done + 1
 
-        def product(b, g, slope, grouped, cols=slice(0, P)):
+        def product(b, g, slope, grouped):
             nc.vector.tensor_tensor(
                 grouped.rearrange("p (c i t) -> p c t i", i=2, t=PACK),
                 slope.rearrange("p t (c i) -> p c t i", i=2),
-                banks[b, g][0][:, :, cols].rearrange("p t (c i) -> p c t i", i=2),
+                banks[b, g][0][:].rearrange("p t (c i) -> p c t i", i=2),
                 MULT,
             )
 
@@ -300,7 +298,7 @@ def tile_list_handover_gradient_kernel(
             product(0, g, slope0[:, :, g * P : (g + 1) * P], h00[:, g * PASS : (g + 1) * PASS])
 
         w1_grouped.append(cast_w1(1, w1_raw[1], WG1B))
-        deal_wf(1, 1, SLOT[0] + 6 * KIB, nc.scalar.copy)
+        deal_wf(1, 1, SLOT[0] + 2 * KIB, nc.scalar.copy)
         for g in range(4):
             passes(1, g, 1)
         for pair in range(2):
@@ -310,16 +308,6 @@ def tile_list_handover_gradient_kernel(
         h_mx = {}
         h_mx[0, 0] = quantize("h00", h00[:], at=SLOT[0] + 8 * KIB + HALF)
         w2_low = cast_w2(0, w2_raw[0], CG00)
-        less4 = placed([P, PACK, P], F32, "less4", W2LO[1] + 2 * KIB)
-        nc.scalar.activation(out=less4[:], in_=xs[1][:, :, HALF : HALF + P], func=COPY, bias=-1.0)
-        slope4 = []
-
-        def pool_slope4(part, at):
-            slope4.append(placed([P, PACK, P // 2], F32, "slope4%d" % part, at))
-            cols = slice(part * P // 2, (part + 1) * P // 2)
-            nc.gpsimd.tensor_tensor(slope4[part][:], less4[:, :, cols], xs[1][:, :, HALF : HALF + P][:, :, cols], MULT)
-
-        pool_slope4(0, CG01)
 
         w2_mx = {}
         h10 = [placed([P, QUARTER * PACK], BF16, "h10_g%d" % q, CG10 + 2 * q * KIB) for q in range(2)]
@@ -359,7 +347,6 @@ def tile_list_handover_gradient_kernel(
         close_second(1)
         w2_mx[0] = quantize("w2_0", w2_low)
         h10_mx[0] = quantize("h10a", h10[0][:], QUARTER)
-        pool_slope4(1, CG10)
         close_second(2)
         close_second(3)
         second_stage("00", 0, 0, [quarter(0)], 0, Y00)
@@ -385,14 +372,11 @@ def tile_list_handover_gradient_kernel(
         slopes1.update({5: slope5[:], 6: slope67[:, 0, :, :], 7: slope67[:, 1, :, :]})
         for g in range(5, 8):
             nc.gpsimd.tensor_tensor(slopes1[g], less_late[:, g - 5, :, :], xs[1][:, :, g * P : (g + 1) * P], MULT)
-        h01 = placed([P, HALF * PACK], BF16, "h01_g", TABLE)
+        h01 = placed([P, HALF * PACK], BF16, "h01_g", ROWS10)
         h11 = placed([P, HALF * PACK], BF16, "h11_g", 84 * KIB)
         for g in range(4, 8):
             product(0, g, slope0[:, :, g * P : (g + 1) * P], h01[:, (g - 4) * PASS : (g - 3) * PASS])
-        for part in range(2):
-            cols = slice(part * P // 2, (part + 1) * P // 2)
-            product(1, 4, slope4[part][:], h11[:, part * QUARTER : (part + 1) * QUARTER], cols)
-        for g in range(5, 8):
+        for g in range(4, 8):
             if g == 7:
                 w2_mx[1] = quantize("w2_1", w2_high, at=ROWS11 + 3 * KIB)
             product(1, g, slopes1[g], h11[:, (g - 4) * PASS : (g - 3) * PASS])

@@ -36,7 +36,7 @@ TABLE = 43 * KIB
 W1A = 31 * KIB
 WF1 = 39 * KIB
 W2LO = [11 * KIB, 15 * KIB]
-W2HI = [43 * KIB, 47 * KIB]
+W2HI = [45 * KIB, 49 * KIB]
 ROWS01 = 51 * KIB
 ROWS00 = 56 * KIB + HALF
 ROWS10 = 76 * KIB
@@ -224,9 +224,6 @@ def tile_list_handover_gradient_kernel(
         c_mx = {}
         c_mx[0, 0] = quantize("c00", c_grouped[0, 0], at=LAST_PLANE + HALF)
         deal_wf(0, 1, LAST_PLANE + 5 * KIB)
-        wgo_sb = placed([P, S], F32, "wgo_sb", W1A + 4 * KIB)
-        nc.sync.dma_start(out=wgo_sb[:], in_=wgo)
-        w2_raw.append(load_w2(1, W2HI))
 
         c_grouped[1, 0] = interleave("c10", rows10[:], CG10)
         w1_grouped = [cast_w1(0, w1_raw[0], WG1A)]
@@ -234,17 +231,23 @@ def tile_list_handover_gradient_kernel(
         c_mx[0, 1] = quantize("c01", c_grouped[0, 1], at=SLOT[2] + 2 * KIB)
         deal_wf(1, 0, LAST_PLANE + 3 * KIB)
         c_mx[1, 0] = quantize("c10", c_grouped[1, 0])
+        deal_wf(1, 1, W1A + 4 * KIB, nc.scalar.copy)
         v_w = {}
 
-        def gather_table(half, at):
-            v_w[half] = placed([P, HALF], U32, "v_w%d" % half, at)
-            picks = idx[:, half * HALF // 16 : (half + 1) * HALF // 16]
-            nc.vector.tensor_copy(v_w[half][:], tab_w[:].bitcast(U32).indirect(picks))
+        def gather_table(first, width, at):
+            words = placed([P, width], U32, "v_w%d" % first, at)
+            picks = idx[:, first // 16 : (first + width) // 16]
+            nc.vector.tensor_copy(words[:], tab_w[:].bitcast(U32).indirect(picks))
+            for g in range(width // P):
+                v_w[first // P + g] = words[:, g * P : (g + 1) * P]
 
         codes, scales = quantize("w1a", w1_grouped[0])
         w1_mx = {(0, t): (codes[:, t * P : (t + 1) * P], scales[:, t * P : (t + 1) * P]) for t in range(PACK)}
-        gather_table(0, W1A)
-        gather_table(1, W1A + 2 * KIB)
+        gather_table(0, QUARTER, W1A)
+        gather_table(QUARTER, S - QUARTER, W1A + KIB)
+        wgo_sb = placed([P, S], F32, "wgo_sb", TABLE - 2 * KIB)
+        nc.sync.dma_start(out=wgo_sb[:], in_=wgo)
+        w2_raw.append(load_w2(1, W2HI))
         for g, at in enumerate((WG1A - KIB, WG1A + KIB, WG1A + 3 * KIB)):
             cols = slice(g * P, (g + 1) * P)
             slope = placed([P, PACK, P], F32, "slope1%d" % g, at)
@@ -263,7 +266,7 @@ def tile_list_handover_gradient_kernel(
                 if kind == "table":
                     lhs = w1_mx[b, t][0].bitcast(E4)
                     lhs_scale = w1_mx[b, t][1]
-                    rhs = v_w[half][:, first : first + P].bitcast(E5)
+                    rhs = v_w[g].bitcast(E5)
                     rhs_scale = v_s[:, g * P : (g + 1) * P]
                 else:
                     lhs = wf_w[kind, b][:, t * P : (t + 1) * P].bitcast(E4)
@@ -276,11 +279,11 @@ def tile_list_handover_gradient_kernel(
                 )
                 banks[b, g][1] = done + 1
 
-        def product(b, g, slope, grouped):
+        def product(b, g, slope, grouped, cols=slice(0, P)):
             nc.vector.tensor_tensor(
                 grouped.rearrange("p (c i t) -> p c t i", i=2, t=PACK),
                 slope.rearrange("p t (c i) -> p c t i", i=2),
-                banks[b, g][0][:].rearrange("p t (c i) -> p c t i", i=2),
+                banks[b, g][0][:, :, cols].rearrange("p t (c i) -> p c t i", i=2),
                 MULT,
             )
 
@@ -289,17 +292,19 @@ def tile_list_handover_gradient_kernel(
             passes(0, g, 0)
         for g in range(4):
             passes(0, g, 1)
-        for g in range(4):
+        for g in range(2):
             open_bank(1, g, 4 + g)
             passes(1, g, 0)
+            passes(1, g, 1)
         h00 = placed([P, HALF * PACK], BF16, "h00_g", CG01)
         for g in range(4):
             passes(0, g, "table")
             product(0, g, slope0[:, :, g * P : (g + 1) * P], h00[:, g * PASS : (g + 1) * PASS])
 
         w1_grouped.append(cast_w1(1, w1_raw[1], WG1B))
-        deal_wf(1, 1, SLOT[0] + 2 * KIB, nc.scalar.copy)
-        for g in range(4):
+        for g in range(2, 4):
+            open_bank(1, g, g - 2)
+            passes(1, g, 0)
             passes(1, g, 1)
         for pair in range(2):
             codes, scales = quantize("w1b%d" % pair, w1_grouped[1][:, pair * KIB : (pair + 1) * KIB], QUARTER)
@@ -308,6 +313,17 @@ def tile_list_handover_gradient_kernel(
         h_mx = {}
         h_mx[0, 0] = quantize("h00", h00[:], at=SLOT[0] + 8 * KIB + HALF)
         w2_low = cast_w2(0, w2_raw[0], CG00)
+        x5 = xs[1][:, :, 5 * P : 6 * P]
+        less5 = placed([P, PACK, P], F32, "less5", W2LO[1] + 2 * KIB)
+        nc.scalar.activation(out=less5[:], in_=x5, func=COPY, bias=-1.0)
+        slope5 = []
+
+        def pool_slope5(part, at):
+            slope5.append(placed([P, PACK, P // 2], F32, "slope5%d" % part, at))
+            cols = slice(part * P // 2, (part + 1) * P // 2)
+            nc.gpsimd.tensor_tensor(slope5[part][:], less5[:, :, cols], x5[:, :, cols], MULT)
+
+        pool_slope5(0, CG01)
 
         w2_mx = {}
         h10 = [placed([P, QUARTER * PACK], BF16, "h10_g%d" % q, CG10 + 2 * q * KIB) for q in range(2)]
@@ -347,44 +363,49 @@ def tile_list_handover_gradient_kernel(
         close_second(1)
         w2_mx[0] = quantize("w2_0", w2_low)
         h10_mx[0] = quantize("h10a", h10[0][:], QUARTER)
+        pool_slope5(1, CG10)
         close_second(2)
         close_second(3)
-        second_stage("00", 0, 0, [quarter(0)], 0, Y00)
+        second_stage("00", 0, 0, [quarter(0)], 2, Y00)
         h10_mx[1] = quantize("h10b", h10[1][:], QUARTER)
-        second_stage("01", 1, 0, [quarter(0)], 1, Y01)
+        second_stage("01", 1, 0, [quarter(0)], 3, Y01)
         rows11 = placed([P, PACK, HALF], BF16, "rows11", ROWS11)
         for t in range(PACK):
             priced(rows11[:, t, :], xs[1][:, t, HALF:S], 1, t)
         c_mx[1, 1] = quantize("c11", interleave("c11", rows11[:], CG11))
-        second_stage("10", 0, QUARTER, [quarter(1)], 2, ROWS11)
-        second_stage("11", 1, QUARTER, [quarter(1)], 3, ROWS11 + 2 * KIB)
-        less_late = placed([P, 3, PACK, P], F32, "less_late", CG11 - 4 * KIB)
-        for g in range(5, 8):
-            nc.scalar.activation(out=less_late[:, g - 5, :, :], in_=xs[1][:, :, g * P : (g + 1) * P], func=COPY, bias=-1.0)
+        second_stage("10", 0, QUARTER, [quarter(1)], 6, ROWS11)
+        second_stage("11", 1, QUARTER, [quarter(1)], 7, ROWS11 + 2 * KIB)
+        less_late = placed([P, 2, PACK, P], F32, "less_late", CG11 - 2 * KIB)
+        for g in range(6, 8):
+            nc.scalar.activation(out=less_late[:, g - 6, :, :], in_=xs[1][:, :, g * P : (g + 1) * P], func=COPY, bias=-1.0)
         w2_high = cast_w2(1, w2_raw[1], CG11 + 2 * KIB)
         for b in range(BLOCKS):
             for g in range(4, 8):
-                open_bank(b, g, g - 4 * b)
+                open_bank(b, g, ((4, 5, 0, 1), (2, 3, 6, 7))[b][g - 4])
                 for kind in ("table", 0, 1):
                     passes(b, g, kind)
-        slope5 = placed([P, PACK, P], F32, "slope5", ROWS11 + 5 * HALF)
         slope67 = placed([P, 2, PACK, P], F32, "slope67", ROWS11 - 3 * HALF)
-        slopes1.update({5: slope5[:], 6: slope67[:, 0, :, :], 7: slope67[:, 1, :, :]})
-        for g in range(5, 8):
-            nc.gpsimd.tensor_tensor(slopes1[g], less_late[:, g - 5, :, :], xs[1][:, :, g * P : (g + 1) * P], MULT)
+        slopes1.update({6: slope67[:, 0, :, :], 7: slope67[:, 1, :, :]})
+        for g in range(6, 8):
+            nc.gpsimd.tensor_tensor(slopes1[g], less_late[:, g - 6, :, :], xs[1][:, :, g * P : (g + 1) * P], MULT)
         h01 = placed([P, HALF * PACK], BF16, "h01_g", ROWS10)
         h11 = placed([P, HALF * PACK], BF16, "h11_g", 84 * KIB)
         for g in range(4, 8):
             product(0, g, slope0[:, :, g * P : (g + 1) * P], h01[:, (g - 4) * PASS : (g - 3) * PASS])
         for g in range(4, 8):
             if g == 7:
-                w2_mx[1] = quantize("w2_1", w2_high, at=ROWS11 + 3 * KIB)
-            product(1, g, slopes1[g], h11[:, (g - 4) * PASS : (g - 3) * PASS])
-        h_mx[0, 1] = quantize("h01", h01[:], at=ROWS11 + 7 * HALF)
+                w2_mx[1] = quantize("w2_1", w2_high, at=CG10)
+            if g == 5:
+                for part in range(2):
+                    cols = slice(part * P // 2, (part + 1) * P // 2)
+                    product(1, g, slope5[part][:], h11[:, PASS + part * QUARTER : PASS + (part + 1) * QUARTER], cols)
+            else:
+                product(1, g, slopes1[g], h11[:, (g - 4) * PASS : (g - 3) * PASS])
+        h_mx[0, 1] = quantize("h01", h01[:], at=CG10 + HALF)
         h_mx[1, 1] = quantize("h11", h11[:])
         for q in range(2):
             second_stage("2%d" % q, 2, q * QUARTER, [quarter(q)], 4 + q, ROWS00 + (1 + q) * KIB)
-        second_stage("3", 3, 0, [quarter(0), quarter(1)], 6, ROWS00 + 3 * KIB)
+        second_stage("3", 3, 0, [quarter(0), quarter(1)], 0, ROWS00 + 3 * KIB)
         for u in range(NT):
-            second_stage("l%d" % u, u, HALF, [(HALF, [(h_mx[0, 1], 0), (h_mx[1, 1], 0)])], (7, 0, 1, 2)[u], Y_LAST + u * 2 * KIB)
+            second_stage("l%d" % u, u, HALF, [(HALF, [(h_mx[0, 1], 0), (h_mx[1, 1], 0)])], (1, 2, 3, 6)[u], Y_LAST + u * 2 * KIB)
             nc.sync.dma_start(out=out[u * P : (u + 1) * P, :], in_=pages[u][:])

@@ -26,7 +26,6 @@ QUARTER = 256
 BLOCKS = H // PASS
 PLANES = BLOCKS * PACK
 NT = N // P
-COLS = N // 2
 BANK = 2048
 
 KIB = 1024
@@ -35,8 +34,8 @@ LAST_PLANE = 21 * KIB
 TABLE = 43 * KIB
 W1A = 31 * KIB
 WF1 = 39 * KIB
-W2LO = [11 * KIB, 15 * KIB]
-W2HI = [45 * KIB, 49 * KIB]
+W2_RAW = [(9 * KIB, 11 * KIB), (13 * KIB, 15 * KIB), (45 * KIB, 49 * KIB)]
+W2_COLS = [(0, P), (P, P), (2 * P, 2 * P)]
 ROWS01 = 51 * KIB
 ROWS00 = 56 * KIB + HALF
 ROWS10 = 76 * KIB
@@ -97,17 +96,18 @@ def tile_list_handover_gradient_kernel(
                 )
             return grouped[:]
 
-        def load_w2(part, at):
+        def load_w2(part):
+            first, width = W2_COLS[part]
             raws = []
             for b in range(BLOCKS):
-                raw = placed([P, PACK, COLS], F32, "w2_raw%d%d" % (part, b), at[b])
-                rows = w2[b * PASS : (b + 1) * PASS, part * COLS : (part + 1) * COLS]
+                raw = placed([P, PACK, width], F32, "w2_raw%d%d" % (part, b), W2_RAW[part][b])
+                rows = w2[b * PASS : (b + 1) * PASS, first : first + width]
                 nc.sync.dma_start(out=raw[:], in_=rows.rearrange("(p j) c -> p j c", j=PACK))
                 raws.append(raw)
             return raws
 
         def cast_w2(part, raws, at):
-            grouped = placed([P, BLOCKS, COLS * PACK], BF16, "w2_g%d" % part, at)
+            grouped = placed([P, BLOCKS, W2_COLS[part][1] * PACK], BF16, "w2_g%d" % part, at)
             for b in range(BLOCKS):
                 nc.scalar.copy(
                     out=grouped[:, b, :].rearrange("p (c i t) -> p c t i", i=4, t=PACK),
@@ -213,7 +213,7 @@ def tile_list_handover_gradient_kernel(
                 out=v_s[32 * q : 32 * q + 4, :].bitcast(I32), in_=v_s_raw[4 * q : 4 * q + 4, :].bitcast(I32)
             )
         w1_raw.append(load_w1(1, SLOT[0] + KIB, 2))
-        w2_raw = [load_w2(0, W2LO)]
+        w2_raw = [load_w2(0), load_w2(1)]
         nc.sync.dma_start(idx2[:], offs2)
 
         deal_wf(0, 0, LAST_PLANE + KIB)
@@ -247,7 +247,7 @@ def tile_list_handover_gradient_kernel(
         gather_table(QUARTER, S - QUARTER, W1A + KIB)
         wgo_sb = placed([P, S], F32, "wgo_sb", TABLE - 2 * KIB)
         nc.sync.dma_start(out=wgo_sb[:], in_=wgo)
-        w2_raw.append(load_w2(1, W2HI))
+        w2_raw.append(load_w2(2))
         for g, at in enumerate((WG1A - KIB, WG1A + KIB, WG1A + 3 * KIB)):
             cols = slice(g * P, (g + 1) * P)
             slope = placed([P, PACK, P], F32, "slope1%d" % g, at)
@@ -312,10 +312,11 @@ def tile_list_handover_gradient_kernel(
                 w1_mx[1, 2 * pair + t] = (codes[:, t * P : (t + 1) * P], scales[:, t * P : (t + 1) * P])
         h_mx = {}
         h_mx[0, 0] = quantize("h00", h00[:], at=SLOT[0] + 8 * KIB + HALF)
-        w2_low = cast_w2(0, w2_raw[0], CG00)
+        w2_low = [cast_w2(0, w2_raw[0], CG00)]
         x5 = xs[1][:, :, 5 * P : 6 * P]
-        less5 = placed([P, PACK, P], F32, "less5", W2LO[1] + 2 * KIB)
+        less5 = placed([P, PACK, P], F32, "less5", W2_RAW[0][0])
         nc.scalar.activation(out=less5[:], in_=x5, func=COPY, bias=-1.0)
+        w2_low.append(cast_w2(1, w2_raw[1], CG00 + 2 * KIB))
         slope5 = []
 
         def pool_slope5(part, at):
@@ -334,7 +335,8 @@ def tile_list_handover_gradient_kernel(
             product(1, g, slopes1[g], h10[g // 2][:, g % 2 * PASS : (g % 2 + 1) * PASS])
 
         def second_stage(name, u, first, pieces, bank, at):
-            part, col = divmod(u * P, COLS)
+            part = min(u, 2)
+            col, cols = u * P - W2_COLS[part][0], W2_COLS[part][1]
             width = sum(w for w, operands in pieces)
             y = psum.tile([P, width], F32, name="y" + name, offset=bank * BANK)
             lo = 0
@@ -343,8 +345,8 @@ def tile_list_handover_gradient_kernel(
                     (codes, scales), start = operands[b]
                     nc.tensor.matmul_mx(
                         out=y[:, lo : lo + w],
-                        lhsT=w2_mx[part][0][:, b * COLS + col : b * COLS + col + P].bitcast(E4),
-                        lhsT_scale=w2_mx[part][1][:, b * COLS + col : b * COLS + col + P],
+                        lhsT=w2_mx[part][0][:, b * cols + col : b * cols + col + P].bitcast(E4),
+                        lhsT_scale=w2_mx[part][1][:, b * cols + col : b * cols + col + P],
                         rhs=codes[:, start : start + w].bitcast(E4),
                         rhs_scale=scales[:, start : start + w],
                         start=(b == 0),
@@ -361,11 +363,12 @@ def tile_list_handover_gradient_kernel(
 
         close_second(0)
         close_second(1)
-        w2_mx[0] = quantize("w2_0", w2_low)
+        w2_mx[0] = quantize("w2_0", w2_low[0], QUARTER)
         h10_mx[0] = quantize("h10a", h10[0][:], QUARTER)
         pool_slope5(1, CG10)
         close_second(2)
         close_second(3)
+        w2_mx[1] = quantize("w2_1", w2_low[1], QUARTER, CG10 + KIB)
         second_stage("00", 0, 0, [quarter(0)], 2, Y00)
         h10_mx[1] = quantize("h10b", h10[1][:], QUARTER)
         second_stage("01", 1, 0, [quarter(0)], 3, Y01)
@@ -378,7 +381,7 @@ def tile_list_handover_gradient_kernel(
         less_late = placed([P, 2, PACK, P], F32, "less_late", CG11 - 2 * KIB)
         for g in range(6, 8):
             nc.scalar.activation(out=less_late[:, g - 6, :, :], in_=xs[1][:, :, g * P : (g + 1) * P], func=COPY, bias=-1.0)
-        w2_high = cast_w2(1, w2_raw[1], CG11 + 2 * KIB)
+        w2_high = cast_w2(2, w2_raw[2], CG11 + 2 * KIB)
         for b in range(BLOCKS):
             for g in range(4, 8):
                 open_bank(b, g, ((4, 5, 0, 1), (2, 3, 6, 7))[b][g - 4])
@@ -394,7 +397,7 @@ def tile_list_handover_gradient_kernel(
             product(0, g, slope0[:, :, g * P : (g + 1) * P], h01[:, (g - 4) * PASS : (g - 3) * PASS])
         for g in range(4, 8):
             if g == 7:
-                w2_mx[1] = quantize("w2_1", w2_high, at=CG10)
+                w2_mx[2] = quantize("w2_2", w2_high, at=CG10)
             if g == 5:
                 for part in range(2):
                     cols = slice(part * P // 2, (part + 1) * P // 2)

@@ -27,6 +27,7 @@ BLOCKS = H // PASS
 PLANES = BLOCKS * PACK
 NT = N // P
 BANK = 2048
+VECTOR_SHARE = 16
 
 KIB = 1024
 SLOT = [0, 9 * KIB, 17 * KIB, 31 * KIB, 39 * KIB]
@@ -226,7 +227,13 @@ def tile_list_handover_gradient_kernel(
         deal_wf(0, 1, LAST_PLANE + 5 * KIB)
 
         c_grouped[1, 0] = interleave("c10", rows10[:], CG10)
-        w1_grouped = [cast_w1(0, w1_raw[0], WG1A)]
+        w1a = placed([P, PASS * PACK], BF16, "w1_g0", WG1A)
+        for copy, cols in ((nc.vector.tensor_copy, slice(0, VECTOR_SHARE)), (nc.scalar.copy, slice(VECTOR_SHARE, P))):
+            copy(
+                out=w1a[:].rearrange("p (t m j) -> p m j t", t=PACK, j=PACK)[:, cols, :, :],
+                in_=w1_raw[0][0][:].rearrange("p j (m t) -> p m j t", t=PACK)[:, cols, :, :],
+            )
+        w1_grouped = [w1a[:]]
         slopes1 = {3: vector_slope(3, LAST_PLANE + 7 * KIB), 4: vector_slope(4, None)}
         c_mx[0, 1] = quantize("c01", c_grouped[0, 1], at=SLOT[2] + 2 * KIB)
         deal_wf(1, 0, LAST_PLANE + 3 * KIB)

@@ -43,6 +43,9 @@ ROWS10 = 76 * KIB
 ROWS11 = 13 * KIB
 CG00, CG01, CG10, WG1A, WG1B = (k * KIB for k in (64, 68, 72, 106, 80))
 Y00, Y01, CG11, Y_LAST = (k * KIB for k in (91, 92, 93, 97))
+W2_HIGH = 15 * KIB
+Y2 = 86 * KIB
+D_SB = {(0, 2): 1 * KIB, (1, 2): 76 * KIB, (0, 3): 80 * KIB, (1, 3): 102 * KIB}
 
 
 def tile_list_handover_gradient_kernel(
@@ -341,7 +344,7 @@ def tile_list_handover_gradient_kernel(
             passes(1, g, "table")
             product(1, g, slopes1[g], h10[g // 2][:, g % 2 * PASS : (g % 2 + 1) * PASS])
 
-        def second_stage(name, u, first, pieces, bank, at):
+        def sums(name, u, pieces, bank):
             part = min(u, 2)
             col, cols = u * P - W2_COLS[part][0], W2_COLS[part][1]
             width = sum(w for w, operands in pieces)
@@ -360,10 +363,26 @@ def tile_list_handover_gradient_kernel(
                         stop=(b == BLOCKS - 1),
                     )
                 lo += w
+            return y, width
+
+        def fused_stage(name, u, first, pieces, bank, at):
+            y, width = sums(name, u, pieces, bank)
             y_sb = placed([P, width], F32, "y_sb" + name, at)
             nc.scalar.activation(out=y_sb[:], in_=y[:], func=COPY, scale=-1.0)
             slots = idx2[:, first // 16 : (first + width) // 16]
             nc.vector.tensor_tensor(pages[u][:].indirect(slots), y_sb[:], wgo_sb[:, first : first + width], MULT)
+
+        def weighted(name, u, first, pieces, bank, at):
+            y, width = sums(name, u, pieces, bank)
+            y_sb = placed([P, width], F32, "y_sb" + name, at)
+            nc.vector.scalar_tensor_tensor(
+                out=y_sb[:], in0=wgo_sb[:, first : first + width], scalar=-1.0, in1=y[:], op0=MULT, op1=MULT
+            )
+            return y_sb
+
+        def put(u, first, values):
+            slots = idx2[:, first // 16 : (first + QUARTER) // 16]
+            nc.vector.tensor_copy(pages[u][:].indirect(slots), values)
 
         def quarter(q):
             return (QUARTER, [(h_mx[0, 0], q * QUARTER), (h10_mx[q], 0)])
@@ -376,46 +395,84 @@ def tile_list_handover_gradient_kernel(
         close_second(2)
         close_second(3)
         w2_mx[1] = quantize("w2_1", w2_low[1], QUARTER, CG10 + KIB)
-        second_stage("00", 0, 0, [quarter(0)], 2, Y00)
+        fused_stage("00", 0, 0, [quarter(0)], 2, Y00)
         h10_mx[1] = quantize("h10b", h10[1][:], QUARTER)
-        second_stage("01", 1, 0, [quarter(0)], 3, Y01)
+        fused_stage("01", 1, 0, [quarter(0)], 3, Y01)
         rows11 = placed([P, PACK, HALF], BF16, "rows11", ROWS11)
         for t in range(PACK):
             priced(rows11[:, t, :], xs[1][:, t, HALF:S], 1, t)
         c_mx[1, 1] = quantize("c11", interleave("c11", rows11[:], CG11))
-        second_stage("10", 0, QUARTER, [quarter(1)], 6, ROWS11)
-        second_stage("11", 1, QUARTER, [quarter(1)], 7, ROWS11 + 2 * KIB)
-        less_late = placed([P, 2, PACK, P], F32, "less_late", CG11 - 2 * KIB)
-        for g in range(6, 8):
-            nc.scalar.activation(out=less_late[:, g - 6, :, :], in_=xs[1][:, :, g * P : (g + 1) * P], func=COPY, bias=-1.0)
-        w2_high = cast_w2(2, w2_raw[2], CG11 + 2 * KIB)
-        for b in range(BLOCKS):
-            for g in range(4, 8):
+        fused_stage("10", 0, QUARTER, [quarter(1)], 6, ROWS11)
+        w2_high = cast_w2(2, w2_raw[2], W2_HIGH)
+        y11 = weighted("11", 1, QUARTER, [quarter(1)], 7, W2_RAW[2][1])
+        w2_mx[2] = quantize("w2_2", w2_high)
+        put(1, QUARTER, y11[:])
+        for g in range(4, 8):
+            for b in range(BLOCKS):
                 open_bank(b, g, ((4, 5, 0, 1), (2, 3, 6, 7))[b][g - 4])
-                for kind in ("table", 0, 1):
-                    passes(b, g, kind)
-        slope67 = placed([P, 2, PACK, P], F32, "slope67", ROWS11 - 3 * HALF)
-        slopes1.update({6: slope67[:, 0, :, :], 7: slope67[:, 1, :, :]})
-        for g in range(6, 8):
-            nc.gpsimd.tensor_tensor(slopes1[g], less_late[:, g - 6, :, :], xs[1][:, :, g * P : (g + 1) * P], MULT)
-        h01 = placed([P, HALF * PACK], BF16, "h01_g", ROWS10)
-        h11 = placed([P, HALF * PACK], BF16, "h11_g", 84 * KIB)
-        for g in range(4, 8):
-            product(0, g, slope0[:, :, g * P : (g + 1) * P], h01[:, (g - 4) * PASS : (g - 3) * PASS])
-        for g in range(4, 8):
-            if g == 7:
-                w2_mx[2] = quantize("w2_2", w2_high, at=CG10)
-            if g == 5:
-                for part in range(2):
-                    cols = slice(part * P // 2, (part + 1) * P // 2)
-                    product(1, g, slope5[part][:], h11[:, PASS + part * QUARTER : PASS + (part + 1) * QUARTER], cols)
-            else:
-                product(1, g, slopes1[g], h11[:, (g - 4) * PASS : (g - 3) * PASS])
-        h_mx[0, 1] = quantize("h01", h01[:], at=CG10 + HALF)
-        h_mx[1, 1] = quantize("h11", h11[:])
+        for pair in ((4, 5), (6, 7)):
+            for b in range(BLOCKS):
+                for g in pair:
+                    for kind in ("table", 0, 1):
+                        passes(b, g, kind)
+
+        d_sb = {}
+
+        def copy_out(b, q):
+            d_sb[b, q] = placed([P, 2, PASS], F32, "d_sb%d%d" % (b, q), D_SB[b, q])
+            for g in range(2):
+                nc.scalar.copy(
+                    out=d_sb[b, q][:, g, :].rearrange("p (c t i) -> p c t i", t=PACK, i=4),
+                    in_=banks[b, 2 * q + g][0][:].rearrange("p t (c i) -> p c t i", i=4),
+                )
+
+        def pool_product(b, q, slope, grouped, first, width):
+            cols = slice(first * PACK, (first + width) * PACK)
+            nc.gpsimd.tensor_tensor(
+                grouped[:, b, cols].rearrange("p (c i t) -> p c t i", i=4, t=PACK),
+                slope.rearrange("p t (c i) -> p c t i", i=4),
+                d_sb[b, q][:].rearrange("p g n -> p (g n)")[:, cols].rearrange("p (c t i) -> p c t i", t=PACK, i=4),
+                MULT,
+            )
+
+        for b in range(BLOCKS):
+            copy_out(b, 2)
+        less_late = placed([P, PACK, QUARTER], F32, "less_late", W2_RAW[2][1] + KIB)
+        x_late = xs[1][:, :, S - QUARTER : S]
+        nc.scalar.activation(out=less_late[:], in_=x_late, func=COPY, bias=-1.0)
+        for b in range(BLOCKS):
+            copy_out(b, 3)
+        h2 = placed([P, BLOCKS, QUARTER * PACK], BF16, "h2_g", W2_HIGH)
+        pool_product(0, 2, slope0[:, :, HALF : HALF + QUARTER], h2, 0, QUARTER)
+        pool_product(1, 2, slopes1[4], h2, 0, P)
+        for part in range(2):
+            pool_product(1, 2, slope5[part][:], h2, P + part * P // 2, P // 2)
+        h2_grouped = h2[:].rearrange("p b n -> p (b n)")
+
+        y2 = [weighted("2%d" % q, 2, q * QUARTER, [quarter(q)], 4 + q, Y2 + q * KIB) for q in range(2)]
         for q in range(2):
-            second_stage("2%d" % q, 2, q * QUARTER, [quarter(q)], 4 + q, ROWS00 + (1 + q) * KIB)
-        second_stage("3", 3, 0, [quarter(0), quarter(1)], 0, ROWS00 + 3 * KIB)
-        for u in range(NT):
-            second_stage("l%d" % u, u, HALF, [(HALF, [(h_mx[0, 1], 0), (h_mx[1, 1], 0)])], (1, 2, 3, 6)[u], Y_LAST + u * 2 * KIB)
+            put(2, q * QUARTER, y2[q][:])
+        y3 = weighted("3", 3, 0, [quarter(0), quarter(1)], 2, D_SB[1, 2])
+        h2_mx = quantize("h2", h2_grouped)
+        for q in range(2):
+            put(3, q * QUARTER, y3[:, q * QUARTER : (q + 1) * QUARTER])
+
+        slope_late = placed([P, PACK, QUARTER], F32, "slope_late", W2_HIGH - 3 * KIB)
+        nc.gpsimd.tensor_tensor(slope_late[:], less_late[:], x_late, MULT)
+        h3 = placed([P, BLOCKS, QUARTER * PACK], BF16, "h3_g", W2_HIGH + KIB)
+        pool_product(0, 3, slope0[:, :, S - QUARTER : S], h3, 0, QUARTER)
+        pool_product(1, 3, slope_late[:], h3, 0, QUARTER)
+        h3_grouped = h3[:].rearrange("p b n -> p (b n)")
+
+        third = (QUARTER, [(h2_mx, 0), (h2_mx, QUARTER)])
+        y_third = [weighted("t%d" % u, u, HALF, [third], 4 + u, Y2 + (2 + u) * KIB) for u in range(2)]
+        for u in range(2):
+            put(u, HALF, y_third[u][:])
+        h3_mx = quantize("h3", h3_grouped)
+        fused_stage("t2", 2, HALF, [third], 3, D_SB[1, 3])
+        fourth = (QUARTER, [(h3_mx, 0), (h3_mx, QUARTER)])
+        for u in range(NT - 1):
+            fused_stage("l%d" % u, u, HALF + QUARTER, [fourth], (0, 1, 6)[u], Y_LAST + u * KIB)
             nc.sync.dma_start(out=out[u * P : (u + 1) * P, :], in_=pages[u][:])
+        fused_stage("l3", 3, HALF, [third, fourth], 7, Y_LAST + 3 * KIB)
+        nc.sync.dma_start(out=out[3 * P : 4 * P, :], in_=pages[3][:])

@@ -45,7 +45,7 @@ CG00, CG01, CG10, WG1A, WG1B = (k * KIB for k in (64, 68, 72, 106, 80))
 Y00, Y01, CG11, Y_LAST = (k * KIB for k in (91, 92, 93, 97))
 W2_HIGH = 15 * KIB
 Y2 = 86 * KIB
-D_SB = {(0, 2): 1 * KIB, (1, 2): 76 * KIB, (0, 3): 80 * KIB, (1, 3): 102 * KIB}
+D_SB = {(0, 2): 1 * KIB, (1, 2): 57 * KIB, (0, 3): 80 * KIB, (1, 3): 102 * KIB}
 
 
 def tile_list_handover_gradient_kernel(
@@ -237,7 +237,7 @@ def tile_list_handover_gradient_kernel(
                 in_=w1_raw[0][0][:].rearrange("p j (m t) -> p m j t", t=PACK)[:, cols, :, :],
             )
         w1_grouped = [w1a[:]]
-        slopes1 = {3: vector_slope(3, LAST_PLANE + 7 * KIB), 4: vector_slope(4, None)}
+        slopes1 = {3: vector_slope(3, LAST_PLANE + 7 * KIB)}
         c_mx[0, 1] = quantize("c01", c_grouped[0, 1], at=SLOT[2] + 2 * KIB)
         deal_wf(1, 0, LAST_PLANE + 3 * KIB)
         c_mx[1, 0] = quantize("c10", c_grouped[1, 0])
@@ -323,18 +323,18 @@ def tile_list_handover_gradient_kernel(
         h_mx = {}
         h_mx[0, 0] = quantize("h00", h00[:], at=SLOT[0] + 8 * KIB + HALF)
         w2_low = [cast_w2(0, w2_raw[0], CG00)]
-        x5 = xs[1][:, :, 5 * P : 6 * P]
-        less5 = placed([P, PACK, P], F32, "less5", W2_RAW[0][0])
-        nc.scalar.activation(out=less5[:], in_=x5, func=COPY, bias=-1.0)
+        x4 = xs[1][:, :, 4 * P : 5 * P]
+        less4 = placed([P, PACK, P], F32, "less4", W2_RAW[0][0])
+        nc.scalar.activation(out=less4[:], in_=x4, func=COPY, bias=-1.0)
         w2_low.append(cast_w2(1, w2_raw[1], CG00 + 2 * KIB))
-        slope5 = []
+        slope4 = []
 
-        def pool_slope5(part, at):
-            slope5.append(placed([P, PACK, P // 2], F32, "slope5%d" % part, at))
+        def pool_slope4(part, at):
+            slope4.append(placed([P, PACK, P // 2], F32, "slope4%d" % part, at))
             cols = slice(part * P // 2, (part + 1) * P // 2)
-            nc.gpsimd.tensor_tensor(slope5[part][:], less5[:, :, cols], x5[:, :, cols], MULT)
+            nc.gpsimd.tensor_tensor(slope4[part][:], less4[:, :, cols], x4[:, :, cols], MULT)
 
-        pool_slope5(0, CG01)
+        pool_slope4(0, CG01)
 
         w2_mx = {}
         h10 = [placed([P, QUARTER * PACK], BF16, "h10_g%d" % q, CG10 + 2 * q * KIB) for q in range(2)]
@@ -363,22 +363,22 @@ def tile_list_handover_gradient_kernel(
                         stop=(b == BLOCKS - 1),
                     )
                 lo += w
-            return y, width
+            return y[:]
 
         def fused_stage(name, u, first, pieces, bank, at):
-            y, width = sums(name, u, pieces, bank)
+            y = sums(name, u, pieces, bank)
+            width = y.shape[1]
             y_sb = placed([P, width], F32, "y_sb" + name, at)
-            nc.scalar.activation(out=y_sb[:], in_=y[:], func=COPY, scale=-1.0)
+            nc.scalar.activation(out=y_sb[:], in_=y, func=COPY, scale=-1.0)
             slots = idx2[:, first // 16 : (first + width) // 16]
             nc.vector.tensor_tensor(pages[u][:].indirect(slots), y_sb[:], wgo_sb[:, first : first + width], MULT)
 
-        def weighted(name, u, first, pieces, bank, at):
-            y, width = sums(name, u, pieces, bank)
-            y_sb = placed([P, width], F32, "y_sb" + name, at)
+        def weighted(name, y, first, at):
+            y_sb = placed([P, QUARTER], F32, "y_sb" + name, at)
             nc.vector.scalar_tensor_tensor(
-                out=y_sb[:], in0=wgo_sb[:, first : first + width], scalar=-1.0, in1=y[:], op0=MULT, op1=MULT
+                out=y_sb[:], in0=wgo_sb[:, first : first + QUARTER], scalar=-1.0, in1=y, op0=MULT, op1=MULT
             )
-            return y_sb
+            return y_sb[:]
 
         def put(u, first, values):
             slots = idx2[:, first // 16 : (first + QUARTER) // 16]
@@ -391,30 +391,40 @@ def tile_list_handover_gradient_kernel(
         close_second(1)
         w2_mx[0] = quantize("w2_0", w2_low[0], QUARTER)
         h10_mx[0] = quantize("h10a", h10[0][:], QUARTER)
-        pool_slope5(1, CG10)
+        pool_slope4(1, CG10)
         close_second(2)
         close_second(3)
         w2_mx[1] = quantize("w2_1", w2_low[1], QUARTER, CG10 + KIB)
-        fused_stage("00", 0, 0, [quarter(0)], 2, Y00)
+        y00 = weighted("00", sums("00", 0, [quarter(0)], 2), 0, Y00)
         h10_mx[1] = quantize("h10b", h10[1][:], QUARTER)
-        fused_stage("01", 1, 0, [quarter(0)], 3, Y01)
+        y01 = weighted("01", sums("01", 1, [quarter(0)], 3), 0, Y01)
+        put(0, 0, y00)
+        put(1, 0, y01)
+        late = placed([P, PACK, 3 * P], F32, "late", CG10 + 2 * KIB)
+        x_late = xs[1][:, :, S - 3 * P : S]
+        nc.gpsimd.tensor_scalar(late[:], x_late, 1.0, -1.0, MULT, ADD)
+        slope5 = placed([P, PACK, P], F32, "slope5")
+        nc.gpsimd.tensor_tensor(slope5[:], late[:, :, 0:P], x_late[:, :, 0:P], MULT)
         rows11 = placed([P, PACK, HALF], BF16, "rows11", ROWS11)
         for t in range(PACK):
             priced(rows11[:, t, :], xs[1][:, t, HALF:S], 1, t)
-        c_mx[1, 1] = quantize("c11", interleave("c11", rows11[:], CG11))
-        fused_stage("10", 0, QUARTER, [quarter(1)], 6, ROWS11)
+        c11_grouped = interleave("c11", rows11[:], CG11)
+        y10 = weighted("10", sums("10", 0, [quarter(1)], 6), QUARTER, ROWS11)
+        c_mx[1, 1] = quantize("c11", c11_grouped)
+        put(0, QUARTER, y10)
+        slope6 = placed([P, PACK, P], F32, "slope6", CG11)
+        nc.gpsimd.tensor_tensor(slope6[:], late[:, :, P:QUARTER], x_late[:, :, P:QUARTER], MULT)
         w2_high = cast_w2(2, w2_raw[2], W2_HIGH)
-        y11 = weighted("11", 1, QUARTER, [quarter(1)], 7, W2_RAW[2][1])
+        y11 = weighted("11", sums("11", 1, [quarter(1)], 7), QUARTER, W2_RAW[2][1])
         w2_mx[2] = quantize("w2_2", w2_high)
-        put(1, QUARTER, y11[:])
-        for g in range(4, 8):
+        put(1, QUARTER, y11)
+
+        def late_sums(q, four):
             for b in range(BLOCKS):
-                open_bank(b, g, ((4, 5, 0, 1), (2, 3, 6, 7))[b][g - 4])
-        for pair in ((4, 5), (6, 7)):
-            for b in range(BLOCKS):
-                for g in pair:
+                for g in range(2):
+                    open_bank(b, 2 * q + g, four[2 * b + g])
                     for kind in ("table", 0, 1):
-                        passes(b, g, kind)
+                        passes(b, 2 * q + g, kind)
 
         d_sb = {}
 
@@ -435,44 +445,45 @@ def tile_list_handover_gradient_kernel(
                 MULT,
             )
 
-        for b in range(BLOCKS):
-            copy_out(b, 2)
-        less_late = placed([P, PACK, QUARTER], F32, "less_late", W2_RAW[2][1] + KIB)
-        x_late = xs[1][:, :, S - QUARTER : S]
-        nc.scalar.activation(out=less_late[:], in_=x_late, func=COPY, bias=-1.0)
-        for b in range(BLOCKS):
-            copy_out(b, 3)
-        h2 = placed([P, BLOCKS, QUARTER * PACK], BF16, "h2_g", W2_HIGH)
+        late_sums(2, (4, 5, 2, 3))
+        y2 = sums("2", 2, [quarter(0), quarter(1)], 0)
+        y3 = sums("3", 3, [quarter(0), quarter(1)], 1)
+        late_sums(3, (6, 7, 0, 4))
+        for q in (2, 3):
+            for b in range(BLOCKS):
+                copy_out(b, q)
+        slope7 = placed([P, PACK, P], F32, "slope7", W2_HIGH + 2 * KIB)
+        nc.gpsimd.tensor_tensor(slope7[:], late[:, :, QUARTER:], x_late[:, :, QUARTER:], MULT)
+        h2 = placed([P, BLOCKS, QUARTER * PACK], BF16, "h2_g", W2_HIGH - 2 * KIB)
         pool_product(0, 2, slope0[:, :, HALF : HALF + QUARTER], h2, 0, QUARTER)
-        pool_product(1, 2, slopes1[4], h2, 0, P)
         for part in range(2):
-            pool_product(1, 2, slope5[part][:], h2, P + part * P // 2, P // 2)
-        h2_grouped = h2[:].rearrange("p b n -> p (b n)")
+            pool_product(1, 2, slope4[part][:], h2, part * P // 2, P // 2)
+        pool_product(1, 2, slope5[:], h2, P, P)
 
-        y2 = [weighted("2%d" % q, 2, q * QUARTER, [quarter(q)], 4 + q, Y2 + q * KIB) for q in range(2)]
-        for q in range(2):
-            put(2, q * QUARTER, y2[q][:])
-        y3 = weighted("3", 3, 0, [quarter(0), quarter(1)], 2, D_SB[1, 2])
-        h2_mx = quantize("h2", h2_grouped)
-        for q in range(2):
-            put(3, q * QUARTER, y3[:, q * QUARTER : (q + 1) * QUARTER])
+        y2a = weighted("2a", y2[:, 0:QUARTER], 0, Y2)
+        y2b = weighted("2b", y2[:, QUARTER:HALF], QUARTER, Y2 + KIB)
+        y3a = weighted("3a", y3[:, 0:QUARTER], 0, Y2 + 2 * KIB)
+        put(2, 0, y2a)
+        put(2, QUARTER, y2b)
+        put(3, 0, y3a)
+        y3b = weighted("3b", y3[:, QUARTER:HALF], QUARTER, D_SB[1, 2])
+        h2_mx = quantize("h2", h2[:].rearrange("p b n -> p (b n)"))
+        put(3, QUARTER, y3b)
 
-        slope_late = placed([P, PACK, QUARTER], F32, "slope_late", W2_HIGH - 3 * KIB)
-        nc.gpsimd.tensor_tensor(slope_late[:], less_late[:], x_late, MULT)
-        h3 = placed([P, BLOCKS, QUARTER * PACK], BF16, "h3_g", W2_HIGH + KIB)
+        h3 = placed([P, BLOCKS, QUARTER * PACK], BF16, "h3_g", W2_HIGH - 2 * KIB)
         pool_product(0, 3, slope0[:, :, S - QUARTER : S], h3, 0, QUARTER)
-        pool_product(1, 3, slope_late[:], h3, 0, QUARTER)
-        h3_grouped = h3[:].rearrange("p b n -> p (b n)")
+        pool_product(1, 3, slope6[:], h3, 0, P)
+        pool_product(1, 3, slope7[:], h3, P, P)
 
         third = (QUARTER, [(h2_mx, 0), (h2_mx, QUARTER)])
-        y_third = [weighted("t%d" % u, u, HALF, [third], 4 + u, Y2 + (2 + u) * KIB) for u in range(2)]
+        y_third = [weighted("t%d" % u, sums("t%d" % u, u, [third], (5, 2)[u]), HALF, (Y2 + 3 * KIB, Y2 + 4 * KIB)[u]) for u in range(2)]
         for u in range(2):
-            put(u, HALF, y_third[u][:])
-        h3_mx = quantize("h3", h3_grouped)
+            put(u, HALF, y_third[u])
+        h3_mx = quantize("h3", h3[:].rearrange("p b n -> p (b n)"))
         fused_stage("t2", 2, HALF, [third], 3, D_SB[1, 3])
         fourth = (QUARTER, [(h3_mx, 0), (h3_mx, QUARTER)])
         for u in range(NT - 1):
-            fused_stage("l%d" % u, u, HALF + QUARTER, [fourth], (0, 1, 6)[u], Y_LAST + u * KIB)
+            fused_stage("l%d" % u, u, HALF + QUARTER, [fourth], (6, 7, 0)[u], Y_LAST + u * KIB)
             nc.sync.dma_start(out=out[u * P : (u + 1) * P, :], in_=pages[u][:])
-        fused_stage("l3", 3, HALF, [third, fourth], 7, Y_LAST + 3 * KIB)
+        fused_stage("l3", 3, HALF, [third, fourth], 4, Y_LAST + 3 * KIB)
         nc.sync.dma_start(out=out[3 * P : 4 * P, :], in_=pages[3][:])

@@ -193,7 +193,7 @@ def tile_list_handover_gradient_kernel(
             if k < PACK - 1:
                 nc.scalar.activation(out=slope0[:, t, :], in_=x, func=COPY, bias=-1.0)
                 nc.gpsimd.tensor_tensor(slope0[:, t, :], slope0[:, t, :], x, MULT)
-            elif k == PACK - 1:
+            elif k < PACK:
                 nc.gpsimd.tensor_scalar(slope0[:, t, :], x, 1.0, -1.0, MULT, ADD)
                 nc.gpsimd.tensor_tensor(slope0[:, t, :], slope0[:, t, :], x, MULT)
             else:
@@ -221,13 +221,12 @@ def tile_list_handover_gradient_kernel(
         nc.sync.dma_start(idx2[:], offs2)
 
         deal_wf(0, 0, LAST_PLANE + KIB)
-        wf_s = placed([P, PASS], U8, "wf_s", LAST_PLANE)
-        nc.vector.tensor_copy(
+        wf_s = placed([P, PASS], U8, "wf_s")
+        nc.gpsimd.tensor_copy(
             out=wf_s[:].rearrange("p (t m) -> p t m", t=PACK), in_=wf_s_raw[:, 0:PASS].rearrange("p (m t) -> p t m", t=PACK)
         )
         c_mx = {}
         c_mx[0, 0] = quantize("c00", c_grouped[0, 0], at=LAST_PLANE + HALF)
-        deal_wf(0, 1, LAST_PLANE + 5 * KIB)
 
         c_grouped[1, 0] = interleave("c10", rows10[:], CG10)
         w1a = placed([P, PASS * PACK], BF16, "w1_g0", WG1A)
@@ -237,10 +236,11 @@ def tile_list_handover_gradient_kernel(
                 in_=w1_raw[0][0][:].rearrange("p j (m t) -> p m j t", t=PACK)[:, cols, :, :],
             )
         w1_grouped = [w1a[:]]
-        slopes1 = {3: vector_slope(3, LAST_PLANE + 7 * KIB)}
-        c_mx[0, 1] = quantize("c01", c_grouped[0, 1], at=SLOT[2] + 2 * KIB)
+        slopes1 = {3: vector_slope(3, LAST_PLANE + 7 * KIB), 4: vector_slope(4, None)}
+        c_mx[0, 1] = quantize("c01", c_grouped[0, 1], at=LAST_PLANE + 5 * KIB)
         deal_wf(1, 0, LAST_PLANE + 3 * KIB)
         c_mx[1, 0] = quantize("c10", c_grouped[1, 0])
+        deal_wf(0, 1, W1A + 6 * KIB, nc.scalar.copy)
         deal_wf(1, 1, W1A + 4 * KIB, nc.scalar.copy)
         v_w = {}
 
@@ -254,7 +254,8 @@ def tile_list_handover_gradient_kernel(
         codes, scales = quantize("w1a", w1_grouped[0])
         w1_mx = {(0, t): (codes[:, t * P : (t + 1) * P], scales[:, t * P : (t + 1) * P]) for t in range(PACK)}
         gather_table(0, QUARTER, W1A)
-        gather_table(QUARTER, S - QUARTER, W1A + KIB)
+        gather_table(QUARTER, QUARTER, W1A + KIB)
+        gather_table(HALF, HALF, W1A + 2 * KIB)
         wgo_sb = placed([P, S], F32, "wgo_sb", TABLE - 2 * KIB)
         nc.sync.dma_start(out=wgo_sb[:], in_=wgo)
         w2_raw.append(load_w2(2))
@@ -302,14 +303,14 @@ def tile_list_handover_gradient_kernel(
             passes(0, g, 0)
         for g in range(4):
             passes(0, g, 1)
-        for g in range(2):
-            open_bank(1, g, 4 + g)
-            passes(1, g, 0)
-            passes(1, g, 1)
         h00 = placed([P, HALF * PACK], BF16, "h00_g", CG01)
         for g in range(4):
             passes(0, g, "table")
             product(0, g, slope0[:, :, g * P : (g + 1) * P], h00[:, g * PASS : (g + 1) * PASS])
+        for g in range(2):
+            open_bank(1, g, 4 + g)
+            passes(1, g, 0)
+            passes(1, g, 1)
 
         w1_grouped.append(cast_w1(1, w1_raw[1], WG1B))
         for g in range(2, 4):
@@ -323,18 +324,18 @@ def tile_list_handover_gradient_kernel(
         h_mx = {}
         h_mx[0, 0] = quantize("h00", h00[:], at=SLOT[0] + 8 * KIB + HALF)
         w2_low = [cast_w2(0, w2_raw[0], CG00)]
-        x4 = xs[1][:, :, 4 * P : 5 * P]
-        less4 = placed([P, PACK, P], F32, "less4", W2_RAW[0][0])
-        nc.scalar.activation(out=less4[:], in_=x4, func=COPY, bias=-1.0)
+        x5 = xs[1][:, :, 5 * P : 6 * P]
+        less5 = placed([P, PACK, P], F32, "less5", W2_RAW[0][0])
+        nc.scalar.activation(out=less5[:], in_=x5, func=COPY, bias=-1.0)
         w2_low.append(cast_w2(1, w2_raw[1], CG00 + 2 * KIB))
-        slope4 = []
+        slope5 = []
 
-        def pool_slope4(part, at):
-            slope4.append(placed([P, PACK, P // 2], F32, "slope4%d" % part, at))
+        def pool_slope5(part, at):
+            slope5.append(placed([P, PACK, P // 2], F32, "slope5%d" % part, at))
             cols = slice(part * P // 2, (part + 1) * P // 2)
-            nc.gpsimd.tensor_tensor(slope4[part][:], less4[:, :, cols], x4[:, :, cols], MULT)
+            nc.gpsimd.tensor_tensor(slope5[part][:], less5[:, :, cols], x5[:, :, cols], MULT)
 
-        pool_slope4(0, CG01)
+        pool_slope5(0, CG01)
 
         w2_mx = {}
         h10 = [placed([P, QUARTER * PACK], BF16, "h10_g%d" % q, CG10 + 2 * q * KIB) for q in range(2)]
@@ -391,20 +392,13 @@ def tile_list_handover_gradient_kernel(
         close_second(1)
         w2_mx[0] = quantize("w2_0", w2_low[0], QUARTER)
         h10_mx[0] = quantize("h10a", h10[0][:], QUARTER)
-        pool_slope4(1, CG10)
+        pool_slope5(1, CG10)
         close_second(2)
         close_second(3)
         w2_mx[1] = quantize("w2_1", w2_low[1], QUARTER, CG10 + KIB)
-        y00 = weighted("00", sums("00", 0, [quarter(0)], 2), 0, Y00)
+        fused_stage("00", 0, 0, [quarter(0)], 2, Y00)
         h10_mx[1] = quantize("h10b", h10[1][:], QUARTER)
-        y01 = weighted("01", sums("01", 1, [quarter(0)], 3), 0, Y01)
-        put(0, 0, y00)
-        put(1, 0, y01)
-        late = placed([P, PACK, 3 * P], F32, "late", CG10 + 2 * KIB)
-        x_late = xs[1][:, :, S - 3 * P : S]
-        nc.gpsimd.tensor_scalar(late[:], x_late, 1.0, -1.0, MULT, ADD)
-        slope5 = placed([P, PACK, P], F32, "slope5")
-        nc.gpsimd.tensor_tensor(slope5[:], late[:, :, 0:P], x_late[:, :, 0:P], MULT)
+        fused_stage("01", 1, 0, [quarter(0)], 3, Y01)
         rows11 = placed([P, PACK, HALF], BF16, "rows11", ROWS11)
         for t in range(PACK):
             priced(rows11[:, t, :], xs[1][:, t, HALF:S], 1, t)
@@ -412,12 +406,22 @@ def tile_list_handover_gradient_kernel(
         y10 = weighted("10", sums("10", 0, [quarter(1)], 6), QUARTER, ROWS11)
         c_mx[1, 1] = quantize("c11", c11_grouped)
         put(0, QUARTER, y10)
-        slope6 = placed([P, PACK, P], F32, "slope6", CG11)
-        nc.gpsimd.tensor_tensor(slope6[:], late[:, :, P:QUARTER], x_late[:, :, P:QUARTER], MULT)
-        w2_high = cast_w2(2, w2_raw[2], W2_HIGH)
+
+        def late_slope(g, less_at, at):
+            x = xs[1][:, :, g * P : (g + 1) * P]
+            less = placed([P, PACK, P], F32, "less%d" % g, less_at)
+            nc.scalar.activation(out=less[:], in_=x, func=COPY, bias=-1.0)
+            slope = placed([P, PACK, P], F32, "slope%d" % g, at)
+            nc.gpsimd.tensor_tensor(slope[:], less[:], x, MULT)
+            return slope[:]
+
+        w2_high_at = W2_HIGH + KIB
+        slope6 = late_slope(6, ROWS11 + KIB, CG11)
+        w2_high = cast_w2(2, w2_raw[2], w2_high_at)
         y11 = weighted("11", sums("11", 1, [quarter(1)], 7), QUARTER, W2_RAW[2][1])
         w2_mx[2] = quantize("w2_2", w2_high)
         put(1, QUARTER, y11)
+        slope7 = late_slope(7, W2_RAW[2][1] + KIB, w2_high_at + 2 * KIB)
 
         def late_sums(q, four):
             for b in range(BLOCKS):
@@ -452,13 +456,11 @@ def tile_list_handover_gradient_kernel(
         for q in (2, 3):
             for b in range(BLOCKS):
                 copy_out(b, q)
-        slope7 = placed([P, PACK, P], F32, "slope7", W2_HIGH + 2 * KIB)
-        nc.gpsimd.tensor_tensor(slope7[:], late[:, :, QUARTER:], x_late[:, :, QUARTER:], MULT)
-        h2 = placed([P, BLOCKS, QUARTER * PACK], BF16, "h2_g", W2_HIGH - 2 * KIB)
+        h2 = placed([P, BLOCKS, QUARTER * PACK], BF16, "h2_g", W2_HIGH - KIB)
         pool_product(0, 2, slope0[:, :, HALF : HALF + QUARTER], h2, 0, QUARTER)
+        pool_product(1, 2, slopes1[4], h2, 0, P)
         for part in range(2):
-            pool_product(1, 2, slope4[part][:], h2, part * P // 2, P // 2)
-        pool_product(1, 2, slope5[:], h2, P, P)
+            pool_product(1, 2, slope5[part][:], h2, P + part * P // 2, P // 2)
 
         y2a = weighted("2a", y2[:, 0:QUARTER], 0, Y2)
         y2b = weighted("2b", y2[:, QUARTER:HALF], QUARTER, Y2 + KIB)
@@ -470,10 +472,10 @@ def tile_list_handover_gradient_kernel(
         h2_mx = quantize("h2", h2[:].rearrange("p b n -> p (b n)"))
         put(3, QUARTER, y3b)
 
-        h3 = placed([P, BLOCKS, QUARTER * PACK], BF16, "h3_g", W2_HIGH - 2 * KIB)
+        h3 = placed([P, BLOCKS, QUARTER * PACK], BF16, "h3_g", W2_HIGH - KIB)
         pool_product(0, 3, slope0[:, :, S - QUARTER : S], h3, 0, QUARTER)
-        pool_product(1, 3, slope6[:], h3, 0, P)
-        pool_product(1, 3, slope7[:], h3, P, P)
+        pool_product(1, 3, slope6, h3, 0, P)
+        pool_product(1, 3, slope7, h3, P, P)
 
         third = (QUARTER, [(h2_mx, 0), (h2_mx, QUARTER)])
         y_third = [weighted("t%d" % u, sums("t%d" % u, u, [third], (5, 2)[u]), HALF, (Y2 + 3 * KIB, Y2 + 4 * KIB)[u]) for u in range(2)]

@@ -27,7 +27,7 @@ BLOCKS = H // PASS
 PLANES = BLOCKS * PACK
 NT = N // P
 BANK = 2048
-VECTOR_SHARE = 16
+VECTOR_SHARE = 28
 
 KIB = 1024
 SLOT = [0, 9 * KIB, 17 * KIB, 31 * KIB, 39 * KIB]
@@ -170,6 +170,7 @@ def tile_list_handover_gradient_kernel(
             return slope[:]
 
         c_grouped = {}
+        c10_grouped = placed([P, HALF * PACK], BF16, "c10_g", CG10)
         for k in range(PLANES):
             b, t = divmod(k, PACK)
             plane = placed([P, T], F32, "plane%d" % k, LAST_PLANE if k == PLANES - 1 else SLOT[k % 5])
@@ -187,9 +188,8 @@ def tile_list_handover_gradient_kernel(
             if k < PLANES - 1:
                 nc.vector.tensor_copy(x, plane[:].indirect(idx[:]))
             else:
-                for half in range(2):
-                    picks = idx[:, half * HALF // 16 : (half + 1) * HALF // 16]
-                    nc.vector.tensor_copy(x[:, half * HALF : (half + 1) * HALF], plane[:].indirect(picks))
+                for lo, hi in ((0, QUARTER), (QUARTER, HALF), (HALF, S)):
+                    nc.vector.tensor_copy(x[:, lo:hi], plane[:].indirect(idx[:, lo // 16 : hi // 16]))
             if k < PACK - 1:
                 nc.scalar.activation(out=slope0[:, t, :], in_=x, func=COPY, bias=-1.0)
                 nc.gpsimd.tensor_tensor(slope0[:, t, :], slope0[:, t, :], x, MULT)
@@ -198,7 +198,16 @@ def tile_list_handover_gradient_kernel(
                 nc.gpsimd.tensor_tensor(slope0[:, t, :], slope0[:, t, :], x, MULT)
             else:
                 nc.gpsimd.tensor_scalar(less10[:, t, :], x[:, 0 : 3 * P], 1.0, -1.0, MULT, ADD)
-            priced((rows00, rows10)[b][:, t, :], x[:, 0:HALF], b, t)
+            if k < PLANES - 1:
+                priced((rows00, rows10)[b][:, t, :], x[:, 0:HALF], b, t)
+            else:
+                for q in range(2):
+                    cols = slice(q * QUARTER, (q + 1) * QUARTER)
+                    priced(rows10[:, t, cols], x[:, cols], b, t)
+                    nc.scalar.copy(
+                        out=c10_grouped[:, q * KIB : (q + 1) * KIB].rearrange("p (c i t) -> p c t i", i=4, t=PACK),
+                        in_=rows10[:, :, cols].rearrange("p t (c i) -> p c t i", i=4),
+                    )
             if b == 0:
                 priced(rows01[:, t, :], x[:, HALF:S], b, t)
             if k == PACK - 1:
@@ -228,7 +237,7 @@ def tile_list_handover_gradient_kernel(
         c_mx = {}
         c_mx[0, 0] = quantize("c00", c_grouped[0, 0], at=LAST_PLANE + HALF)
 
-        c_grouped[1, 0] = interleave("c10", rows10[:], CG10)
+        c_grouped[1, 0] = c10_grouped[:]
         w1a = placed([P, PASS * PACK], BF16, "w1_g0", WG1A)
         for copy, cols in ((nc.vector.tensor_copy, slice(0, VECTOR_SHARE)), (nc.scalar.copy, slice(VECTOR_SHARE, P))):
             copy(
@@ -236,7 +245,7 @@ def tile_list_handover_gradient_kernel(
                 in_=w1_raw[0][0][:].rearrange("p j (m t) -> p m j t", t=PACK)[:, cols, :, :],
             )
         w1_grouped = [w1a[:]]
-        slopes1 = {3: vector_slope(3, LAST_PLANE + 7 * KIB), 4: vector_slope(4, None)}
+        slopes1 = {3: vector_slope(3, LAST_PLANE + 7 * KIB)}
         c_mx[0, 1] = quantize("c01", c_grouped[0, 1], at=LAST_PLANE + 5 * KIB)
         deal_wf(1, 0, LAST_PLANE + 3 * KIB)
         c_mx[1, 0] = quantize("c10", c_grouped[1, 0])
@@ -388,6 +397,14 @@ def tile_list_handover_gradient_kernel(
         def quarter(q):
             return (QUARTER, [(h_mx[0, 0], q * QUARTER), (h10_mx[q], 0)])
 
+        def late_slope(g, less_at, at):
+            x = xs[1][:, :, g * P : (g + 1) * P]
+            less = placed([P, PACK, P], F32, "less%d" % g, less_at)
+            nc.scalar.activation(out=less[:], in_=x, func=COPY, bias=-1.0)
+            slope = placed([P, PACK, P], F32, "slope%d" % g, at)
+            nc.gpsimd.tensor_tensor(slope[:], less[:], x, MULT)
+            return slope[:]
+
         close_second(0)
         close_second(1)
         w2_mx[0] = quantize("w2_0", w2_low[0], QUARTER)
@@ -396,8 +413,10 @@ def tile_list_handover_gradient_kernel(
         close_second(2)
         close_second(3)
         w2_mx[1] = quantize("w2_1", w2_low[1], QUARTER, CG10 + KIB)
-        fused_stage("00", 0, 0, [quarter(0)], 2, Y00)
+        y00 = weighted("00", sums("00", 0, [quarter(0)], 2), 0, Y00)
         h10_mx[1] = quantize("h10b", h10[1][:], QUARTER)
+        put(0, 0, y00)
+        slopes1[4] = late_slope(4, W2_RAW[0][1], CG10 + 2 * KIB)
         fused_stage("01", 1, 0, [quarter(0)], 3, Y01)
         rows11 = placed([P, PACK, HALF], BF16, "rows11", ROWS11)
         for t in range(PACK):
@@ -406,14 +425,6 @@ def tile_list_handover_gradient_kernel(
         y10 = weighted("10", sums("10", 0, [quarter(1)], 6), QUARTER, ROWS11)
         c_mx[1, 1] = quantize("c11", c11_grouped)
         put(0, QUARTER, y10)
-
-        def late_slope(g, less_at, at):
-            x = xs[1][:, :, g * P : (g + 1) * P]
-            less = placed([P, PACK, P], F32, "less%d" % g, less_at)
-            nc.scalar.activation(out=less[:], in_=x, func=COPY, bias=-1.0)
-            slope = placed([P, PACK, P], F32, "slope%d" % g, at)
-            nc.gpsimd.tensor_tensor(slope[:], less[:], x, MULT)
-            return slope[:]
 
         w2_high_at = W2_HIGH + KIB
         slope6 = late_slope(6, ROWS11 + KIB, CG11)

@@ -28,6 +28,7 @@ PLANES = BLOCKS * PACK
 NT = N // P
 BANK = 2048
 VECTOR_SHARE = 28
+HEAD_CLEAR = 768
 
 KIB = 1024
 SLOT = [0, 9 * KIB, 17 * KIB, 31 * KIB, 39 * KIB]
@@ -142,8 +143,11 @@ def tile_list_handover_gradient_kernel(
         nc.vector.memset(tab_s[64:P, :].bitcast(I32), 0)
         wf_s_raw = placed([P, PASS + 4], U8, "wf_s_raw")
         nc.vector.memset(wf_s_raw[:].bitcast(I32), 0)
-        for page in pages:
+        nc.vector.memset(pages[3][:, 0 : HEAD_CLEAR - 1], 0.0)
+        nc.vector.memset(pages[3][:, HEAD_CLEAR - 1 : HEAD_CLEAR], 0.0)
+        for page in pages[:3]:
             nc.gpsimd.memset(page[:], 0.0)
+        nc.gpsimd.memset(pages[3][:, HEAD_CLEAR:], 0.0)
 
         nc.sync.dma_start(idx[:], offs)
         for first in (0, 16):
@@ -333,21 +337,20 @@ def tile_list_handover_gradient_kernel(
         h_mx = {}
         h_mx[0, 0] = quantize("h00", h00[:], at=SLOT[0] + 8 * KIB + HALF)
         w2_low = [cast_w2(0, w2_raw[0], CG00)]
-        x5 = xs[1][:, :, 5 * P : 6 * P]
-        less5 = placed([P, PACK, P], F32, "less5", W2_RAW[0][0])
-        nc.scalar.activation(out=less5[:], in_=x5, func=COPY, bias=-1.0)
-        w2_low.append(cast_w2(1, w2_raw[1], CG00 + 2 * KIB))
-        slope5 = []
-
-        def pool_slope5(part, at):
-            slope5.append(placed([P, PACK, P // 2], F32, "slope5%d" % part, at))
-            cols = slice(part * P // 2, (part + 1) * P // 2)
-            nc.gpsimd.tensor_tensor(slope5[part][:], less5[:, :, cols], x5[:, :, cols], MULT)
-
-        pool_slope5(0, CG01)
-
         w2_mx = {}
-        h10 = [placed([P, QUARTER * PACK], BF16, "h10_g%d" % q, CG10 + 2 * q * KIB) for q in range(2)]
+        w2_mx[0] = quantize("w2_0", w2_low[0], QUARTER)
+
+        def late_slope(g, less_at, at):
+            x = xs[1][:, :, g * P : (g + 1) * P]
+            less = placed([P, PACK, P], F32, "less%d" % g, less_at)
+            nc.scalar.activation(out=less[:], in_=x, func=COPY, bias=-1.0)
+            slope = placed([P, PACK, P], F32, "slope%d" % g, at)
+            nc.gpsimd.tensor_tensor(slope[:], less[:], x, MULT)
+            return slope[:]
+
+        slopes1[5] = late_slope(5, W2_RAW[0][0], CG00)
+        w2_low.append(cast_w2(1, w2_raw[1], CG00 + 2 * KIB))
+        h10 = [placed([P, QUARTER * PACK], BF16, "h10_g%d" % q, (W2_RAW[0][1], CG10 + 2 * KIB)[q]) for q in range(2)]
         h10_mx = {}
 
         def close_second(g):
@@ -384,39 +387,29 @@ def tile_list_handover_gradient_kernel(
             nc.vector.tensor_tensor(pages[u][:].indirect(slots), y_sb[:], wgo_sb[:, first : first + width], MULT)
 
         def weighted(name, y, first, at):
-            y_sb = placed([P, QUARTER], F32, "y_sb" + name, at)
+            width = y.shape[1]
+            y_sb = placed([P, width], F32, "y_sb" + name, at)
             nc.vector.scalar_tensor_tensor(
-                out=y_sb[:], in0=wgo_sb[:, first : first + QUARTER], scalar=-1.0, in1=y, op0=MULT, op1=MULT
+                out=y_sb[:], in0=wgo_sb[:, first : first + width], scalar=-1.0, in1=y, op0=MULT, op1=MULT
             )
             return y_sb[:]
 
         def put(u, first, values):
-            slots = idx2[:, first // 16 : (first + QUARTER) // 16]
+            slots = idx2[:, first // 16 : (first + values.shape[1]) // 16]
             nc.vector.tensor_copy(pages[u][:].indirect(slots), values)
 
         def quarter(q):
             return (QUARTER, [(h_mx[0, 0], q * QUARTER), (h10_mx[q], 0)])
 
-        def late_slope(g, less_at, at):
-            x = xs[1][:, :, g * P : (g + 1) * P]
-            less = placed([P, PACK, P], F32, "less%d" % g, less_at)
-            nc.scalar.activation(out=less[:], in_=x, func=COPY, bias=-1.0)
-            slope = placed([P, PACK, P], F32, "slope%d" % g, at)
-            nc.gpsimd.tensor_tensor(slope[:], less[:], x, MULT)
-            return slope[:]
-
-        close_second(0)
-        close_second(1)
-        w2_mx[0] = quantize("w2_0", w2_low[0], QUARTER)
+        for g in range(3):
+            close_second(g)
         h10_mx[0] = quantize("h10a", h10[0][:], QUARTER)
-        pool_slope5(1, CG10)
-        close_second(2)
         close_second(3)
-        w2_mx[1] = quantize("w2_1", w2_low[1], QUARTER, CG10 + KIB)
+        w2_mx[1] = quantize("w2_1", w2_low[1], QUARTER, W2_RAW[0][1])
         y00 = weighted("00", sums("00", 0, [quarter(0)], 2), 0, Y00)
         h10_mx[1] = quantize("h10b", h10[1][:], QUARTER)
         put(0, 0, y00)
-        slopes1[4] = late_slope(4, W2_RAW[0][1], CG10 + 2 * KIB)
+        slopes1[4] = late_slope(4, SLOT[0] + 5 * KIB, CG10 + 2 * KIB)
         fused_stage("01", 1, 0, [quarter(0)], 3, Y01)
         rows11 = placed([P, PACK, HALF], BF16, "rows11", ROWS11)
         for t in range(PACK):
@@ -469,15 +462,12 @@ def tile_list_handover_gradient_kernel(
                 copy_out(b, q)
         h2 = placed([P, BLOCKS, QUARTER * PACK], BF16, "h2_g", W2_HIGH - KIB)
         pool_product(0, 2, slope0[:, :, HALF : HALF + QUARTER], h2, 0, QUARTER)
-        pool_product(1, 2, slopes1[4], h2, 0, P)
-        for part in range(2):
-            pool_product(1, 2, slope5[part][:], h2, P + part * P // 2, P // 2)
+        for g in range(2):
+            pool_product(1, 2, slopes1[4 + g], h2, g * P, P)
 
-        y2a = weighted("2a", y2[:, 0:QUARTER], 0, Y2)
-        y2b = weighted("2b", y2[:, QUARTER:HALF], QUARTER, Y2 + KIB)
+        y2_sb = weighted("2", y2, 0, Y2)
         y3a = weighted("3a", y3[:, 0:QUARTER], 0, Y2 + 2 * KIB)
-        put(2, 0, y2a)
-        put(2, QUARTER, y2b)
+        put(2, 0, y2_sb)
         put(3, 0, y3a)
         y3b = weighted("3b", y3[:, QUARTER:HALF], QUARTER, D_SB[1, 2])
         h2_mx = quantize("h2", h2[:].rearrange("p b n -> p (b n)"))

@@ -29,6 +29,7 @@ NT = N // P
 BANK = 2048
 VECTOR_SHARE = 28
 HEAD_CLEAR = 768
+VECTOR_USERS = 32
 
 KIB = 1024
 SLOT = [0, 9 * KIB, 17 * KIB, 31 * KIB, 39 * KIB]
@@ -439,9 +440,10 @@ def tile_list_handover_gradient_kernel(
         def copy_out(b, q):
             d_sb[b, q] = placed([P, 2, PASS], F32, "d_sb%d%d" % (b, q), D_SB[b, q])
             for g in range(2):
+                users = P - VECTOR_USERS if (b, q, g) == (1, 3, 1) else P
                 nc.scalar.copy(
-                    out=d_sb[b, q][:, g, :].rearrange("p (c t i) -> p c t i", t=PACK, i=4),
-                    in_=banks[b, 2 * q + g][0][:].rearrange("p t (c i) -> p c t i", i=4),
+                    out=d_sb[b, q][:, g, 0 : users * PACK].rearrange("p (c t i) -> p c t i", t=PACK, i=4),
+                    in_=banks[b, 2 * q + g][0][:, :, 0:users].rearrange("p t (c i) -> p c t i", i=4),
                 )
 
         def pool_product(b, q, slope, grouped, first, width):
@@ -476,7 +478,9 @@ def tile_list_handover_gradient_kernel(
         h3 = placed([P, BLOCKS, QUARTER * PACK], BF16, "h3_g", W2_HIGH - KIB)
         pool_product(0, 3, slope0[:, :, S - QUARTER : S], h3, 0, QUARTER)
         pool_product(1, 3, slope6, h3, 0, P)
-        pool_product(1, 3, slope7, h3, P, P)
+        users = P - VECTOR_USERS
+        pool_product(1, 3, slope7[:, :, 0:users], h3, P, users)
+        product(1, 7, slope7[:, :, users:P], h3[:, 1, (P + users) * PACK :], slice(users, P))
 
         third = (QUARTER, [(h2_mx, 0), (h2_mx, QUARTER)])
         y_third = [weighted("t%d" % u, sums("t%d" % u, u, [third], (5, 2)[u]), HALF, (Y2 + 3 * KIB, Y2 + 4 * KIB)[u]) for u in range(2)]

from contextlib import ExitStack

import concourse.mybir as mybir

T, S, K, H, N, T2 = 2048, 1024, 512, 1024, 512, 2048
FLOPS = 2 * S * (K * H + H * H + H * N)

F32 = mybir.dt.float32
BF16 = mybir.dt.bfloat16
I32 = mybir.dt.int32
U32 = mybir.dt.uint32
U16 = mybir.dt.uint16
U8 = mybir.dt.uint8
E4 = mybir.dt.float8_e4m3fn_x4
E5 = mybir.dt.float8_e5m2_x4
MULT = mybir.AluOpType.mult
SUB = mybir.AluOpType.subtract
ADD = mybir.AluOpType.add
COPY = mybir.ActivationFunctionType.Copy

P = 128
PACK = 4
PASS = P * PACK
HALF = 512
QUARTER = 256
BLOCKS = H // PASS
PLANES = BLOCKS * PACK
NT = N // P
BANK = 2048
VECTOR_SHARE = 28
HEAD_CLEAR = 768
VECTOR_USERS = 32

KIB = 1024
SLOT = [0, 9 * KIB, 17 * KIB, 31 * KIB, 39 * KIB]
LAST_PLANE = 21 * KIB
TABLE = 43 * KIB
W1A = 31 * KIB
WF1 = 39 * KIB
W2_RAW = [(9 * KIB, 11 * KIB), (13 * KIB, 15 * KIB), (45 * KIB, 49 * KIB)]
W2_COLS = [(0, P), (P, P), (2 * P, 2 * P)]
ROWS01 = 51 * KIB
ROWS00 = 56 * KIB + HALF
ROWS10 = 76 * KIB
ROWS11 = 13 * KIB
CG00, CG01, CG10, WG1A, WG1B = (k * KIB for k in (64, 68, 72, 106, 80))
Y00, Y01, CG11, Y_LAST = (k * KIB for k in (91, 92, 93, 97))
W2_HIGH = 15 * KIB
Y2 = 86 * KIB
D_SB = {(0, 2): 1 * KIB, (1, 2): 57 * KIB, (0, 3): 80 * KIB, (1, 3): 102 * KIB}


def tile_list_handover_gradient_kernel(
    tc, tab_words, tab_scales, offs, sT, w1, price, wf_words, wf_scales, w2, offs2, wgo, out
):
    nc = tc.nc
    with ExitStack() as ctx:
        keep = ctx.enter_context(tc.tile_pool(name="keep", bufs=1))
        arena = ctx.enter_context(tc.tile_pool(name="arena", bufs=1))
        psum = ctx.enter_context(tc.psum_pool(name="psum", bufs=1))

        def placed(shape, dtype, name, at=None):
            if at is None:
                return keep.tile(shape, dtype, name=name, align_bytes=64)
            return arena.tile(shape, dtype, name=name, align_bytes=64, offset=at)

        idx = keep.tile([P, S // 16], U16, name="idx")
        idx2 = keep.tile([P, S // 16], U16, name="idx2")

        def quantize(name, grouped, width=HALF, at=None):
            codes = placed([P, width], U32, name + "_w")
            scales = placed([P, width], U8, name + "_s", at)
            nc.vector.quantize_mx(out=codes[:].bitcast(E4), scales=scales[:], in_=grouped)
            return codes, scales

        def interleave(name, rows, at):
            grouped = placed([P, HALF * PACK], BF16, name + "_g", at)
            nc.scalar.copy(
                out=grouped[:].rearrange("p (c i t) -> p c t i", i=4, t=PACK),
                in_=rows.rearrange("p t (c i) -> p c t i", i=4),
            )
            return grouped[:]

        def load_w1(b, at, parts):
            width = PASS // parts
            raws = []
            for part in range(parts):
                raw = placed([P, PACK, width], F32, "w1_raw%d%d" % (b, part), at + part * width * PACK * 4)
                cols = w1[:, b * PASS + part * width : b * PASS + (part + 1) * width]
                nc.sync.dma_start(out=raw[:], in_=cols.rearrange("(p j) c -> p j c", j=PACK))
                raws.append(raw)
            return raws

        def cast_w1(b, raws, at):
            grouped = placed([P, PASS * PACK], BF16, "w1_g%d" % b, at)
            dealt = grouped[:].rearrange("p (t m j) -> p m j t", t=PACK, j=PACK)
            width = P // len(raws)
            for part, raw in enumerate(raws):
                nc.scalar.copy(
                    out=dealt[:, part * width : (part + 1) * width, :, :],
                    in_=raw[:].rearrange("p j (m t) -> p m j t", t=PACK),
                )
            return grouped[:]

        def load_w2(part):
            first, width = W2_COLS[part]
            raws = []
            for b in range(BLOCKS):
                raw = placed([P, PACK, width], F32, "w2_raw%d%d" % (part, b), W2_RAW[part][b])
                rows = w2[b * PASS : (b + 1) * PASS, first : first + width]
                nc.sync.dma_start(out=raw[:], in_=rows.rearrange("(p j) c -> p j c", j=PACK))
                raws.append(raw)
            return raws

        def cast_w2(part, raws, at):
            grouped = placed([P, BLOCKS, W2_COLS[part][1] * PACK], BF16, "w2_g%d" % part, at)
            for b in range(BLOCKS):
                nc.scalar.copy(
                    out=grouped[:, b, :].rearrange("p (c i t) -> p c t i", i=4, t=PACK),
                    in_=raws[b][:].rearrange("p t (c i) -> p c t i", i=4),
                )
            return grouped[:].rearrange("p b n -> p (b n)")

        wf_raw = {}
        wf_w = {}

        def load_wf(a, at):
            wf_raw[a] = placed([P, H], I32, "wf_raw%d" % a, at)
            nc.sync.dma_start(out=wf_raw[a][:], in_=wf_words[a].rearrange("p n t -> p (n t)").bitcast(I32))

        def deal_wf(a, b, at, copy=nc.vector.tensor_copy):
            wf_w[a, b] = placed([P, PASS], U32, "wf_w%d%d" % (a, b), at)
            copy(
                out=wf_w[a, b][:].rearrange("p (t c i) -> p c t i", t=PACK, i=4),
                in_=wf_raw[a][:, b * PASS : (b + 1) * PASS].bitcast(U32).rearrange("p (c i t) -> p c t i", t=PACK, i=4),
            )


        s_rows = sT.rearrange("(b p t) n -> b t p n", p=P, t=PACK)

        tab_s = placed([P, T + 4], U8, "tab_s")
        pages = [placed([P, T2], F32, "page%d" % u) for u in range(NT)]
        nc.vector.memset(tab_s[32:64, :].bitcast(I32), 0)
        nc.vector.memset(tab_s[64:P, :].bitcast(I32), 0)
        wf_s_raw = placed([P, PASS + 4], U8, "wf_s_raw")
        nc.vector.memset(wf_s_raw[:].bitcast(I32), 0)
        nc.vector.memset(pages[3][:, 0 : HEAD_CLEAR - 1], 0.0)
        nc.vector.memset(pages[3][:, HEAD_CLEAR - 1 : HEAD_CLEAR], 0.0)
        for page in pages[:3]:
            nc.gpsimd.memset(page[:], 0.0)
        nc.gpsimd.memset(pages[3][:, HEAD_CLEAR:], 0.0)

        nc.sync.dma_start(idx[:], offs)
        for first in (0, 16):
            nc.sync.dma_start(out=tab_s[first : first + 16, 0:T].bitcast(I32), in_=tab_scales[0].bitcast(I32))
        price_sb = placed([P, BLOCKS, PACK], F32, "price_sb")

        v_s_raw = placed([P, S], U8, "v_s_raw")
        nc.vector.tensor_copy(v_s_raw[:], tab_s[:, 0:T].indirect(idx[:]))

        xs = [placed([P, PACK, S], F32, "x%d" % b) for b in range(BLOCKS)]
        slope0 = placed([P, PACK, S], F32, "slope0")
        less10 = placed([P, PACK, 3 * P], F32, "less10")
        rows00 = placed([P, PACK, HALF], BF16, "rows00", ROWS00)
        rows01 = placed([P, PACK, HALF], BF16, "rows01", ROWS01)
        rows10 = placed([P, PACK, HALF], BF16, "rows10", ROWS10)

        def priced(dst, src, b, t):
            nc.scalar.activation(out=dst, in_=src, func=COPY, scale=price_sb[:, b, t : t + 1])

        def vector_slope(g, at):
            slope = placed([P, PACK, P], F32, "slope%d" % g, at)
            x = xs[1][:, :, g * P : (g + 1) * P]
            nc.vector.scalar_tensor_tensor(out=slope[:], in0=x, scalar=1.0, in1=x, op0=SUB, op1=MULT)
            return slope[:]

        c_grouped = {}
        c10_grouped = placed([P, HALF * PACK], BF16, "c10_g", CG10)
        for k in range(PLANES):
            b, t = divmod(k, PACK)
            plane = placed([P, T], F32, "plane%d" % k, LAST_PLANE if k == PLANES - 1 else SLOT[k % 5])
            nc.sync.dma_start(out=plane[:], in_=s_rows[b, t])
            if k == 0:
                nc.sync.dma_start(out=price_sb[:], in_=price.rearrange("(b p t) -> p b t", p=P, t=PACK))
            if 1 <= k <= 4:
                for block in range(BLOCKS):
                    row = 32 * (k - 1) + 8 * block
                    nc.sync.dma_start(
                        out=wf_s_raw[row : row + 8, 0:PASS].bitcast(I32),
                        in_=wf_scales[:, 4 * (k - 1) : 4 * k, block * PASS : (block + 1) * PASS].bitcast(I32),
                    )
            x = xs[b][:, t, :]
            if k < PLANES - 1:
                nc.vector.tensor_copy(x, plane[:].indirect(idx[:]))
            else:
                for lo, hi in ((0, QUARTER), (QUARTER, HALF), (HALF, S)):
                    nc.vector.tensor_copy(x[:, lo:hi], plane[:].indirect(idx[:, lo // 16 : hi // 16]))
            if k < PACK - 1:
                nc.scalar.activation(out=slope0[:, t, :], in_=x, func=COPY, bias=-1.0)
                nc.gpsimd.tensor_tensor(slope0[:, t, :], slope0[:, t, :], x, MULT)
            elif k < PACK:
                nc.gpsimd.tensor_scalar(slope0[:, t, :], x, 1.0, -1.0, MULT, ADD)
                nc.gpsimd.tensor_tensor(slope0[:, t, :], slope0[:, t, :], x, MULT)
            else:
                nc.gpsimd.tensor_scalar(less10[:, t, :], x[:, 0 : 3 * P], 1.0, -1.0, MULT, ADD)
            if k < PLANES - 1:
                priced((rows00, rows10)[b][:, t, :], x[:, 0:HALF], b, t)
            else:
                for q in range(2):
                    cols = slice(q * QUARTER, (q + 1) * QUARTER)
                    priced(rows10[:, t, cols], x[:, cols], b, t)
                    nc.scalar.copy(
                        out=c10_grouped[:, q * KIB : (q + 1) * KIB].rearrange("p (c i t) -> p c t i", i=4, t=PACK),
                        in_=rows10[:, :, cols].rearrange("p t (c i) -> p c t i", i=4),
                    )
            if b == 0:
                priced(rows01[:, t, :], x[:, HALF:S], b, t)
            if k == PACK - 1:
                c_grouped[0, 0] = interleave("c00", rows00[:], CG00)
            if k == PACK + 1:
                c_grouped[0, 1] = interleave("c01", rows01[:], 84 * KIB)

        load_wf(0, SLOT[2])
        w1_raw = [load_w1(0, W1A, 1)]
        load_wf(1, WF1)
        tab_w = placed([P, T], I32, "tab_w", TABLE)
        nc.sync.dma_start(out=tab_w[:], in_=tab_words[0].rearrange("p n t -> p (n t)").bitcast(I32))
        v_s = placed([P, S], U8, "v_s", SLOT[0])
        for q in range(4):
            nc.sync.dma_start(
                out=v_s[32 * q : 32 * q + 4, :].bitcast(I32), in_=v_s_raw[4 * q : 4 * q + 4, :].bitcast(I32)
            )
        w1_raw.append(load_w1(1, SLOT[0] + KIB, 2))
        w2_raw = [load_w2(0), load_w2(1)]
        nc.sync.dma_start(idx2[:], offs2)

        deal_wf(0, 0, LAST_PLANE + KIB)
        wf_s = placed([P, PASS], U8, "wf_s")
        nc.gpsimd.tensor_copy(
            out=wf_s[:].rearrange("p (t m) -> p t m", t=PACK), in_=wf_s_raw[:, 0:PASS].rearrange("p (m t) -> p t m", t=PACK)
        )
        c_mx = {}
        c_mx[0, 0] = quantize("c00", c_grouped[0, 0], at=LAST_PLANE + HALF)

        c_grouped[1, 0] = c10_grouped[:]
        w1a = placed([P, PASS * PACK], BF16, "w1_g0", WG1A)
        for copy, cols in ((nc.vector.tensor_copy, slice(0, VECTOR_SHARE)), (nc.scalar.copy, slice(VECTOR_SHARE, P))):
            copy(
                out=w1a[:].rearrange("p (t m j) -> p m j t", t=PACK, j=PACK)[:, cols, :, :],
                in_=w1_raw[0][0][:].rearrange("p j (m t) -> p m j t", t=PACK)[:, cols, :, :],
            )
        w1_grouped = [w1a[:]]
        slopes1 = {3: vector_slope(3, LAST_PLANE + 7 * KIB)}
        c_mx[0, 1] = quantize("c01", c_grouped[0, 1], at=LAST_PLANE + 5 * KIB)
        deal_wf(1, 0, LAST_PLANE + 3 * KIB)
        c_mx[1, 0] = quantize("c10", c_grouped[1, 0])
        deal_wf(0, 1, W1A + 6 * KIB, nc.scalar.copy)
        deal_wf(1, 1, W1A + 4 * KIB, nc.scalar.copy)
        v_w = {}

        def gather_table(first, width, at):
            words = placed([P, width], U32, "v_w%d" % first, at)
            picks = idx[:, first // 16 : (first + width) // 16]
            nc.vector.tensor_copy(words[:], tab_w[:].bitcast(U32).indirect(picks))
            for g in range(width // P):
                v_w[first // P + g] = words[:, g * P : (g + 1) * P]

        codes, scales = quantize("w1a", w1_grouped[0])
        w1_mx = {(0, t): (codes[:, t * P : (t + 1) * P], scales[:, t * P : (t + 1) * P]) for t in range(PACK)}
        gather_table(0, QUARTER, W1A)
        gather_table(QUARTER, QUARTER, W1A + KIB)
        gather_table(HALF, HALF, W1A + 2 * KIB)
        wgo_sb = placed([P, S], F32, "wgo_sb", TABLE - 2 * KIB)
        nc.sync.dma_start(out=wgo_sb[:], in_=wgo)
        w2_raw.append(load_w2(2))
        for g, at in enumerate((WG1A - KIB, WG1A + KIB, WG1A + 3 * KIB)):
            cols = slice(g * P, (g + 1) * P)
            slope = placed([P, PACK, P], F32, "slope1%d" % g, at)
            nc.gpsimd.tensor_tensor(slope[:], less10[:, :, cols], xs[1][:, :, cols], MULT)
            slopes1[g] = slope[:]

        banks = {}

        def open_bank(b, g, bank):
            banks[b, g] = [psum.tile([P, PACK, P], F32, name="d%d%d" % (b, g), offset=bank * BANK), 0]

        def passes(b, g, kind):
            half, first = divmod(g * P, HALF)
            for t in range(PACK):
                d, done = banks[b, g]
                if kind == "table":
                    lhs = w1_mx[b, t][0].bitcast(E4)
                    lhs_scale = w1_mx[b, t][1]
                    rhs = v_w[g].bitcast(E5)
                    rhs_scale = v_s[:, g * P : (g + 1) * P]
                else:
                    lhs = wf_w[kind, b][:, t * P : (t + 1) * P].bitcast(E4)
                    lhs_scale = wf_s[8 * b + 4 * kind : P, t * P : (t + 1) * P]
                    rhs = c_mx[kind, half][0][:, first : first + P].bitcast(E4)
                    rhs_scale = c_mx[kind, half][1][:, first : first + P]
                nc.tensor.matmul_mx(
                    out=d[:, t, :], lhsT=lhs, lhsT_scale=lhs_scale, rhs=rhs, rhs_scale=rhs_scale,
                    start=(done == 0), stop=(done == 3 * PACK - 1),
                )
                banks[b, g][1] = done + 1

        def product(b, g, slope, grouped, cols=slice(0, P)):
            nc.vector.tensor_tensor(
                grouped.rearrange("p (c i t) -> p c t i", i=2, t=PACK),
                slope.rearrange("p t (c i) -> p c t i", i=2),
                banks[b, g][0][:, :, cols].rearrange("p t (c i) -> p c t i", i=2),
                MULT,
            )

        for g in range(4):
            open_bank(0, g, g)
            passes(0, g, 0)
        for g in range(4):
            passes(0, g, 1)
        h00 = placed([P, HALF * PACK], BF16, "h00_g", CG01)
        for g in range(4):
            passes(0, g, "table")
            product(0, g, slope0[:, :, g * P : (g + 1) * P], h00[:, g * PASS : (g + 1) * PASS])
        for g in range(2):
            open_bank(1, g, 4 + g)
            passes(1, g, 0)
            passes(1, g, 1)

        w1_grouped.append(cast_w1(1, w1_raw[1], WG1B))
        for g in range(2, 4):
            open_bank(1, g, g - 2)
            passes(1, g, 0)
            passes(1, g, 1)
        for pair in range(2):
            codes, scales = quantize("w1b%d" % pair, w1_grouped[1][:, pair * KIB : (pair + 1) * KIB], QUARTER)
            for t in range(2):
                w1_mx[1, 2 * pair + t] = (codes[:, t * P : (t + 1) * P], scales[:, t * P : (t + 1) * P])
        h_mx = {}
        h_mx[0, 0] = quantize("h00", h00[:], at=SLOT[0] + 8 * KIB + HALF)
        w2_low = [cast_w2(0, w2_raw[0], CG00)]
        w2_mx = {}
        w2_mx[0] = quantize("w2_0", w2_low[0], QUARTER)

        def late_slope(g, less_at, at):
            x = xs[1][:, :, g * P : (g + 1) * P]
            less = placed([P, PACK, P], F32, "less%d" % g, less_at)
            nc.scalar.activation(out=less[:], in_=x, func=COPY, bias=-1.0)
            slope = placed([P, PACK, P], F32, "slope%d" % g, at)
            nc.gpsimd.tensor_tensor(slope[:], less[:], x, MULT)
            return slope[:]

        slopes1[5] = late_slope(5, W2_RAW[0][0], CG00)
        w2_low.append(cast_w2(1, w2_raw[1], CG00 + 2 * KIB))
        h10 = [placed([P, QUARTER * PACK], BF16, "h10_g%d" % q, (W2_RAW[0][1], CG10 + 2 * KIB)[q]) for q in range(2)]
        h10_mx = {}

        def close_second(g):
            passes(1, g, "table")
            product(1, g, slopes1[g], h10[g // 2][:, g % 2 * PASS : (g % 2 + 1) * PASS])

        def sums(name, u, pieces, bank):
            part = min(u, 2)
            col, cols = u * P - W2_COLS[part][0], W2_COLS[part][1]
            width = sum(w for w, operands in pieces)
            y = psum.tile([P, width], F32, name="y" + name, offset=bank * BANK)
            lo = 0
            for w, operands in pieces:
                for b in range(BLOCKS):
                    (codes, scales), start = operands[b]
                    nc.tensor.matmul_mx(
                        out=y[:, lo : lo + w],
                        lhsT=w2_mx[part][0][:, b * cols + col : b * cols + col + P].bitcast(E4),
                        lhsT_scale=w2_mx[part][1][:, b * cols + col : b * cols + col + P],
                        rhs=codes[:, start : start + w].bitcast(E4),
                        rhs_scale=scales[:, start : start + w],
                        start=(b == 0),
                        stop=(b == BLOCKS - 1),
                    )
                lo += w
            return y[:]

        def fused_stage(name, u, first, pieces, bank, at):
            y = sums(name, u, pieces, bank)
            width = y.shape[1]
            y_sb = placed([P, width], F32, "y_sb" + name, at)
            nc.scalar.activation(out=y_sb[:], in_=y, func=COPY, scale=-1.0)
            slots = idx2[:, first // 16 : (first + width) // 16]
            nc.vector.tensor_tensor(pages[u][:].indirect(slots), y_sb[:], wgo_sb[:, first : first + width], MULT)

        def weighted(name, y, first, at):
            width = y.shape[1]
            y_sb = placed([P, width], F32, "y_sb" + name, at)
            nc.vector.scalar_tensor_tensor(
                out=y_sb[:], in0=wgo_sb[:, first : first + width], scalar=-1.0, in1=y, op0=MULT, op1=MULT
            )
            return y_sb[:]

        def put(u, first, values):
            slots = idx2[:, first // 16 : (first + values.shape[1]) // 16]
            nc.vector.tensor_copy(pages[u][:].indirect(slots), values)

        def quarter(q):
            return (QUARTER, [(h_mx[0, 0], q * QUARTER), (h10_mx[q], 0)])

        for g in range(3):
            close_second(g)
        h10_mx[0] = quantize("h10a", h10[0][:], QUARTER)
        close_second(3)
        w2_mx[1] = quantize("w2_1", w2_low[1], QUARTER, W2_RAW[0][1])
        y00 = weighted("00", sums("00", 0, [quarter(0)], 2), 0, Y00)
        h10_mx[1] = quantize("h10b", h10[1][:], QUARTER)
        put(0, 0, y00)
        slopes1[4] = late_slope(4, SLOT[0] + 5 * KIB, CG10 + 2 * KIB)
        fused_stage("01", 1, 0, [quarter(0)], 3, Y01)
        rows11 = placed([P, PACK, HALF], BF16, "rows11", ROWS11)
        for t in range(PACK):
            priced(rows11[:, t, :], xs[1][:, t, HALF:S], 1, t)
        c11_grouped = interleave("c11", rows11[:], CG11)
        y10 = weighted("10", sums("10", 0, [quarter(1)], 6), QUARTER, ROWS11)
        c_mx[1, 1] = quantize("c11", c11_grouped)
        put(0, QUARTER, y10)

        w2_high_at = W2_HIGH + KIB
        slope6 = late_slope(6, ROWS11 + KIB, CG11)
        w2_high = cast_w2(2, w2_raw[2], w2_high_at)
        y11 = weighted("11", sums("11", 1, [quarter(1)], 7), QUARTER, W2_RAW[2][1])
        w2_mx[2] = quantize("w2_2", w2_high)
        put(1, QUARTER, y11)
        slope7 = late_slope(7, W2_RAW[2][1] + KIB, w2_high_at + 2 * KIB)

        def late_sums(q, four):
            for b in range(BLOCKS):
                for g in range(2):
                    open_bank(b, 2 * q + g, four[2 * b + g])
                    for kind in ("table", 0, 1):
                        passes(b, 2 * q + g, kind)

        d_sb = {}

        def copy_out(b, q):
            d_sb[b, q] = placed([P, 2, PASS], F32, "d_sb%d%d" % (b, q), D_SB[b, q])
            for g in range(2):
                users = P - VECTOR_USERS if (b, q, g) == (1, 3, 1) else P
                nc.scalar.copy(
                    out=d_sb[b, q][:, g, 0 : users * PACK].rearrange("p (c t i) -> p c t i", t=PACK, i=4),
                    in_=banks[b, 2 * q + g][0][:, :, 0:users].rearrange("p t (c i) -> p c t i", i=4),
                )

        def pool_product(b, q, slope, grouped, first, width):
            cols = slice(first * PACK, (first + width) * PACK)
            nc.gpsimd.tensor_tensor(
                grouped[:, b, cols].rearrange("p (c i t) -> p c t i", i=4, t=PACK),
                slope.rearrange("p t (c i) -> p c t i", i=4),
                d_sb[b, q][:].rearrange("p g n -> p (g n)")[:, cols].rearrange("p (c t i) -> p c t i", t=PACK, i=4),
                MULT,
            )

        late_sums(2, (4, 5, 2, 3))
        y2 = sums("2", 2, [quarter(0), quarter(1)], 0)
        y3 = sums("3", 3, [quarter(0), quarter(1)], 1)
        late_sums(3, (6, 7, 0, 4))
        for q in (2, 3):
            for b in range(BLOCKS):
                copy_out(b, q)
        h2 = placed([P, BLOCKS, QUARTER * PACK], BF16, "h2_g", W2_HIGH - KIB)
        pool_product(0, 2, slope0[:, :, HALF : HALF + QUARTER], h2, 0, QUARTER)
        for g in range(2):
            pool_product(1, 2, slopes1[4 + g], h2, g * P, P)

        y2_sb = weighted("2", y2, 0, Y2)
        y3a = weighted("3a", y3[:, 0:QUARTER], 0, Y2 + 2 * KIB)
        put(2, 0, y2_sb)
        put(3, 0, y3a)
        y3b = weighted("3b", y3[:, QUARTER:HALF], QUARTER, D_SB[1, 2])
        h2_mx = quantize("h2", h2[:].rearrange("p b n -> p (b n)"))
        put(3, QUARTER, y3b)

        h3 = placed([P, BLOCKS, QUARTER * PACK], BF16, "h3_g", W2_HIGH - KIB)
        pool_product(0, 3, slope0[:, :, S - QUARTER : S], h3, 0, QUARTER)
        pool_product(1, 3, slope6, h3, 0, P)
        users = P - VECTOR_USERS
        pool_product(1, 3, slope7[:, :, 0:users], h3, P, users)
        product(1, 7, slope7[:, :, users:P], h3[:, 1, (P + users) * PACK :], slice(users, P))

        third = (QUARTER, [(h2_mx, 0), (h2_mx, QUARTER)])
        y_third = [weighted("t%d" % u, sums("t%d" % u, u, [third], (5, 2)[u]), HALF, (Y2 + 3 * KIB, Y2 + 4 * KIB)[u]) for u in range(2)]
        for u in range(2):
            put(u, HALF, y_third[u])
        h3_mx = quantize("h3", h3[:].rearrange("p b n -> p (b n)"))
        fused_stage("t2", 2, HALF, [third], 3, D_SB[1, 3])
        fourth = (QUARTER, [(h3_mx, 0), (h3_mx, QUARTER)])
        for u in range(NT - 1):
            fused_stage("l%d" % u, u, HALF + QUARTER, [fourth], (6, 7, 0)[u], Y_LAST + u * KIB)
            nc.sync.dma_start(out=out[u * P : (u + 1) * P, :], in_=pages[u][:])
        fused_stage("l3", 3, HALF, [third, fourth], 4, Y_LAST + 3 * KIB)
        nc.sync.dma_start(out=out[3 * P : 4 * P, :], in_=pages[3][:])
